import numpy as np
import ml_dtypes


def mxq(x, axis, fmt="e4m3"):
    dtype, down = {"e4m3": (ml_dtypes.float8_e4m3fn, 7), "e5m2": (ml_dtypes.float8_e5m2, 14)}[fmt]
    v = np.moveaxis(np.asarray(x, np.float32).astype(ml_dtypes.bfloat16).astype(np.float64), axis, -1)
    blocks = v.reshape(v.shape[:-1] + (-1, 32))
    amax = np.abs(blocks).max(-1, keepdims=True)
    byte = np.maximum(np.where(amax > 0, np.frexp(amax)[1] - 1 + 127, 0) - down, 1)
    scale = np.exp2(byte - 127.0)
    codes = (blocks / scale).astype(np.float32).astype(dtype).astype(np.float64)
    return np.moveaxis((codes * scale).reshape(v.shape), -1, axis)


WIDE = False


def mx_kscale(k):
    if not WIDE:
        return np.ones(k)
    levels = np.array([10, -10, 5, -5, 0])
    if k % 512:
        return np.exp2(np.random.permutation(np.resize(levels, k // 32))).repeat(32)
    a = np.empty((k // 512, 16))
    for p in range(k // 512):
        a[p, :8] = np.random.permutation(np.resize(levels, 8))
        for g in range(8):
            far = levels[np.abs(levels - a[p, g]) >= 10]
            a[p, g + 8] = far[np.random.randint(len(far))]
    return np.exp2(a.ravel()).repeat(32)


def f64(x):
    return np.asarray(x).astype(np.float64)


def striped(idx):
    return np.tile(idx.reshape(-1, 16).T, (8, 1)).astype(np.uint16)


def unstriped(offs):
    return offs[:16].T.reshape(-1).astype(np.int64)


E2M1 = np.array([0.0, 0.5, 1.0, 1.5, 2.0, 3.0, 4.0, 6.0, -0.0, -0.5, -1.0, -1.5, -2.0, -3.0, -4.0, -6.0])


def pack_weight(w, fmt):
    k, n = w.shape
    w = f64(np.asarray(w, np.float32).astype(ml_dtypes.bfloat16)).reshape(k // 32, 32, n)
    amax = np.abs(w).max(1)
    if fmt == "e4m3":
        byte = np.frexp(amax)[1] - 1 + 127 - 7
    else:
        mant, ex = np.frexp(amax / 6.0)
        byte = np.where(mant > 0.5, ex, ex - 1) + 127
    byte = np.clip(np.where(amax > 0, byte, 1), 1, 254)
    scaled = (w * np.exp2(127.0 - byte)[:, None, :]).reshape(k, n).astype(np.float32)
    by_word = np.ascontiguousarray(scaled.reshape(k // 512, 128, 4, n).transpose(0, 1, 3, 2))
    if fmt == "e4m3":
        words = by_word.astype(ml_dtypes.float8_e4m3fn).view(np.uint8)
    else:
        c = by_word.astype(ml_dtypes.float4_e2m1fn).view(np.uint8) & 0xF
        words = (c[..., 0::2] | (c[..., 1::2] << 4)).reshape(k // 512, 128, 2 * n)
    return np.ascontiguousarray(words), np.ascontiguousarray(byte.astype(np.uint8).reshape(k // 512, 16, n))


def unpack_weight(words, scales, fmt):
    g, _, n = scales.shape
    words = np.ascontiguousarray(words).reshape(g, 128, n, -1)
    if fmt == "e4m3":
        vals = words.view(ml_dtypes.float8_e4m3fn).astype(np.float64)
    else:
        nib = np.empty((g, 128, n, 4), np.uint8)
        nib[..., 0::2] = words & 0xF
        nib[..., 1::2] = words >> 4
        vals = E2M1[nib]
    vals = vals * np.repeat(np.exp2(scales.astype(np.float64) - 127.0), 8, axis=1)[..., None]
    return vals.transpose(0, 1, 3, 2).reshape(g * 512, n)


def gelu(v):
    return 0.5 * v * (1.0 + np.tanh(np.sqrt(2.0 / np.pi) * (v + 0.044715 * v**3)))


def bf(x):
    return np.asarray(x, np.float32).astype(ml_dtypes.bfloat16)

def planes(Y):
    n, m = Y.shape
    b = f64(bf(Y)).reshape(n // 32, 32, m)
    amax = np.abs(b).max(1)
    byte = np.clip(np.where(amax > 0, np.frexp(amax)[1] - 1 + 127 - 7, 1), 1, 254)
    codes = (b * np.exp2(127.0 - byte)[:, None, :]).reshape(n, m).astype(np.float32).astype(ml_dtypes.float8_e4m3fn).view(np.uint8)
    words = codes.reshape(n // 512, 128, 4, m).transpose(0, 1, 3, 2)
    return np.ascontiguousarray(words), np.ascontiguousarray(byte.astype(np.uint8).reshape(n // 512, 16, m))


K, H, N, T, S = 512, 1024, 1024, 4096, 1024

def setup_inputs():
    n = np.random.standard_normal
    s = mx_kscale(K)[:, None]
    u = mx_kscale(H)[:, None]
    gain = np.exp(0.8 * n(N))
    tab_words, tab_scales = pack_weight(n((K, T)) * s, "e4m3")
    wg4_words, wg4_scales = pack_weight(n((K, H)) / np.sqrt(K) / s * u.T, "e2m1")
    bg = (0.5 * n(H) * u[:, 0]).astype(np.float32)
    wv = (n((K, H)) / np.sqrt(K) / s).astype(np.float32)
    erev = (np.where(np.random.rand(H) < 0.7, 1.2, -0.8) + 0.2 * n(H)).astype(np.float32)
    wo8_words, wo8_scales = pack_weight(n((H, N)) / np.sqrt(H) / u * gain, "e4m3")
    bo = (0.5 * n(N) * gain).astype(np.float32)
    offs = striped(np.random.permutation(T)[:S])
    return {"tab_words": tab_words, "tab_scales": tab_scales, "offs": offs,
            "wg4_words": wg4_words, "wg4_scales": wg4_scales, "bg": bg,
            "wv": wv, "erev": erev,
            "wo8_words": wo8_words, "wo8_scales": wo8_scales, "bo": bo}

def reference(tab_words, tab_scales, offs, wg4_words, wg4_scales, bg, wv, erev, wo8_words, wo8_scales, bo):
    v = unpack_weight(tab_words, tab_scales, "e4m3")[:, unstriped(offs)]
    wg = unpack_weight(wg4_words, wg4_scales, "e2m1")
    wo = unpack_weight(wo8_words, wo8_scales, "e4m3")
    g = np.maximum((wg.T @ v) + f64(bg)[:, None], 0.0)
    d = f64(erev)[:, None] - (mxq(f64(wv), 0, "e4m3").T @ v)
    h = g * d
    y = (wo.T @ mxq(h, 0, "e4m3")) + f64(bo)[:, None]
    words, scales = planes(y)
    return y, words, scales

@@ -1,0 +1,279 @@
+from contextlib import ExitStack
+
+import concourse.mybir as mybir
+
+K, H, N, T, S = 512, 1024, 1024, 4096, 1024
+FLOPS = 2 * S * (2 * K * H + H * N)
+
+F32 = mybir.dt.float32
+BF16 = mybir.dt.bfloat16
+I32 = mybir.dt.int32
+U32 = mybir.dt.uint32
+U16 = mybir.dt.uint16
+U8 = mybir.dt.uint8
+FP8X4 = mybir.dt.float8_e4m3fn_x4
+FP4X4 = mybir.dt.float4_e2m1fn_x4
+ALU = mybir.AluOpType
+ACT = mybir.ActivationFunctionType
+
+P = 128
+PACK = 4
+GROUP = P * PACK
+CHUNK = 512
+QUADRANTS = 4
+
+WV_VECTOR_SHARE = (80, 0)
+LAST_VECTOR_SHARE = 352
+TABLE_LEAD = 1024
+
+
+def tile_list_synaptic_channel_currents_kernel(
+    tc, tab_words, tab_scales, offs, wg4_words, wg4_scales, bg, wv, erev, wo8_words, wo8_scales, bo, out_0, out_1, out_2
+):
+    nc = tc.nc
+    with ExitStack() as ctx:
+        keep = ctx.enter_context(tc.tile_pool(name="keep", bufs=1))
+        psum = ctx.enter_context(tc.psum_pool(name="psum", bufs=1))
+
+        def sb(name, shape, dtype, tag=None):
+            return keep.tile(shape, dtype, name=name, tag=tag or name, align_bytes=64)
+
+        def bank(index, name):
+            return psum.tile([P, CHUNK], F32, name=name, tag="bank%d" % index)
+
+        offsets = keep.tile([P, S // 16], U16, name="offsets")
+        table = sb("table", [P, T], U32)
+        table_planes = sb("table_planes", [P, T], U8)
+        wg_raw = sb("wg_raw", [P, 2 * H], U8)
+        wg_planes_raw = sb("wg_planes_raw", [P, H], U8)
+        wo_planes_raw = sb("wo_planes_raw", [P, N], U8)
+        wv_raw = [sb("wv_raw%d" % a, [P, PACK, GROUP], F32) for a in range(2)]
+        wo_raw = sb("wo_raw", [P, 2, N], U32)
+        bg_sb = sb("bg_sb", [P, 2, 8], F32)
+        erev_sb = sb("erev_sb", [P, 2, 8], F32)
+        bo_sb = sb("bo_sb", [P, 2, 8], F32)
+
+        nc.vector.memset(table_planes[:].bitcast(I32), 0)
+        nc.gpsimd.memset(wg_planes_raw[:].bitcast(I32), 0)
+        nc.gpsimd.memset(wo_planes_raw[:].bitcast(I32), 0)
+
+        def dealt(vec):
+            return vec.rearrange("(a p t) -> p a t", p=P, t=PACK)
+
+        def rows_of_quadrant(q, count):
+            return slice(32 * q, 32 * q + count)
+
+        def load_planes(planes, scales):
+            for q in range(QUADRANTS):
+                nc.sync.dma_start(
+                    planes[rows_of_quadrant(q, 4 * scales.shape[0]), :].bitcast(I32),
+                    scales[:, 4 * q : 4 * q + 4, :].bitcast(I32),
+                )
+
+        def load_wv(a):
+            nc.sync.dma_start(wv_raw[a][:], wv[:, GROUP * a : GROUP * (a + 1)].rearrange("(p j) c -> p j c", j=PACK))
+
+        table_dram = tab_words[0].rearrange("p t i -> p (t i)").bitcast(I32)
+        nc.sync.dma_start(offsets[:], offs)
+        nc.sync.dma_start(wg_raw[:].bitcast(I32), wg4_words[0].bitcast(I32))
+        nc.sync.dma_start(table[:, :TABLE_LEAD].bitcast(I32), table_dram[:, :TABLE_LEAD])
+        load_planes(table_planes, tab_scales)
+        nc.sync.dma_start(table[:, TABLE_LEAD:].bitcast(I32), table_dram[:, TABLE_LEAD:])
+        load_planes(wg_planes_raw, wg4_scales)
+        nc.sync.dma_start(bg_sb[:, :, 0:PACK], dealt(bg))
+        nc.sync.dma_start(erev_sb[:, :, 0:PACK], dealt(erev))
+        load_wv(0)
+        load_wv(1)
+        nc.sync.dma_start(wo_raw[:].bitcast(I32), wo8_words.rearrange("a p c i -> p a (c i)").bitcast(I32))
+        load_planes(wo_planes_raw, wo8_scales)
+        nc.sync.dma_start(bo_sb[:, :, 0:PACK], dealt(bo))
+
+        wg = sb("wg", [P, 2 * H], U8)
+        wg_planes = sb("wg_planes", [P, H], U8)
+        wo = sb("wo", [P, 2 * N], U32)
+        wo_planes = sb("wo_planes", [P, N], U8)
+        wv_codes = [sb("wv_codes%d" % a, [P, GROUP], U32) for a in range(2)]
+        wv_planes = [sb("wv_planes%d" % a, [P, GROUP], U8) for a in range(2)]
+        v_codes = [sb("v_codes%d" % c, [P, CHUNK], U32) for c in range(2)]
+        v_planes = [sb("v_planes%d" % c, [P, CHUNK], U8) for c in range(2)]
+        y_planes = sb("y_planes", [P, 2, S], U8)
+        units = [(c, a) for c in range(2) for a in range(2)]
+        g = {u: sb("g%d%d" % u, [P, PACK, CHUNK], F32) for u in units}
+        h_rows = {u: sb("h_rows%d%d" % u, [P, PACK, CHUNK], BF16) for u in units}
+        h_woven = {u: sb("h_woven%d%d" % u, [P, CHUNK, PACK], BF16) for u in units}
+        h_codes = {u: sb("h_codes%d%d" % u, [P, CHUNK], U32) for u in units}
+        h_planes = {u: sb("h_planes%d%d" % u, [P, CHUNK], U8) for u in units}
+        y = {u: sb("y%d%d" % u, [P, PACK, CHUNK], F32) for u in units}
+        y_woven = {u: sb("y_woven%d%d" % u, [P, CHUNK, PACK], BF16) for u in units}
+        y_codes = {u: sb("y_codes%d%d" % u, [P, CHUNK], U32) for u in units}
+        wv_woven = [sb("wv_woven%d" % a, [P, PACK, P, PACK], BF16) for a in range(2)]
+
+        def deal(dst, src, width):
+            nc.vector.tensor_copy(
+                dst.rearrange("p (a t m e) -> p a m t e", t=PACK, m=P, e=width),
+                src.rearrange("p (a m t e) -> p a m t e", t=PACK, m=P, e=width),
+            )
+
+        def list_of(c):
+            return offsets[:, c * CHUNK // 16 : (c + 1) * CHUNK // 16]
+
+        def weave_wv(a):
+            split = WV_VECTOR_SHARE[a]
+            dst = wv_woven[a][:].rearrange("p t m j -> p m j t")
+            src = wv_raw[a][:].rearrange("p j (m t) -> p m j t", t=PACK)
+            if split:
+                nc.vector.tensor_scalar(dst[:, :split], src[:, :split], -1.0, None, ALU.mult)
+            nc.scalar.activation(dst[:, split:], src[:, split:], ACT.Copy, scale=-1.0)
+
+        def quantize_wv(a):
+            nc.vector.quantize_mx(
+                out=wv_codes[a][:].bitcast(FP8X4),
+                scales=wv_planes[a][:],
+                in_=wv_woven[a][:].rearrange("p t m j -> p (t m j)"),
+            )
+
+        def weave(engine, woven, rows, first, last):
+            dst = woven[:, first:last, :].rearrange("p (c i) t -> p c t i", i=4)
+            src = rows[:, :, first:last].rearrange("p t (c i) -> p c t i", i=4)
+            if engine == "vector":
+                nc.vector.tensor_copy(dst, src)
+            else:
+                nc.scalar.copy(dst, src)
+
+        def conductances(c, a):
+            for t in range(PACK):
+                col = GROUP * a + P * t
+                acc = bank(t % 2, "g_acc")
+                nc.tensor.matmul_mx(
+                    out=acc[:],
+                    lhsT=wg[:, 2 * col : 2 * (col + P)].bitcast(FP4X4),
+                    lhsT_scale=wg_planes[:, col : col + P],
+                    rhs=v_codes[c][:].bitcast(FP8X4),
+                    rhs_scale=v_planes[c][:],
+                    start=True,
+                    stop=True,
+                )
+                nc.scalar.activation(g[c, a][:, t, :], acc[:], ACT.Relu, bias=bg_sb[:, a, t : t + 1])
+
+        def currents(c, a):
+            for t in range(PACK):
+                acc = bank(2 + (PACK * (2 * c + a) + t) % 3, "d_acc")
+                nc.tensor.matmul_mx(
+                    out=acc[:],
+                    lhsT=wv_codes[a][:, P * t : P * (t + 1)].bitcast(FP8X4),
+                    lhsT_scale=wv_planes[a][:, P * t : P * (t + 1)],
+                    rhs=v_codes[c][:].bitcast(FP8X4),
+                    rhs_scale=v_planes[c][:],
+                    start=True,
+                    stop=True,
+                )
+                nc.vector.scalar_tensor_tensor(
+                    h_rows[c, a][:, t, :], acc[:], erev_sb[:, a, t : t + 1], g[c, a][:, t, :], ALU.add, ALU.mult
+                )
+
+        def quantize_h(c, a):
+            nc.vector.quantize_mx(
+                out=h_codes[c, a][:].bitcast(FP8X4),
+                scales=h_planes[c, a][:],
+                in_=h_woven[c, a][:].rearrange("p j t -> p (j t)"),
+            )
+
+        def mix_pass(acc, c, b, t, a):
+            col = GROUP * b + P * t
+            nc.tensor.matmul_mx(
+                out=acc[:],
+                lhsT=wo[:, N * a + col : N * a + col + P].bitcast(FP8X4),
+                lhsT_scale=wo_planes[4 * a :, col : col + P],
+                rhs=h_codes[c, a][:].bitcast(FP8X4),
+                rhs_scale=h_planes[c, a][:],
+                start=(a == 0),
+                stop=(a == 1),
+            )
+
+        def add_bias(engine, acc, c, b, t):
+            if engine == "vector":
+                nc.vector.tensor_scalar(y[c, b][:, t, :], acc[:], bo_sb[:, b, t : t + 1], None, ALU.add)
+            else:
+                nc.scalar.activation(y[c, b][:, t, :], acc[:], ACT.Identity, bias=bo_sb[:, b, t : t + 1])
+
+        def store_y(c, b, first, last):
+            rows = out_0[GROUP * b : GROUP * (b + 1), CHUNK * c : CHUNK * (c + 1)].rearrange("(p t) j -> p t j", t=PACK)
+            nc.sync.dma_start(rows[:, first:last, :], y[c, b][:, first:last, :])
+
+        def quantize_y(c, b):
+            nc.vector.quantize_mx(
+                out=y_codes[c, b][:].bitcast(FP8X4),
+                scales=y_planes[:, b, CHUNK * c : CHUNK * (c + 1)],
+                in_=y_woven[c, b][:].rearrange("p j t -> p (j t)"),
+            )
+            words = out_1[b].rearrange("p m t -> p (m t)")[:, 4 * CHUNK * c : 4 * CHUNK * (c + 1)]
+            nc.sync.dma_start(words.bitcast(I32), y_codes[c, b][:].bitcast(I32))
+
+        deal(wg[:], wg_raw[:], 2)
+        for c in range(2):
+            nc.vector.tensor_copy(v_planes[c][:], table_planes[:].indirect(list_of(c)))
+        nc.vector.tensor_copy(v_codes[0][:], table[:].indirect(list_of(0)))
+        deal(wg_planes[:], wg_planes_raw[:], 1)
+        nc.vector.tensor_copy(v_codes[1][:], table[:].indirect(list_of(1)))
+
+        weave_wv(0)
+        quantize_wv(0)
+        conductances(0, 0)
+        weave_wv(1)
+        currents(0, 0)
+        quantize_wv(1)
+        conductances(0, 1)
+        weave("vector", h_woven[0, 0], h_rows[0, 0], 0, CHUNK)
+        currents(0, 1)
+        quantize_h(0, 0)
+        weave("scalar", h_woven[0, 1], h_rows[0, 1], 0, CHUNK)
+        deal(wo[:].bitcast(I32), wo_raw[:].bitcast(I32).rearrange("p a c -> p (a c)"), 1)
+        deal(wo_planes[:], wo_planes_raw[:], 1)
+        quantize_h(0, 1)
+        conductances(1, 0)
+        currents(1, 0)
+        conductances(1, 1)
+        currents(1, 1)
+
+        for b in range(2):
+            for t in range(PACK):
+                acc = bank(5 + (PACK * b + t) % 3, "y_acc")
+                for a in range(2):
+                    mix_pass(acc, 0, b, t, a)
+                add_bias("scalar", acc, 0, b, t)
+                if t % 2 == 1:
+                    store_y(0, b, t - 1, t + 1)
+
+        weave("vector", h_woven[1, 0], h_rows[1, 0], 0, CHUNK)
+        weave("vector", h_woven[1, 1], h_rows[1, 1], 0, CHUNK)
+        quantize_h(1, 0)
+        quantize_h(1, 1)
+
+        late_banks = (0, 1, 2, 3, 4, 7, 5, 6)
+        accs = [bank(index, "y_acc") for index in late_banks]
+        for i in range(2 * PACK):
+            mix_pass(accs[i], 1, i // PACK, i % PACK, 0)
+        for i in range(2 * PACK):
+            mix_pass(accs[i], 1, i // PACK, i % PACK, 1)
+
+        for b in range(2):
+            for t in range(PACK):
+                add_bias("vector" if (b, t) == (1, 3) else "scalar", accs[PACK * b + t], 1, b, t)
+                if t % 2 == 1:
+                    store_y(1, b, t - 1, t + 1)
+        weave("scalar", y_woven[0, 0], y[0, 0], 0, CHUNK // 2)
+        weave("scalar", y_woven[0, 0], y[0, 0], CHUNK // 2, CHUNK)
+        weave("vector", y_woven[0, 1], y[0, 1], 0, CHUNK)
+        quantize_y(0, 0)
+        quantize_y(0, 1)
+        weave("vector", y_woven[1, 0], y[1, 0], 0, CHUNK)
+        quantize_y(1, 0)
+        weave("vector", y_woven[1, 1], y[1, 1], 0, LAST_VECTOR_SHARE)
+        weave("scalar", y_woven[1, 1], y[1, 1], LAST_VECTOR_SHARE, CHUNK)
+        quantize_y(1, 1)
+        for q in range(QUADRANTS):
+            queue = nc.sync if q % 2 == 0 else nc.scalar
+            queue.dma_start(
+                out_2[:, 4 * q : 4 * q + 4, :].rearrange("b r m -> r b m").bitcast(I32),
+                y_planes[rows_of_quadrant(q, 4), :, :].bitcast(I32),
+            )

@@ -22,9 +22,9 @@ GROUP = P * PACK
 CHUNK = 512
 QUADRANTS = 4
 
-WV_VECTOR_SHARE = (80, 0)
-LAST_VECTOR_SHARE = 352
-TABLE_LEAD = 1024
+WV_VECTOR_SHARE = (0, 64)
+H_VECTOR_SHARE = 320
+Y_VECTOR_SHARE = 384
 
 
 def tile_list_synaptic_channel_currents_kernel(
@@ -53,9 +53,9 @@ def tile_list_synaptic_channel_currents_kernel(
         erev_sb = sb("erev_sb", [P, 2, 8], F32)
         bo_sb = sb("bo_sb", [P, 2, 8], F32)
 
+        nc.vector.memset(wg_planes_raw[:].bitcast(I32), 0)
         nc.vector.memset(table_planes[:].bitcast(I32), 0)
-        nc.gpsimd.memset(wg_planes_raw[:].bitcast(I32), 0)
-        nc.gpsimd.memset(wo_planes_raw[:].bitcast(I32), 0)
+        nc.vector.memset(wo_planes_raw[:].bitcast(I32), 0)
 
         def dealt(vec):
             return vec.rearrange("(a p t) -> p a t", p=P, t=PACK)
@@ -63,34 +63,34 @@ def tile_list_synaptic_channel_currents_kernel(
         def rows_of_quadrant(q, count):
             return slice(32 * q, 32 * q + count)
 
-        def load_planes(planes, scales):
+        def load_planes(queue, planes, scales):
             for q in range(QUADRANTS):
-                nc.sync.dma_start(
+                queue.dma_start(
                     planes[rows_of_quadrant(q, 4 * scales.shape[0]), :].bitcast(I32),
                     scales[:, 4 * q : 4 * q + 4, :].bitcast(I32),
                 )
 
-        def load_wv(a):
-            nc.sync.dma_start(wv_raw[a][:], wv[:, GROUP * a : GROUP * (a + 1)].rearrange("(p j) c -> p j c", j=PACK))
+        def load_wv(a, first, last):
+            rows = wv[:, GROUP * a : GROUP * (a + 1)].rearrange("(p j) c -> p j c", j=PACK)
+            nc.sync.dma_start(wv_raw[a][:, first:last, :], rows[:, first:last, :])
 
-        table_dram = tab_words[0].rearrange("p t i -> p (t i)").bitcast(I32)
+        load_planes(nc.scalar, wg_planes_raw, wg4_scales)
         nc.sync.dma_start(offsets[:], offs)
         nc.sync.dma_start(wg_raw[:].bitcast(I32), wg4_words[0].bitcast(I32))
-        nc.sync.dma_start(table[:, :TABLE_LEAD].bitcast(I32), table_dram[:, :TABLE_LEAD])
-        load_planes(table_planes, tab_scales)
-        nc.sync.dma_start(table[:, TABLE_LEAD:].bitcast(I32), table_dram[:, TABLE_LEAD:])
-        load_planes(wg_planes_raw, wg4_scales)
+        load_wv(0, 0, 2)
+        load_wv(0, 2, 4)
+        load_planes(nc.sync, table_planes, tab_scales)
+        nc.sync.dma_start(table[:].bitcast(I32), tab_words[0].rearrange("p t i -> p (t i)").bitcast(I32))
         nc.sync.dma_start(bg_sb[:, :, 0:PACK], dealt(bg))
         nc.sync.dma_start(erev_sb[:, :, 0:PACK], dealt(erev))
-        load_wv(0)
-        load_wv(1)
+        load_wv(1, 0, 4)
         nc.sync.dma_start(wo_raw[:].bitcast(I32), wo8_words.rearrange("a p c i -> p a (c i)").bitcast(I32))
-        load_planes(wo_planes_raw, wo8_scales)
+        load_planes(nc.sync, wo_planes_raw, wo8_scales)
         nc.sync.dma_start(bo_sb[:, :, 0:PACK], dealt(bo))
 
         wg = sb("wg", [P, 2 * H], U8)
         wg_planes = sb("wg_planes", [P, H], U8)
-        wo = sb("wo", [P, 2 * N], U32)
+        wo = [sb("wo%d" % b, [P, 2, GROUP], U32) for b in range(2)]
         wo_planes = sb("wo_planes", [P, N], U8)
         wv_codes = [sb("wv_codes%d" % a, [P, GROUP], U32) for a in range(2)]
         wv_planes = [sb("wv_planes%d" % a, [P, GROUP], U8) for a in range(2)]
@@ -108,10 +108,23 @@ def tile_list_synaptic_channel_currents_kernel(
         y_codes = {u: sb("y_codes%d%d" % u, [P, CHUNK], U32) for u in units}
         wv_woven = [sb("wv_woven%d" % a, [P, PACK, P, PACK], BF16) for a in range(2)]
 
-        def deal(dst, src, width):
+        def deal_wg(a):
+            cols = slice(2 * GROUP * a, 2 * GROUP * (a + 1))
             nc.vector.tensor_copy(
-                dst.rearrange("p (a t m e) -> p a m t e", t=PACK, m=P, e=width),
-                src.rearrange("p (a m t e) -> p a m t e", t=PACK, m=P, e=width),
+                wg[:, cols].rearrange("p (t k i e) -> p k t i e", t=PACK, i=8, e=2),
+                wg_raw[:, cols].rearrange("p (k i t e) -> p k t i e", t=PACK, i=8, e=2),
+            )
+
+        def deal_planes(dst, src):
+            nc.vector.tensor_copy(
+                dst[:].rearrange("p (a t k i) -> p a k t i", a=2, t=PACK, i=16),
+                src[:].rearrange("p (a k i t) -> p a k t i", a=2, t=PACK, i=16),
+            )
+
+        def deal_wo(b):
+            nc.vector.tensor_copy(
+                wo[b][:].bitcast(I32).rearrange("p a (t k i) -> p a k t i", t=PACK, i=4),
+                wo_raw[:, :, GROUP * b : GROUP * (b + 1)].bitcast(I32).rearrange("p a (k i t) -> p a k t i", t=PACK, i=4),
             )
 
         def list_of(c):
@@ -119,11 +132,13 @@ def tile_list_synaptic_channel_currents_kernel(
 
         def weave_wv(a):
             split = WV_VECTOR_SHARE[a]
-            dst = wv_woven[a][:].rearrange("p t m j -> p m j t")
-            src = wv_raw[a][:].rearrange("p j (m t) -> p m j t", t=PACK)
+            dst = wv_woven[a][:].rearrange("p t m j -> p m t j")
+            src = wv_raw[a][:].rearrange("p j (m t) -> p m t j", t=PACK)
             if split:
                 nc.vector.tensor_scalar(dst[:, :split], src[:, :split], -1.0, None, ALU.mult)
-            nc.scalar.activation(dst[:, split:], src[:, split:], ACT.Copy, scale=-1.0)
+                nc.scalar.activation(dst[:, split:], src[:, split:], ACT.Copy, scale=-1.0)
+            else:
+                nc.scalar.activation(dst, src, ACT.Copy, scale=-1.0)
 
         def quantize_wv(a):
             nc.vector.quantize_mx(
@@ -143,7 +158,7 @@ def tile_list_synaptic_channel_currents_kernel(
         def conductances(c, a):
             for t in range(PACK):
                 col = GROUP * a + P * t
-                acc = bank(t % 2, "g_acc")
+                acc = bank((PACK * (2 * c + a) + t) % 3, "g_acc")
                 nc.tensor.matmul_mx(
                     out=acc[:],
                     lhsT=wg[:, 2 * col : 2 * (col + P)].bitcast(FP4X4),
@@ -157,7 +172,7 @@ def tile_list_synaptic_channel_currents_kernel(
 
         def currents(c, a):
             for t in range(PACK):
-                acc = bank(2 + (PACK * (2 * c + a) + t) % 3, "d_acc")
+                acc = bank(3 + (PACK * (2 * c + a) + t) % 3, "d_acc")
                 nc.tensor.matmul_mx(
                     out=acc[:],
                     lhsT=wv_codes[a][:, P * t : P * (t + 1)].bitcast(FP8X4),
@@ -182,7 +197,7 @@ def tile_list_synaptic_channel_currents_kernel(
             col = GROUP * b + P * t
             nc.tensor.matmul_mx(
                 out=acc[:],
-                lhsT=wo[:, N * a + col : N * a + col + P].bitcast(FP8X4),
+                lhsT=wo[b][:, a, P * t : P * (t + 1)].bitcast(FP8X4),
                 lhsT_scale=wo_planes[4 * a :, col : col + P],
                 rhs=h_codes[c, a][:].bitcast(FP8X4),
                 rhs_scale=h_planes[c, a][:],
@@ -209,67 +224,73 @@ def tile_list_synaptic_channel_currents_kernel(
             words = out_1[b].rearrange("p m t -> p (m t)")[:, 4 * CHUNK * c : 4 * CHUNK * (c + 1)]
             nc.sync.dma_start(words.bitcast(I32), y_codes[c, b][:].bitcast(I32))
 
-        deal(wg[:], wg_raw[:], 2)
+        def weave_h(c, a):
+            weave("vector", h_woven[c, a], h_rows[c, a], 0, H_VECTOR_SHARE)
+            weave("scalar", h_woven[c, a], h_rows[c, a], H_VECTOR_SHARE, CHUNK)
+
+        def weave_y(c, b):
+            weave("vector", y_woven[c, b], y[c, b], 0, Y_VECTOR_SHARE)
+            weave("scalar", y_woven[c, b], y[c, b], Y_VECTOR_SHARE, CHUNK)
+
+        def mix_early(c, b):
+            for t in range(PACK):
+                acc = bank(6 + t % 2, "y_acc")
+                for a in range(2):
+                    mix_pass(acc, c, b, t, a)
+                add_bias("scalar", acc, c, b, t)
+                store_y(c, b, t, t + 1)
+
+        def mix_late(c, b, banks):
+            accs = [bank(index, "y_acc") for index in banks]
+            for t in range(PACK):
+                mix_pass(accs[t], c, b, t, 0)
+            for t in range(PACK):
+                mix_pass(accs[t], c, b, t, 1)
+                add_bias("vector" if t == 0 else "scalar", accs[t], c, b, t)
+                store_y(c, b, t, t + 1)
+
+        for a in range(2):
+            deal_wg(a)
+        weave_wv(0)
         for c in range(2):
             nc.vector.tensor_copy(v_planes[c][:], table_planes[:].indirect(list_of(c)))
-        nc.vector.tensor_copy(v_codes[0][:], table[:].indirect(list_of(0)))
-        deal(wg_planes[:], wg_planes_raw[:], 1)
-        nc.vector.tensor_copy(v_codes[1][:], table[:].indirect(list_of(1)))
-
-        weave_wv(0)
         quantize_wv(0)
+        deal_planes(wg_planes, wg_planes_raw)
+        for c in range(2):
+            nc.vector.tensor_copy(v_codes[c][:], table[:].indirect(list_of(c)))
+
         conductances(0, 0)
         weave_wv(1)
         currents(0, 0)
         quantize_wv(1)
         conductances(0, 1)
-        weave("vector", h_woven[0, 0], h_rows[0, 0], 0, CHUNK)
+        weave_h(0, 0)
         currents(0, 1)
         quantize_h(0, 0)
-        weave("scalar", h_woven[0, 1], h_rows[0, 1], 0, CHUNK)
-        deal(wo[:].bitcast(I32), wo_raw[:].bitcast(I32).rearrange("p a c -> p (a c)"), 1)
-        deal(wo_planes[:], wo_planes_raw[:], 1)
+        weave_h(0, 1)
+        deal_wo(0)
+        deal_planes(wo_planes, wo_planes_raw)
+        deal_wo(1)
         quantize_h(0, 1)
         conductances(1, 0)
         currents(1, 0)
         conductances(1, 1)
+        mix_early(0, 0)
         currents(1, 1)
-
-        for b in range(2):
-            for t in range(PACK):
-                acc = bank(5 + (PACK * b + t) % 3, "y_acc")
-                for a in range(2):
-                    mix_pass(acc, 0, b, t, a)
-                add_bias("scalar", acc, 0, b, t)
-                if t % 2 == 1:
-                    store_y(0, b, t - 1, t + 1)
-
-        weave("vector", h_woven[1, 0], h_rows[1, 0], 0, CHUNK)
-        weave("vector", h_woven[1, 1], h_rows[1, 1], 0, CHUNK)
+        weave_h(1, 0)
+        weave_h(1, 1)
+        mix_early(0, 1)
         quantize_h(1, 0)
         quantize_h(1, 1)
-
-        late_banks = (0, 1, 2, 3, 4, 7, 5, 6)
-        accs = [bank(index, "y_acc") for index in late_banks]
-        for i in range(2 * PACK):
-            mix_pass(accs[i], 1, i // PACK, i % PACK, 0)
-        for i in range(2 * PACK):
-            mix_pass(accs[i], 1, i // PACK, i % PACK, 1)
-
-        for b in range(2):
-            for t in range(PACK):
-                add_bias("vector" if (b, t) == (1, 3) else "scalar", accs[PACK * b + t], 1, b, t)
-                if t % 2 == 1:
-                    store_y(1, b, t - 1, t + 1)
-        weave("scalar", y_woven[0, 0], y[0, 0], 0, CHUNK // 2)
-        weave("scalar", y_woven[0, 0], y[0, 0], CHUNK // 2, CHUNK)
-        weave("vector", y_woven[0, 1], y[0, 1], 0, CHUNK)
+        weave_y(0, 0)
+        mix_late(1, 0, (0, 1, 2, 3))
         quantize_y(0, 0)
+        weave_y(0, 1)
+        mix_late(1, 1, (4, 5, 6, 7))
         quantize_y(0, 1)
-        weave("vector", y_woven[1, 0], y[1, 0], 0, CHUNK)
+        weave_y(1, 0)
+        weave_y(1, 1)
         quantize_y(1, 0)
-        weave("vector", y_woven[1, 1], y[1, 1], 0, LAST_VECTOR_SHARE)
-        weave("scalar", y_woven[1, 1], y[1, 1], LAST_VECTOR_SHARE, CHUNK)
         quantize_y(1, 1)
         for q in range(QUADRANTS):
             queue = nc.sync if q % 2 == 0 else nc.scalar

@@ -53,8 +53,8 @@ def tile_list_synaptic_channel_currents_kernel(
         erev_sb = sb("erev_sb", [P, 2, 8], F32)
         bo_sb = sb("bo_sb", [P, 2, 8], F32)
 
-        nc.vector.memset(wg_planes_raw[:].bitcast(I32), 0)
         nc.vector.memset(table_planes[:].bitcast(I32), 0)
+        nc.vector.memset(wg_planes_raw[:].bitcast(I32), 0)
         nc.vector.memset(wo_planes_raw[:].bitcast(I32), 0)
 
         def dealt(vec):
@@ -63,9 +63,9 @@ def tile_list_synaptic_channel_currents_kernel(
         def rows_of_quadrant(q, count):
             return slice(32 * q, 32 * q + count)
 
-        def load_planes(queue, planes, scales):
+        def load_planes(queues, planes, scales):
             for q in range(QUADRANTS):
-                queue.dma_start(
+                queues[q].dma_start(
                     planes[rows_of_quadrant(q, 4 * scales.shape[0]), :].bitcast(I32),
                     scales[:, 4 * q : 4 * q + 4, :].bitcast(I32),
                 )
@@ -74,18 +74,17 @@ def tile_list_synaptic_channel_currents_kernel(
             rows = wv[:, GROUP * a : GROUP * (a + 1)].rearrange("(p j) c -> p j c", j=PACK)
             nc.sync.dma_start(wv_raw[a][:, first:last, :], rows[:, first:last, :])
 
-        load_planes(nc.scalar, wg_planes_raw, wg4_scales)
-        nc.sync.dma_start(offsets[:], offs)
         nc.sync.dma_start(wg_raw[:].bitcast(I32), wg4_words[0].bitcast(I32))
-        load_wv(0, 0, 2)
-        load_wv(0, 2, 4)
-        load_planes(nc.sync, table_planes, tab_scales)
+        nc.sync.dma_start(offsets[:], offs)
+        load_wv(0, 0, 4)
+        load_planes((nc.sync,) * 4, table_planes, tab_scales)
         nc.sync.dma_start(table[:].bitcast(I32), tab_words[0].rearrange("p t i -> p (t i)").bitcast(I32))
+        load_planes((nc.sync,) * 4, wg_planes_raw, wg4_scales)
         nc.sync.dma_start(bg_sb[:, :, 0:PACK], dealt(bg))
         nc.sync.dma_start(erev_sb[:, :, 0:PACK], dealt(erev))
         load_wv(1, 0, 4)
         nc.sync.dma_start(wo_raw[:].bitcast(I32), wo8_words.rearrange("a p c i -> p a (c i)").bitcast(I32))
-        load_planes(nc.sync, wo_planes_raw, wo8_scales)
+        load_planes((nc.sync,) * 4, wo_planes_raw, wo8_scales)
         nc.sync.dma_start(bo_sb[:, :, 0:PACK], dealt(bo))
 
         wg = sb("wg", [P, 2 * H], U8)
@@ -94,7 +93,7 @@ def tile_list_synaptic_channel_currents_kernel(
         wo_planes = sb("wo_planes", [P, N], U8)
         wv_codes = [sb("wv_codes%d" % a, [P, GROUP], U32) for a in range(2)]
         wv_planes = [sb("wv_planes%d" % a, [P, GROUP], U8) for a in range(2)]
-        v_codes = [sb("v_codes%d" % c, [P, CHUNK], U32) for c in range(2)]
+        v_codes = []
         v_planes = [sb("v_planes%d" % c, [P, CHUNK], U8) for c in range(2)]
         y_planes = sb("y_planes", [P, 2, S], U8)
         units = [(c, a) for c in range(2) for a in range(2)]
@@ -255,9 +254,11 @@ def tile_list_synaptic_channel_currents_kernel(
         for c in range(2):
             nc.vector.tensor_copy(v_planes[c][:], table_planes[:].indirect(list_of(c)))
         quantize_wv(0)
+        v_codes.append(sb("v_codes0", [P, CHUNK], U32))
+        nc.vector.tensor_copy(v_codes[0][:], table[:].indirect(list_of(0)))
         deal_planes(wg_planes, wg_planes_raw)
-        for c in range(2):
-            nc.vector.tensor_copy(v_codes[c][:], table[:].indirect(list_of(c)))
+        v_codes.append(sb("v_codes1", [P, CHUNK], U32, tag="wg_planes_raw"))
+        nc.vector.tensor_copy(v_codes[1][:], table[:].indirect(list_of(1)))
 
         conductances(0, 0)
         weave_wv(1)

@@ -19,12 +19,17 @@ ACT = mybir.ActivationFunctionType
 P = 128
 PACK = 4
 GROUP = P * PACK
-CHUNK = 512
+BANK = 512
+LOOKUP = 512
 QUADRANTS = 4
 
-WV_VECTOR_SHARE = (0, 64)
-H_VECTOR_SHARE = 320
-Y_VECTOR_SHARE = 384
+CHUNKS = ((0,256),(256,256),(512,256),(768,256))
+G_CHUNKS = ((0,512),(512,512))
+G_BANKS = (0, 1, 2,)
+D_BANKS = (3, 4, 5,)
+Y_BANKS = (6, 7,)
+H_VECTOR_SHARE = (192, 192, 192, 192,)
+Y_VECTOR_SHARE = (128, 128, 128, 192,)
 
 
 def tile_list_synaptic_channel_currents_kernel(
@@ -38,8 +43,12 @@ def tile_list_synaptic_channel_currents_kernel(
         def sb(name, shape, dtype, tag=None):
             return keep.tile(shape, dtype, name=name, tag=tag or name, align_bytes=64)
 
-        def bank(index, name):
-            return psum.tile([P, CHUNK], F32, name=name, tag="bank%d" % index)
+        taken = {"g": 0, "d": 0, "y": 0}
+
+        def bank(role, banks):
+            index = banks[taken[role] % len(banks)]
+            taken[role] = taken[role] + 1
+            return psum.tile([P, BANK], F32, name=role + "_acc", tag="bank%d" % index)
 
         offsets = keep.tile([P, S // 16], U16, name="offsets")
         table = sb("table", [P, T], U32)
@@ -47,7 +56,7 @@ def tile_list_synaptic_channel_currents_kernel(
         wg_raw = sb("wg_raw", [P, 2 * H], U8)
         wg_planes_raw = sb("wg_planes_raw", [P, H], U8)
         wo_planes_raw = sb("wo_planes_raw", [P, N], U8)
-        wv_raw = [sb("wv_raw%d" % a, [P, PACK, GROUP], F32) for a in range(2)]
+        wv_raw = [[sb("wv_raw%d%d" % (a, u), [P, PACK, GROUP // 2], F32) for u in range(2)] for a in range(2)]
         wo_raw = sb("wo_raw", [P, 2, N], U32)
         bg_sb = sb("bg_sb", [P, 2, 8], F32)
         erev_sb = sb("erev_sb", [P, 2, 8], F32)
@@ -60,31 +69,35 @@ def tile_list_synaptic_channel_currents_kernel(
         def dealt(vec):
             return vec.rearrange("(a p t) -> p a t", p=P, t=PACK)
 
-        def rows_of_quadrant(q, count):
-            return slice(32 * q, 32 * q + count)
+        def load_plane(planes, scales):
+            rows = scales[0].rearrange("(q r) c -> r q c", r=4)
+            for r in range(4):
+                nc.sync.dma_start(planes[r:P:32, :].bitcast(I32), rows[r].bitcast(I32))
 
-        def load_planes(queues, planes, scales):
+        def load_packed_planes(planes, scales):
             for q in range(QUADRANTS):
-                queues[q].dma_start(
-                    planes[rows_of_quadrant(q, 4 * scales.shape[0]), :].bitcast(I32),
-                    scales[:, 4 * q : 4 * q + 4, :].bitcast(I32),
+                nc.sync.dma_start(
+                    planes[32 * q : 32 * q + 8, :].bitcast(I32), scales[:, 4 * q : 4 * q + 4, :].bitcast(I32)
                 )
 
-        def load_wv(a, first, last):
-            rows = wv[:, GROUP * a : GROUP * (a + 1)].rearrange("(p j) c -> p j c", j=PACK)
-            nc.sync.dma_start(wv_raw[a][:, first:last, :], rows[:, first:last, :])
+        def load_wv(a, u):
+            first = GROUP * a + GROUP // 2 * u
+            rows = wv[:, first : first + GROUP // 2].rearrange("(p j) c -> p j c", j=PACK)
+            nc.sync.dma_start(wv_raw[a][u][:], rows)
 
         nc.sync.dma_start(wg_raw[:].bitcast(I32), wg4_words[0].bitcast(I32))
         nc.sync.dma_start(offsets[:], offs)
-        load_wv(0, 0, 4)
-        load_planes((nc.sync,) * 4, table_planes, tab_scales)
-        nc.sync.dma_start(table[:].bitcast(I32), tab_words[0].rearrange("p t i -> p (t i)").bitcast(I32))
-        load_planes((nc.sync,) * 4, wg_planes_raw, wg4_scales)
         nc.sync.dma_start(bg_sb[:, :, 0:PACK], dealt(bg))
+        load_plane(table_planes, tab_scales)
+        nc.sync.dma_start(table[:].bitcast(I32), tab_words[0].rearrange("p t i -> p (t i)").bitcast(I32))
+        load_plane(wg_planes_raw, wg4_scales)
+        load_wv(0, 0)
+        load_wv(0, 1)
         nc.sync.dma_start(erev_sb[:, :, 0:PACK], dealt(erev))
-        load_wv(1, 0, 4)
+        load_wv(1, 0)
+        load_wv(1, 1)
         nc.sync.dma_start(wo_raw[:].bitcast(I32), wo8_words.rearrange("a p c i -> p a (c i)").bitcast(I32))
-        load_planes((nc.sync,) * 4, wo_planes_raw, wo8_scales)
+        load_packed_planes(wo_planes_raw, wo8_scales)
         nc.sync.dma_start(bo_sb[:, :, 0:PACK], dealt(bo))
 
         wg = sb("wg", [P, 2 * H], U8)
@@ -94,17 +107,18 @@ def tile_list_synaptic_channel_currents_kernel(
         wv_codes = [sb("wv_codes%d" % a, [P, GROUP], U32) for a in range(2)]
         wv_planes = [sb("wv_planes%d" % a, [P, GROUP], U8) for a in range(2)]
         v_codes = []
-        v_planes = [sb("v_planes%d" % c, [P, CHUNK], U8) for c in range(2)]
+        v_planes = [sb("v_planes%d" % half, [P, LOOKUP], U8) for half in range(2)]
         y_planes = sb("y_planes", [P, 2, S], U8)
-        units = [(c, a) for c in range(2) for a in range(2)]
-        g = {u: sb("g%d%d" % u, [P, PACK, CHUNK], F32) for u in units}
-        h_rows = {u: sb("h_rows%d%d" % u, [P, PACK, CHUNK], BF16) for u in units}
-        h_woven = {u: sb("h_woven%d%d" % u, [P, CHUNK, PACK], BF16) for u in units}
-        h_codes = {u: sb("h_codes%d%d" % u, [P, CHUNK], U32) for u in units}
-        h_planes = {u: sb("h_planes%d%d" % u, [P, CHUNK], U8) for u in units}
-        y = {u: sb("y%d%d" % u, [P, PACK, CHUNK], F32) for u in units}
-        y_woven = {u: sb("y_woven%d%d" % u, [P, CHUNK, PACK], BF16) for u in units}
-        y_codes = {u: sb("y_codes%d%d" % u, [P, CHUNK], U32) for u in units}
+        units = [(c, a) for c in range(len(CHUNKS)) for a in range(2)]
+        width = {u: CHUNKS[u[0]][1] for u in units}
+        g = []
+        h_rows = {u: sb("h_rows%d%d" % u, [P, PACK, width[u]], BF16) for u in units}
+        h_woven = {u: sb("h_woven%d%d" % u, [P, width[u], PACK], BF16) for u in units}
+        h_codes = {u: sb("h_codes%d%d" % u, [P, width[u]], U32) for u in units}
+        h_planes = {u: sb("h_planes%d%d" % u, [P, width[u]], U8) for u in units}
+        y = {u: sb("y%d%d" % u, [P, PACK, width[u]], F32) for u in units}
+        y_woven = {}
+        y_codes = [sb("y_codes%d" % c, [P, 2, CHUNKS[c][1]], U32) for c in range(len(CHUNKS))]
         wv_woven = [sb("wv_woven%d" % a, [P, PACK, P, PACK], BF16) for a in range(2)]
 
         def deal_wg(a):
@@ -127,15 +141,13 @@ def tile_list_synaptic_channel_currents_kernel(
             )
 
         def list_of(c):
-            return offsets[:, c * CHUNK // 16 : (c + 1) * CHUNK // 16]
+            return offsets[:, c * LOOKUP // 16 : (c + 1) * LOOKUP // 16]
 
-        def weave_wv(a):
-            split = WV_VECTOR_SHARE[a]
-            dst = wv_woven[a][:].rearrange("p t m j -> p m t j")
-            src = wv_raw[a][:].rearrange("p j (m t) -> p m t j", t=PACK)
-            if split:
-                nc.vector.tensor_scalar(dst[:, :split], src[:, :split], -1.0, None, ALU.mult)
-                nc.scalar.activation(dst[:, split:], src[:, split:], ACT.Copy, scale=-1.0)
+        def weave_wv(a, u, engine="scalar"):
+            dst = wv_woven[a][:, :, P // 2 * u : P // 2 * (u + 1), :].rearrange("p t m j -> p m t j")
+            src = wv_raw[a][u][:].rearrange("p j (m t) -> p m t j", t=PACK)
+            if engine == "vector":
+                nc.vector.tensor_scalar(dst, src, -1.0, None, ALU.mult)
             else:
                 nc.scalar.activation(dst, src, ACT.Copy, scale=-1.0)
 
@@ -146,44 +158,79 @@ def tile_list_synaptic_channel_currents_kernel(
                 in_=wv_woven[a][:].rearrange("p t m j -> p (t m j)"),
             )
 
-        def weave(engine, woven, rows, first, last):
-            dst = woven[:, first:last, :].rearrange("p (c i) t -> p c t i", i=4)
-            src = rows[:, :, first:last].rearrange("p t (c i) -> p c t i", i=4)
-            if engine == "vector":
-                nc.vector.tensor_copy(dst, src)
-            else:
-                nc.scalar.copy(dst, src)
+        def weave(woven, rows, share):
+            for engine, first, last in (("vector", 0, share), ("scalar", share, woven.shape[1])):
+                if first == last:
+                    continue
+                dst = woven[:, first:last, :].rearrange("p (c i) t -> p c t i", i=4)
+                src = rows[:, :, first:last].rearrange("p t (c i) -> p c t i", i=4)
+                if engine == "vector":
+                    nc.vector.tensor_copy(dst, src)
+                else:
+                    nc.scalar.copy(dst, src)
+
+        def looked_up(chunk):
+            half, first = divmod(chunk[0], LOOKUP)
+            cols = slice(first, first + chunk[1])
+            return v_codes[half][:, cols].bitcast(FP8X4), v_planes[half][:, cols]
+
+        def look_up_scales(half):
+            nc.vector.tensor_copy(v_planes[half][:], table_planes[:].indirect(list_of(half)))
+
+        def look_up_words(half, slot=None):
+            v_codes.append(sb("v_codes%d" % half, [P, LOOKUP], U32, tag=slot))
+            nc.vector.tensor_copy(v_codes[half][:], table[:].indirect(list_of(half)))
+
+        def bank_groups(w):
+            side = min(BANK // w, PACK)
+            return [range(t, t + side) for t in range(0, PACK, side)]
+
+        def part(acc, w, ts, t):
+            return acc[:, w * (t - ts[0]) : w * (t - ts[0] + 1)]
 
         def conductances(c, a):
-            for t in range(PACK):
-                col = GROUP * a + P * t
-                acc = bank((PACK * (2 * c + a) + t) % 3, "g_acc")
-                nc.tensor.matmul_mx(
-                    out=acc[:],
-                    lhsT=wg[:, 2 * col : 2 * (col + P)].bitcast(FP4X4),
-                    lhsT_scale=wg_planes[:, col : col + P],
-                    rhs=v_codes[c][:].bitcast(FP8X4),
-                    rhs_scale=v_planes[c][:],
-                    start=True,
-                    stop=True,
-                )
-                nc.scalar.activation(g[c, a][:, t, :], acc[:], ACT.Relu, bias=bg_sb[:, a, t : t + 1])
+            first, w = G_CHUNKS[c]
+            if c == 0:
+                g.append(sb("g%d" % a, [P, PACK, S], F32, tag=("wv_raw00", "wv_raw10")[a]))
+            codes, planes = looked_up(G_CHUNKS[c])
+            for ts in bank_groups(w):
+                acc = bank("g", G_BANKS)
+                for t in ts:
+                    col = GROUP * a + P * t
+                    nc.tensor.matmul_mx(
+                        out=part(acc, w, ts, t),
+                        lhsT=wg[:, 2 * col : 2 * (col + P)].bitcast(FP4X4),
+                        lhsT_scale=wg_planes[:, col : col + P],
+                        rhs=codes,
+                        rhs_scale=planes,
+                        start=True,
+                        stop=True,
+                    )
+                for t in ts:
+                    nc.scalar.activation(g[a][:, t, first : first + w], part(acc, w, ts, t), ACT.Relu, bias=bg_sb[:, a, t : t + 1])
 
         def currents(c, a):
-            for t in range(PACK):
-                acc = bank(3 + (PACK * (2 * c + a) + t) % 3, "d_acc")
-                nc.tensor.matmul_mx(
-                    out=acc[:],
-                    lhsT=wv_codes[a][:, P * t : P * (t + 1)].bitcast(FP8X4),
-                    lhsT_scale=wv_planes[a][:, P * t : P * (t + 1)],
-                    rhs=v_codes[c][:].bitcast(FP8X4),
-                    rhs_scale=v_planes[c][:],
-                    start=True,
-                    stop=True,
-                )
-                nc.vector.scalar_tensor_tensor(
-                    h_rows[c, a][:, t, :], acc[:], erev_sb[:, a, t : t + 1], g[c, a][:, t, :], ALU.add, ALU.mult
-                )
+            w = CHUNKS[c][1]
+            codes, planes = looked_up(CHUNKS[c])
+            for ts in bank_groups(w):
+                acc = bank("d", D_BANKS)
+                for t in ts:
+                    nc.tensor.matmul_mx(
+                        out=part(acc, w, ts, t),
+                        lhsT=wv_codes[a][:, P * t : P * (t + 1)].bitcast(FP8X4),
+                        lhsT_scale=wv_planes[a][:, P * t : P * (t + 1)],
+                        rhs=codes,
+                        rhs_scale=planes,
+                        start=True,
+                        stop=True,
+                    )
+                for t in ts:
+                    nc.vector.scalar_tensor_tensor(
+                        h_rows[c, a][:, t, :], part(acc, w, ts, t), erev_sb[:, a, t : t + 1], g[a][:, t, columns(c)], ALU.add, ALU.mult
+                    )
+
+        def weave_h(c, a):
+            weave(h_woven[c, a], h_rows[c, a], H_VECTOR_SHARE[c])
 
         def quantize_h(c, a):
             nc.vector.quantize_mx(
@@ -192,110 +239,129 @@ def tile_list_synaptic_channel_currents_kernel(
                 in_=h_woven[c, a][:].rearrange("p j t -> p (j t)"),
             )
 
-        def mix_pass(acc, c, b, t, a):
+        def columns(c):
+            return slice(CHUNKS[c][0], CHUNKS[c][0] + CHUNKS[c][1])
+
+        def mix_pass(acc, c, b, ts, t, a, start, stop):
             col = GROUP * b + P * t
             nc.tensor.matmul_mx(
-                out=acc[:],
+                out=part(acc, CHUNKS[c][1], ts, t),
                 lhsT=wo[b][:, a, P * t : P * (t + 1)].bitcast(FP8X4),
                 lhsT_scale=wo_planes[4 * a :, col : col + P],
                 rhs=h_codes[c, a][:].bitcast(FP8X4),
                 rhs_scale=h_planes[c, a][:],
-                start=(a == 0),
-                stop=(a == 1),
+                start=start,
+                stop=stop,
             )
 
-        def add_bias(engine, acc, c, b, t):
-            if engine == "vector":
-                nc.vector.tensor_scalar(y[c, b][:, t, :], acc[:], bo_sb[:, b, t : t + 1], None, ALU.add)
-            else:
-                nc.scalar.activation(y[c, b][:, t, :], acc[:], ACT.Identity, bias=bo_sb[:, b, t : t + 1])
+        def add_bias(acc, c, b, ts, on_vector, per_store):
+            rows = out_0[GROUP * b : GROUP * (b + 1), columns(c)].rearrange("(p t) j -> p t j", t=PACK)
+            for t in ts:
+                sums = part(acc, CHUNKS[c][1], ts, t)
+                if on_vector:
+                    nc.vector.tensor_scalar(y[c, b][:, t, :], sums, bo_sb[:, b, t : t + 1], None, ALU.add)
+                else:
+                    nc.scalar.activation(y[c, b][:, t, :], sums, ACT.Identity, bias=bo_sb[:, b, t : t + 1])
+                if (t + 1) % per_store == 0:
+                    nc.sync.dma_start(rows[:, t + 1 - per_store : t + 1, :], y[c, b][:, t + 1 - per_store : t + 1, :])
 
-        def store_y(c, b, first, last):
-            rows = out_0[GROUP * b : GROUP * (b + 1), CHUNK * c : CHUNK * (c + 1)].rearrange("(p t) j -> p t j", t=PACK)
-            nc.sync.dma_start(rows[:, first:last, :], y[c, b][:, first:last, :])
+        def mix(c, b, per_store=2):
+            for ts in bank_groups(CHUNKS[c][1]):
+                acc = bank("y", Y_BANKS)
+                for t in ts:
+                    for a in range(2):
+                        mix_pass(acc, c, b, ts, t, a, a == 0, a == 1)
+                add_bias(acc, c, b, ts, False, per_store)
+
+        def mix_last(c, banks, on_vector, per_store=2):
+            groups = [(b, ts) for b in range(2) for ts in bank_groups(CHUNKS[c][1])]
+            accs = [bank("y", banks) for group in groups]
+            for acc, (b, ts) in zip(accs, groups):
+                for t in ts:
+                    mix_pass(acc, c, b, ts, t, 0, t == ts[0], False)
+            for index, (b, ts) in enumerate(groups):
+                for t in ts:
+                    mix_pass(accs[index], c, b, ts, t, 1, False, t == ts[-1])
+                add_bias(accs[index], c, b, ts, index in on_vector, per_store)
+
+        def weave_y(c, b, slot=None):
+            y_woven[c, b] = sb("y_woven%d%d" % (c, b), [P, CHUNKS[c][1], PACK], BF16, tag=slot)
+            weave(y_woven[c, b], y[c, b], Y_VECTOR_SHARE[c])
 
         def quantize_y(c, b):
             nc.vector.quantize_mx(
-                out=y_codes[c, b][:].bitcast(FP8X4),
-                scales=y_planes[:, b, CHUNK * c : CHUNK * (c + 1)],
+                out=y_codes[c][:, b, :].bitcast(FP8X4),
+                scales=y_planes[:, b, columns(c)],
                 in_=y_woven[c, b][:].rearrange("p j t -> p (j t)"),
             )
-            words = out_1[b].rearrange("p m t -> p (m t)")[:, 4 * CHUNK * c : 4 * CHUNK * (c + 1)]
-            nc.sync.dma_start(words.bitcast(I32), y_codes[c, b][:].bitcast(I32))
 
-        def weave_h(c, a):
-            weave("vector", h_woven[c, a], h_rows[c, a], 0, H_VECTOR_SHARE)
-            weave("scalar", h_woven[c, a], h_rows[c, a], H_VECTOR_SHARE, CHUNK)
+        def store_y_codes(c, first, last):
+            words = out_1.rearrange("b p m t -> p b (m t)").bitcast(I32)[:, first:last, columns(c)]
+            nc.sync.dma_start(words, y_codes[c][:, first:last, :].bitcast(I32))
 
-        def weave_y(c, b):
-            weave("vector", y_woven[c, b], y[c, b], 0, Y_VECTOR_SHARE)
-            weave("scalar", y_woven[c, b], y[c, b], Y_VECTOR_SHARE, CHUNK)
-
-        def mix_early(c, b):
-            for t in range(PACK):
-                acc = bank(6 + t % 2, "y_acc")
-                for a in range(2):
-                    mix_pass(acc, c, b, t, a)
-                add_bias("scalar", acc, c, b, t)
-                store_y(c, b, t, t + 1)
-
-        def mix_late(c, b, banks):
-            accs = [bank(index, "y_acc") for index in banks]
-            for t in range(PACK):
-                mix_pass(accs[t], c, b, t, 0)
-            for t in range(PACK):
-                mix_pass(accs[t], c, b, t, 1)
-                add_bias("vector" if t == 0 else "scalar", accs[t], c, b, t)
-                store_y(c, b, t, t + 1)
+        def store_y_planes(first, last, queues):
+            rows = out_2[:, :, first:last].rearrange("b (q r) m -> r q b m", r=4)
+            for r in range(4):
+                queues[r % len(queues)].dma_start(rows[r].bitcast(I32), y_planes[r:P:32, :, first:last].bitcast(I32))
 
         for a in range(2):
             deal_wg(a)
-        weave_wv(0)
-        for c in range(2):
-            nc.vector.tensor_copy(v_planes[c][:], table_planes[:].indirect(list_of(c)))
-        quantize_wv(0)
-        v_codes.append(sb("v_codes0", [P, CHUNK], U32))
-        nc.vector.tensor_copy(v_codes[0][:], table[:].indirect(list_of(0)))
+        look_up_scales(0)
+        look_up_scales(1)
+        look_up_words(0)
         deal_planes(wg_planes, wg_planes_raw)
-        v_codes.append(sb("v_codes1", [P, CHUNK], U32, tag="wg_planes_raw"))
-        nc.vector.tensor_copy(v_codes[1][:], table[:].indirect(list_of(1)))
+        weave_wv(0, 0)
+        weave_wv(0, 1, "vector")
+        quantize_wv(0)
+        look_up_words(1, "wg_planes_raw")
 
         conductances(0, 0)
-        weave_wv(1)
         currents(0, 0)
+        weave_wv(1, 0)
+        weave_wv(1, 1, "scalar")
         quantize_wv(1)
         conductances(0, 1)
-        weave_h(0, 0)
         currents(0, 1)
+        weave_h(0, 0)
         quantize_h(0, 0)
         weave_h(0, 1)
+        quantize_h(0, 1)
         deal_wo(0)
         deal_planes(wo_planes, wo_planes_raw)
         deal_wo(1)
-        quantize_h(0, 1)
-        conductances(1, 0)
-        currents(1, 0)
-        conductances(1, 1)
-        mix_early(0, 0)
-        currents(1, 1)
-        weave_h(1, 0)
-        weave_h(1, 1)
-        mix_early(0, 1)
-        quantize_h(1, 0)
-        quantize_h(1, 1)
-        weave_y(0, 0)
-        mix_late(1, 0, (0, 1, 2, 3))
-        quantize_y(0, 0)
-        weave_y(0, 1)
-        mix_late(1, 1, (4, 5, 6, 7))
-        quantize_y(0, 1)
-        weave_y(1, 0)
-        weave_y(1, 1)
-        quantize_y(1, 0)
-        quantize_y(1, 1)
-        for q in range(QUADRANTS):
-            queue = nc.sync if q % 2 == 0 else nc.scalar
-            queue.dma_start(
-                out_2[:, 4 * q : 4 * q + 4, :].rearrange("b r m -> r b m").bitcast(I32),
-                y_planes[rows_of_quadrant(q, 4), :, :].bitcast(I32),
-            )
+        last = len(CHUNKS) - 1
+        made = 1
+
+        def finish(c):
+            for b in range(2):
+                weave_y(c, b)
+            for b in range(2):
+                quantize_y(c, b)
+            store_y_codes(c, 0, 2)
+
+        for c in range(1, last + 1):
+            fresh = CHUNKS[c][0] + CHUNKS[c][1] > G_CHUNKS[made - 1][0] + G_CHUNKS[made - 1][1]
+            if fresh:
+                conductances(made, 0)
+            mix(c - 1, 0, 4)
+            currents(c, 0)
+            if fresh:
+                conductances(made, 1)
+                made = made + 1
+            mix(c - 1, 1, 4)
+            weave_h(c, 0)
+            currents(c, 1)
+            quantize_h(c, 0)
+            weave_h(c, 1)
+            quantize_h(c, 1)
+            if c == last:
+                mix_last(c, G_BANKS + D_BANKS, (0,), 4)
+            if c >= 2:
+                finish(c - 2)
+        finish(last - 1)
+        weave_y(last, 0)
+        weave_y(last, 1)
+        for b in range(2):
+            quantize_y(last, b)
+            store_y_codes(last, b, b + 1)
+        store_y_planes(0, S, (nc.scalar, nc.sync))

@@ -29,7 +29,7 @@ G_BANKS = (0, 1, 2,)
 D_BANKS = (3, 4, 5,)
 Y_BANKS = (6, 7,)
 H_VECTOR_SHARE = (192, 192, 192, 192,)
-Y_VECTOR_SHARE = (128, 128, 128, 192,)
+Y_VECTOR_SHARE = (160, 160, 160, 160,)
 
 
 def tile_list_synaptic_channel_currents_kernel(
@@ -53,10 +53,12 @@ def tile_list_synaptic_channel_currents_kernel(
         offsets = keep.tile([P, S // 16], U16, name="offsets")
         table = sb("table", [P, T], U32)
         table_planes = sb("table_planes", [P, T], U8)
-        wg_raw = sb("wg_raw", [P, 2 * H], U8)
+        wg_raw = [sb("wg_raw%d" % a, [P, H], U8) for a in range(2)]
         wg_planes_raw = sb("wg_planes_raw", [P, H], U8)
         wo_planes_raw = sb("wo_planes_raw", [P, N], U8)
-        wv_raw = [[sb("wv_raw%d%d" % (a, u), [P, PACK, GROUP // 2], F32) for u in range(2)] for a in range(2)]
+        wv_first = [sb("wv_raw0%d" % u, [P, PACK, GROUP // 2], F32) for u in range(2)]
+        wv_second = sb("wv_raw10", [P, PACK, GROUP], F32)
+        wv_raw = [[half[:] for half in wv_first], [wv_second[:, :, : GROUP // 2], wv_second[:, :, GROUP // 2 :]]]
         wo_raw = sb("wo_raw", [P, 2, N], U32)
         bg_sb = sb("bg_sb", [P, 2, 8], F32)
         erev_sb = sb("erev_sb", [P, 2, 8], F32)
@@ -83,19 +85,19 @@ def tile_list_synaptic_channel_currents_kernel(
         def load_wv(a, u):
             first = GROUP * a + GROUP // 2 * u
             rows = wv[:, first : first + GROUP // 2].rearrange("(p j) c -> p j c", j=PACK)
-            nc.sync.dma_start(wv_raw[a][u][:], rows)
+            nc.sync.dma_start(wv_raw[a][u], rows)
 
-        nc.sync.dma_start(wg_raw[:].bitcast(I32), wg4_words[0].bitcast(I32))
+        for a in range(2):
+            nc.sync.dma_start(wg_raw[a][:].bitcast(I32), wg4_words[0][:, H * a : H * (a + 1)].bitcast(I32))
         nc.sync.dma_start(offsets[:], offs)
-        nc.sync.dma_start(bg_sb[:, :, 0:PACK], dealt(bg))
         load_plane(table_planes, tab_scales)
         nc.sync.dma_start(table[:].bitcast(I32), tab_words[0].rearrange("p t i -> p (t i)").bitcast(I32))
         load_plane(wg_planes_raw, wg4_scales)
+        nc.sync.dma_start(bg_sb[:, :, 0:PACK], dealt(bg))
         load_wv(0, 0)
         load_wv(0, 1)
         nc.sync.dma_start(erev_sb[:, :, 0:PACK], dealt(erev))
-        load_wv(1, 0)
-        load_wv(1, 1)
+        nc.sync.dma_start(wv_second[:], wv[:, GROUP:].rearrange("(p j) c -> p j c", j=PACK))
         nc.sync.dma_start(wo_raw[:].bitcast(I32), wo8_words.rearrange("a p c i -> p a (c i)").bitcast(I32))
         load_packed_planes(wo_planes_raw, wo8_scales)
         nc.sync.dma_start(bo_sb[:, :, 0:PACK], dealt(bo))
@@ -125,7 +127,7 @@ def tile_list_synaptic_channel_currents_kernel(
             cols = slice(2 * GROUP * a, 2 * GROUP * (a + 1))
             nc.vector.tensor_copy(
                 wg[:, cols].rearrange("p (t k i e) -> p k t i e", t=PACK, i=8, e=2),
-                wg_raw[:, cols].rearrange("p (k i t e) -> p k t i e", t=PACK, i=8, e=2),
+                wg_raw[a][:].rearrange("p (k i t e) -> p k t i e", t=PACK, i=8, e=2),
             )
 
         def deal_planes(dst, src):
@@ -145,7 +147,7 @@ def tile_list_synaptic_channel_currents_kernel(
 
         def weave_wv(a, u, engine="scalar"):
             dst = wv_woven[a][:, :, P // 2 * u : P // 2 * (u + 1), :].rearrange("p t m j -> p m t j")
-            src = wv_raw[a][u][:].rearrange("p j (m t) -> p m t j", t=PACK)
+            src = wv_raw[a][u].rearrange("p j (m t) -> p m t j", t=PACK)
             if engine == "vector":
                 nc.vector.tensor_scalar(dst, src, -1.0, None, ALU.mult)
             else:
@@ -265,9 +267,9 @@ def tile_list_synaptic_channel_currents_kernel(
                 if (t + 1) % per_store == 0:
                     nc.sync.dma_start(rows[:, t + 1 - per_store : t + 1, :], y[c, b][:, t + 1 - per_store : t + 1, :])
 
-        def mix(c, b, per_store=2):
+        def mix(c, b, per_store=2, banks=Y_BANKS):
             for ts in bank_groups(CHUNKS[c][1]):
-                acc = bank("y", Y_BANKS)
+                acc = bank("y", banks)
                 for t in ts:
                     for a in range(2):
                         mix_pass(acc, c, b, ts, t, a, a == 0, a == 1)
@@ -310,14 +312,14 @@ def tile_list_synaptic_channel_currents_kernel(
         look_up_scales(1)
         look_up_words(0)
         deal_planes(wg_planes, wg_planes_raw)
-        weave_wv(0, 0)
+        weave_wv(0, 0, "scalar")
         weave_wv(0, 1, "vector")
         quantize_wv(0)
         look_up_words(1, "wg_planes_raw")
 
         conductances(0, 0)
         currents(0, 0)
-        weave_wv(1, 0)
+        weave_wv(1, 0, "vector")
         weave_wv(1, 1, "scalar")
         quantize_wv(1)
         conductances(0, 1)
@@ -330,38 +332,35 @@ def tile_list_synaptic_channel_currents_kernel(
         deal_planes(wo_planes, wo_planes_raw)
         deal_wo(1)
         last = len(CHUNKS) - 1
-        made = 1
 
         def finish(c):
             for b in range(2):
                 weave_y(c, b)
             for b in range(2):
                 quantize_y(c, b)
-            store_y_codes(c, 0, 2)
+                if c == last:
+                    store_y_codes(c, b, b + 1)
+            if c < last:
+                store_y_codes(c, 0, 2)
 
         for c in range(1, last + 1):
-            fresh = CHUNKS[c][0] + CHUNKS[c][1] > G_CHUNKS[made - 1][0] + G_CHUNKS[made - 1][1]
-            if fresh:
-                conductances(made, 0)
-            mix(c - 1, 0, 4)
+            banks = Y_BANKS if c == 1 else G_BANKS[:2] + Y_BANKS
             currents(c, 0)
-            if fresh:
-                conductances(made, 1)
-                made = made + 1
-            mix(c - 1, 1, 4)
             weave_h(c, 0)
             currents(c, 1)
             quantize_h(c, 0)
             weave_h(c, 1)
             quantize_h(c, 1)
+            mix(c - 1, 0, 2, banks)
+            if c == 1:
+                conductances(1, 0)
+            mix(c - 1, 1, 2, banks)
+            if c == 1:
+                conductances(1, 1)
             if c == last:
-                mix_last(c, G_BANKS + D_BANKS, (0,), 4)
-            if c >= 2:
-                finish(c - 2)
-        finish(last - 1)
-        weave_y(last, 0)
-        weave_y(last, 1)
-        for b in range(2):
-            quantize_y(last, b)
-            store_y_codes(last, b, b + 1)
+                mix_last(c, D_BANKS + G_BANKS[2:], (1,), 2)
+            if c >= 3:
+                finish(c - 3)
+        for c in range(last + 1 - 3, last + 1):
+            finish(c)
         store_y_planes(0, S, (nc.scalar, nc.sync))

@@ -24,7 +24,7 @@ LOOKUP = 512
 QUADRANTS = 4
 
 CHUNKS = ((0,256),(256,256),(512,256),(768,256))
-G_CHUNKS = ((0,512),(512,512))
+G_CHUNKS = ((0,256),(256,256),(512,512))
 G_BANKS = (0, 1, 2,)
 D_BANKS = (3, 4, 5,)
 Y_BANKS = (6, 7,)
@@ -53,7 +53,7 @@ def tile_list_synaptic_channel_currents_kernel(
         offsets = keep.tile([P, S // 16], U16, name="offsets")
         table = sb("table", [P, T], U32)
         table_planes = sb("table_planes", [P, T], U8)
-        wg_raw = [sb("wg_raw%d" % a, [P, H], U8) for a in range(2)]
+        wg_raw = sb("wg_raw", [P, 2 * H], U8)
         wg_planes_raw = sb("wg_planes_raw", [P, H], U8)
         wo_planes_raw = sb("wo_planes_raw", [P, N], U8)
         wv_first = [sb("wv_raw0%d" % u, [P, PACK, GROUP // 2], F32) for u in range(2)]
@@ -64,9 +64,13 @@ def tile_list_synaptic_channel_currents_kernel(
         erev_sb = sb("erev_sb", [P, 2, 8], F32)
         bo_sb = sb("bo_sb", [P, 2, 8], F32)
 
-        nc.vector.memset(table_planes[:].bitcast(I32), 0)
         nc.vector.memset(wg_planes_raw[:].bitcast(I32), 0)
+        nc.vector.memset(table_planes[:].bitcast(I32), 0)
         nc.vector.memset(wo_planes_raw[:].bitcast(I32), 0)
+
+        v_rows = sb("v_rows", [P, S], U8)
+        v_plane = sb("v_plane", [P, S], U8)
+        nc.vector.memset(v_plane[:].bitcast(I32), 0)
 
         def dealt(vec):
             return vec.rearrange("(a p t) -> p a t", p=P, t=PACK)
@@ -87,14 +91,16 @@ def tile_list_synaptic_channel_currents_kernel(
             rows = wv[:, first : first + GROUP // 2].rearrange("(p j) c -> p j c", j=PACK)
             nc.sync.dma_start(wv_raw[a][u], rows)
 
-        for a in range(2):
-            nc.sync.dma_start(wg_raw[a][:].bitcast(I32), wg4_words[0][:, H * a : H * (a + 1)].bitcast(I32))
+        nc.sync.dma_start(wg_raw[:].bitcast(I32), wg4_words[0].bitcast(I32))
         nc.sync.dma_start(offsets[:], offs)
-        load_plane(table_planes, tab_scales)
-        nc.sync.dma_start(table[:].bitcast(I32), tab_words[0].rearrange("p t i -> p (t i)").bitcast(I32))
         load_plane(wg_planes_raw, wg4_scales)
-        nc.sync.dma_start(bg_sb[:, :, 0:PACK], dealt(bg))
+        nc.sync.dma_start(table_planes[0:16, :].bitcast(I32), tab_scales[0].bitcast(I32))
+        nc.sync.dma_start(table[:].bitcast(I32), tab_words[0].rearrange("p t i -> p (t i)").bitcast(I32))
         load_wv(0, 0)
+        nc.vector.tensor_copy(v_rows[:], table_planes[:].indirect(offsets[:]))
+        for q in range(QUADRANTS):
+            nc.sync.dma_start(v_plane[32 * q : 32 * q + 4, :].bitcast(I32), v_rows[4 * q : 4 * q + 4, :].bitcast(I32))
+        nc.sync.dma_start(bg_sb[:, :, 0:PACK], dealt(bg))
         load_wv(0, 1)
         nc.sync.dma_start(erev_sb[:, :, 0:PACK], dealt(erev))
         nc.sync.dma_start(wv_second[:], wv[:, GROUP:].rearrange("(p j) c -> p j c", j=PACK))
@@ -109,11 +115,11 @@ def tile_list_synaptic_channel_currents_kernel(
         wv_codes = [sb("wv_codes%d" % a, [P, GROUP], U32) for a in range(2)]
         wv_planes = [sb("wv_planes%d" % a, [P, GROUP], U8) for a in range(2)]
         v_codes = []
-        v_planes = [sb("v_planes%d" % half, [P, LOOKUP], U8) for half in range(2)]
+        v_planes = [v_plane[:, LOOKUP * half : LOOKUP * (half + 1)] for half in range(2)]
         y_planes = sb("y_planes", [P, 2, S], U8)
         units = [(c, a) for c in range(len(CHUNKS)) for a in range(2)]
         width = {u: CHUNKS[u[0]][1] for u in units}
-        g = []
+        g = {}
         h_rows = {u: sb("h_rows%d%d" % u, [P, PACK, width[u]], BF16) for u in units}
         h_woven = {u: sb("h_woven%d%d" % u, [P, width[u], PACK], BF16) for u in units}
         h_codes = {u: sb("h_codes%d%d" % u, [P, width[u]], U32) for u in units}
@@ -121,13 +127,13 @@ def tile_list_synaptic_channel_currents_kernel(
         y = {u: sb("y%d%d" % u, [P, PACK, width[u]], F32) for u in units}
         y_woven = {}
         y_codes = [sb("y_codes%d" % c, [P, 2, CHUNKS[c][1]], U32) for c in range(len(CHUNKS))]
-        wv_woven = [sb("wv_woven%d" % a, [P, PACK, P, PACK], BF16) for a in range(2)]
+        wv_woven = [sb("wv_woven0", [P, PACK, P, PACK], BF16)]
 
         def deal_wg(a):
             cols = slice(2 * GROUP * a, 2 * GROUP * (a + 1))
             nc.vector.tensor_copy(
                 wg[:, cols].rearrange("p (t k i e) -> p k t i e", t=PACK, i=8, e=2),
-                wg_raw[a][:].rearrange("p (k i t e) -> p k t i e", t=PACK, i=8, e=2),
+                wg_raw[:, cols].rearrange("p (k i t e) -> p k t i e", t=PACK, i=8, e=2),
             )
 
         def deal_planes(dst, src):
@@ -153,12 +159,15 @@ def tile_list_synaptic_channel_currents_kernel(
             else:
                 nc.scalar.activation(dst, src, ACT.Copy, scale=-1.0)
 
-        def quantize_wv(a):
-            nc.vector.quantize_mx(
-                out=wv_codes[a][:].bitcast(FP8X4),
-                scales=wv_planes[a][:],
-                in_=wv_woven[a][:].rearrange("p t m j -> p (t m j)"),
-            )
+        def quantize_wv(a, calls=1):
+            slices = PACK // calls
+            for first in range(0, PACK, slices):
+                cols = slice(P * first, P * (first + slices))
+                nc.vector.quantize_mx(
+                    out=wv_codes[a][:, cols].bitcast(FP8X4),
+                    scales=wv_planes[a][:, cols],
+                    in_=wv_woven[a][:, first : first + slices].rearrange("p t m j -> p (t m j)"),
+                )
 
         def weave(woven, rows, share):
             for engine, first, last in (("vector", 0, share), ("scalar", share, woven.shape[1])):
@@ -176,9 +185,6 @@ def tile_list_synaptic_channel_currents_kernel(
             cols = slice(first, first + chunk[1])
             return v_codes[half][:, cols].bitcast(FP8X4), v_planes[half][:, cols]
 
-        def look_up_scales(half):
-            nc.vector.tensor_copy(v_planes[half][:], table_planes[:].indirect(list_of(half)))
-
         def look_up_words(half, slot=None):
             v_codes.append(sb("v_codes%d" % half, [P, LOOKUP], U32, tag=slot))
             nc.vector.tensor_copy(v_codes[half][:], table[:].indirect(list_of(half)))
@@ -191,9 +197,8 @@ def tile_list_synaptic_channel_currents_kernel(
             return acc[:, w * (t - ts[0]) : w * (t - ts[0] + 1)]
 
         def conductances(c, a):
-            first, w = G_CHUNKS[c]
-            if c == 0:
-                g.append(sb("g%d" % a, [P, PACK, S], F32, tag=("wv_raw00", "wv_raw10")[a]))
+            w = G_CHUNKS[c][1]
+            g[c, a] = sb("g%d%d" % (c, a), [P, PACK, w], F32, tag="wv_raw0%d" % a if c == 0 else None)
             codes, planes = looked_up(G_CHUNKS[c])
             for ts in bank_groups(w):
                 acc = bank("g", G_BANKS)
@@ -209,10 +214,13 @@ def tile_list_synaptic_channel_currents_kernel(
                         stop=True,
                     )
                 for t in ts:
-                    nc.scalar.activation(g[a][:, t, first : first + w], part(acc, w, ts, t), ACT.Relu, bias=bg_sb[:, a, t : t + 1])
+                    nc.scalar.activation(g[c, a][:, t, :], part(acc, w, ts, t), ACT.Relu, bias=bg_sb[:, a, t : t + 1])
 
         def currents(c, a):
             w = CHUNKS[c][1]
+            held = max(i for i, chunk in enumerate(G_CHUNKS) if chunk[0] <= CHUNKS[c][0])
+            offset = CHUNKS[c][0] - G_CHUNKS[held][0]
+            gates = g[held, a][:, :, offset : offset + w]
             codes, planes = looked_up(CHUNKS[c])
             for ts in bank_groups(w):
                 acc = bank("d", D_BANKS)
@@ -228,7 +236,7 @@ def tile_list_synaptic_channel_currents_kernel(
                     )
                 for t in ts:
                     nc.vector.scalar_tensor_tensor(
-                        h_rows[c, a][:, t, :], part(acc, w, ts, t), erev_sb[:, a, t : t + 1], g[a][:, t, columns(c)], ALU.add, ALU.mult
+                        h_rows[c, a][:, t, :], part(acc, w, ts, t), erev_sb[:, a, t : t + 1], gates[:, t, :], ALU.add, ALU.mult
                     )
 
         def weave_h(c, a):
@@ -308,23 +316,24 @@ def tile_list_synaptic_channel_currents_kernel(
 
         for a in range(2):
             deal_wg(a)
-        look_up_scales(0)
-        look_up_scales(1)
-        look_up_words(0)
         deal_planes(wg_planes, wg_planes_raw)
+        look_up_words(0)
         weave_wv(0, 0, "scalar")
         weave_wv(0, 1, "vector")
-        quantize_wv(0)
-        look_up_words(1, "wg_planes_raw")
+        quantize_wv(0, 2)
+        look_up_words(1)
 
         conductances(0, 0)
+        conductances(0, 1)
+        conductances(1, 0)
         currents(0, 0)
+        wv_woven.append(sb("wv_woven1", [P, PACK, P, PACK], BF16, tag="wv_raw00"))
         weave_wv(1, 0, "vector")
         weave_wv(1, 1, "scalar")
         quantize_wv(1)
-        conductances(0, 1)
-        currents(0, 1)
         weave_h(0, 0)
+        currents(1, 0)
+        currents(0, 1)
         quantize_h(0, 0)
         weave_h(0, 1)
         quantize_h(0, 1)
@@ -345,18 +354,21 @@ def tile_list_synaptic_channel_currents_kernel(
 
         for c in range(1, last + 1):
             banks = Y_BANKS if c == 1 else G_BANKS[:2] + Y_BANKS
-            currents(c, 0)
+            if c > 1:
+                currents(c, 0)
             weave_h(c, 0)
+            if c == 1:
+                conductances(1, 1)
             currents(c, 1)
             quantize_h(c, 0)
             weave_h(c, 1)
             quantize_h(c, 1)
             mix(c - 1, 0, 2, banks)
             if c == 1:
-                conductances(1, 0)
+                conductances(2, 0)
             mix(c - 1, 1, 2, banks)
             if c == 1:
-                conductances(1, 1)
+                conductances(2, 1)
             if c == last:
                 mix_last(c, D_BANKS + G_BANKS[2:], (1,), 2)
             if c >= 3:

@@ -25,6 +25,7 @@ QUADRANTS = 4
 
 CHUNKS = ((0,256),(256,256),(512,256),(768,256))
 G_CHUNKS = ((0,256),(256,256),(512,512))
+WV_VECTOR_SHARE = (80, 64)
 G_BANKS = (0, 1, 2,)
 D_BANKS = (3, 4, 5,)
 Y_BANKS = (6, 7,)
@@ -56,9 +57,7 @@ def tile_list_synaptic_channel_currents_kernel(
         wg_raw = sb("wg_raw", [P, 2 * H], U8)
         wg_planes_raw = sb("wg_planes_raw", [P, H], U8)
         wo_planes_raw = sb("wo_planes_raw", [P, N], U8)
-        wv_first = [sb("wv_raw0%d" % u, [P, PACK, GROUP // 2], F32) for u in range(2)]
-        wv_second = sb("wv_raw10", [P, PACK, GROUP], F32)
-        wv_raw = [[half[:] for half in wv_first], [wv_second[:, :, : GROUP // 2], wv_second[:, :, GROUP // 2 :]]]
+        wv_raw = [sb("wv_raw%d" % a, [P, PACK, GROUP], F32) for a in range(2)]
         wo_raw = sb("wo_raw", [P, 2, N], U32)
         bg_sb = sb("bg_sb", [P, 2, 8], F32)
         erev_sb = sb("erev_sb", [P, 2, 8], F32)
@@ -86,24 +85,22 @@ def tile_list_synaptic_channel_currents_kernel(
                     planes[32 * q : 32 * q + 8, :].bitcast(I32), scales[:, 4 * q : 4 * q + 4, :].bitcast(I32)
                 )
 
-        def load_wv(a, u):
-            first = GROUP * a + GROUP // 2 * u
-            rows = wv[:, first : first + GROUP // 2].rearrange("(p j) c -> p j c", j=PACK)
-            nc.sync.dma_start(wv_raw[a][u], rows)
+        def load_wv(a):
+            rows = wv[:, GROUP * a : GROUP * (a + 1)].rearrange("(p j) c -> p j c", j=PACK)
+            nc.sync.dma_start(wv_raw[a][:], rows)
 
         nc.sync.dma_start(wg_raw[:].bitcast(I32), wg4_words[0].bitcast(I32))
         nc.sync.dma_start(offsets[:], offs)
         load_plane(wg_planes_raw, wg4_scales)
-        nc.sync.dma_start(table_planes[0:16, :].bitcast(I32), tab_scales[0].bitcast(I32))
+        nc.sync.dma_start(table_planes[0:P:8, :].bitcast(I32), tab_scales[0].bitcast(I32))
         nc.sync.dma_start(table[:].bitcast(I32), tab_words[0].rearrange("p t i -> p (t i)").bitcast(I32))
-        load_wv(0, 0)
+        load_wv(0)
         nc.vector.tensor_copy(v_rows[:], table_planes[:].indirect(offsets[:]))
         for q in range(QUADRANTS):
-            nc.sync.dma_start(v_plane[32 * q : 32 * q + 4, :].bitcast(I32), v_rows[4 * q : 4 * q + 4, :].bitcast(I32))
+            nc.sync.dma_start(v_plane[32 * q : 32 * q + 4, :].bitcast(I32), v_rows[32 * q : 32 * (q + 1) : 8, :].bitcast(I32))
         nc.sync.dma_start(bg_sb[:, :, 0:PACK], dealt(bg))
-        load_wv(0, 1)
         nc.sync.dma_start(erev_sb[:, :, 0:PACK], dealt(erev))
-        nc.sync.dma_start(wv_second[:], wv[:, GROUP:].rearrange("(p j) c -> p j c", j=PACK))
+        load_wv(1)
         nc.sync.dma_start(wo_raw[:].bitcast(I32), wo8_words.rearrange("a p c i -> p a (c i)").bitcast(I32))
         load_packed_planes(wo_planes_raw, wo8_scales)
         nc.sync.dma_start(bo_sb[:, :, 0:PACK], dealt(bo))
@@ -151,13 +148,12 @@ def tile_list_synaptic_channel_currents_kernel(
         def list_of(c):
             return offsets[:, c * LOOKUP // 16 : (c + 1) * LOOKUP // 16]
 
-        def weave_wv(a, u, engine="scalar"):
-            dst = wv_woven[a][:, :, P // 2 * u : P // 2 * (u + 1), :].rearrange("p t m j -> p m t j")
-            src = wv_raw[a][u].rearrange("p j (m t) -> p m t j", t=PACK)
-            if engine == "vector":
-                nc.vector.tensor_scalar(dst, src, -1.0, None, ALU.mult)
-            else:
-                nc.scalar.activation(dst, src, ACT.Copy, scale=-1.0)
+        def weave_wv(a):
+            split = WV_VECTOR_SHARE[a]
+            dst = wv_woven[a][:].rearrange("p t m j -> p m t j")
+            src = wv_raw[a][:].rearrange("p j (m t) -> p m t j", t=PACK)
+            nc.vector.tensor_scalar(dst[:, :split], src[:, :split], -1.0, None, ALU.mult)
+            nc.scalar.activation(dst[:, split:], src[:, split:], ACT.Copy, scale=-1.0)
 
         def quantize_wv(a, calls=1):
             slices = PACK // calls
@@ -198,7 +194,7 @@ def tile_list_synaptic_channel_currents_kernel(
 
         def conductances(c, a):
             w = G_CHUNKS[c][1]
-            g[c, a] = sb("g%d%d" % (c, a), [P, PACK, w], F32, tag="wv_raw0%d" % a if c == 0 else None)
+            g[c, a] = sb("g%d%d" % (c, a), [P, PACK, w], F32)
             codes, planes = looked_up(G_CHUNKS[c])
             for ts in bank_groups(w):
                 acc = bank("g", G_BANKS)
@@ -318,8 +314,7 @@ def tile_list_synaptic_channel_currents_kernel(
             deal_wg(a)
         deal_planes(wg_planes, wg_planes_raw)
         look_up_words(0)
-        weave_wv(0, 0, "scalar")
-        weave_wv(0, 1, "vector")
+        weave_wv(0)
         quantize_wv(0, 2)
         look_up_words(1)
 
@@ -327,9 +322,8 @@ def tile_list_synaptic_channel_currents_kernel(
         conductances(0, 1)
         conductances(1, 0)
         currents(0, 0)
-        wv_woven.append(sb("wv_woven1", [P, PACK, P, PACK], BF16, tag="wv_raw00"))
-        weave_wv(1, 0, "vector")
-        weave_wv(1, 1, "scalar")
+        wv_woven.append(sb("wv_woven1", [P, PACK, P, PACK], BF16, tag="g00"))
+        weave_wv(1)
         quantize_wv(1)
         weave_h(0, 0)
         currents(1, 0)

@@ -39,10 +39,14 @@ def tile_list_synaptic_channel_currents_kernel(
     nc = tc.nc
     with ExitStack() as ctx:
         keep = ctx.enter_context(tc.tile_pool(name="keep", bufs=1))
+        head = ctx.enter_context(tc.tile_pool(name="head", bufs=1))
         psum = ctx.enter_context(tc.psum_pool(name="psum", bufs=1))
 
         def sb(name, shape, dtype, tag=None):
             return keep.tile(shape, dtype, name=name, tag=tag or name, align_bytes=64)
+
+        def placed(name, shape, dtype, offset):
+            return head.tile(shape, dtype, name=name, align_bytes=64, offset=offset)
 
         taken = {"g": 0, "d": 0, "y": 0}
 
@@ -53,7 +57,7 @@ def tile_list_synaptic_channel_currents_kernel(
 
         offsets = keep.tile([P, S // 16], U16, name="offsets")
         table = sb("table", [P, T], U32)
-        table_planes = sb("table_planes", [P, T], U8)
+        table_planes = placed("table_planes", [P, T], U8, 0)
         wg_raw = sb("wg_raw", [P, 2 * H], U8)
         wg_planes_raw = sb("wg_planes_raw", [P, H], U8)
         wo_planes_raw = sb("wo_planes_raw", [P, N], U8)
@@ -85,6 +89,13 @@ def tile_list_synaptic_channel_currents_kernel(
                     planes[32 * q : 32 * q + 8, :].bitcast(I32), scales[:, 4 * q : 4 * q + 4, :].bitcast(I32)
                 )
 
+        def deal_wg(a):
+            cols = slice(2 * GROUP * a, 2 * GROUP * (a + 1))
+            nc.vector.tensor_copy(
+                wg[a][:].bitcast(U16).rearrange("p (t k i) -> p k t i", t=PACK, i=8),
+                wg_raw[:, cols].bitcast(U16).rearrange("p (k i t) -> p k t i", t=PACK, i=8),
+            )
+
         def load_wv(a):
             rows = wv[:, GROUP * a : GROUP * (a + 1)].rearrange("(p j) c -> p j c", j=PACK)
             nc.sync.dma_start(wv_raw[a][:], rows)
@@ -95,6 +106,8 @@ def tile_list_synaptic_channel_currents_kernel(
         nc.sync.dma_start(table_planes[0:P:8, :].bitcast(I32), tab_scales[0].bitcast(I32))
         nc.sync.dma_start(table[:].bitcast(I32), tab_words[0].rearrange("p t i -> p (t i)").bitcast(I32))
         load_wv(0)
+        wg = [sb("wg0", [P, 2 * GROUP], U8)]
+        deal_wg(0)
         nc.vector.tensor_copy(v_rows[:], table_planes[:].indirect(offsets[:]))
         for q in range(QUADRANTS):
             nc.sync.dma_start(v_plane[32 * q : 32 * q + 4, :].bitcast(I32), v_rows[32 * q : 32 * (q + 1) : 8, :].bitcast(I32))
@@ -105,8 +118,8 @@ def tile_list_synaptic_channel_currents_kernel(
         load_packed_planes(wo_planes_raw, wo8_scales)
         nc.sync.dma_start(bo_sb[:, :, 0:PACK], dealt(bo))
 
-        wg = sb("wg", [P, 2 * H], U8)
-        wg_planes = sb("wg_planes", [P, H], U8)
+        wg.append(placed("wg1", [P, 2 * GROUP], U8, 0))
+        wg_planes = placed("wg_planes", [P, H], U8, 2 * GROUP)
         wo = [sb("wo%d" % b, [P, 2, GROUP], U32) for b in range(2)]
         wo_planes = sb("wo_planes", [P, N], U8)
         wv_codes = [sb("wv_codes%d" % a, [P, GROUP], U32) for a in range(2)]
@@ -125,13 +138,6 @@ def tile_list_synaptic_channel_currents_kernel(
         y_woven = {}
         y_codes = [sb("y_codes%d" % c, [P, 2, CHUNKS[c][1]], U32) for c in range(len(CHUNKS))]
         wv_woven = [sb("wv_woven0", [P, PACK, P, PACK], BF16)]
-
-        def deal_wg(a):
-            cols = slice(2 * GROUP * a, 2 * GROUP * (a + 1))
-            nc.vector.tensor_copy(
-                wg[:, cols].rearrange("p (t k i e) -> p k t i e", t=PACK, i=8, e=2),
-                wg_raw[:, cols].rearrange("p (k i t e) -> p k t i e", t=PACK, i=8, e=2),
-            )
 
         def deal_planes(dst, src):
             nc.vector.tensor_copy(
@@ -202,7 +208,7 @@ def tile_list_synaptic_channel_currents_kernel(
                     col = GROUP * a + P * t
                     nc.tensor.matmul_mx(
                         out=part(acc, w, ts, t),
-                        lhsT=wg[:, 2 * col : 2 * (col + P)].bitcast(FP4X4),
+                        lhsT=wg[a][:, 2 * P * t : 2 * P * (t + 1)].bitcast(FP4X4),
                         lhsT_scale=wg_planes[:, col : col + P],
                         rhs=codes,
                         rhs_scale=planes,
@@ -310,9 +316,8 @@ def tile_list_synaptic_channel_currents_kernel(
             for r in range(4):
                 queues[r % len(queues)].dma_start(rows[r].bitcast(I32), y_planes[r:P:32, :, first:last].bitcast(I32))
 
-        for a in range(2):
-            deal_wg(a)
         deal_planes(wg_planes, wg_planes_raw)
+        deal_wg(1)
         look_up_words(0)
         weave_wv(0)
         quantize_wv(0, 2)

@@ -58,18 +58,12 @@ def tile_list_synaptic_channel_currents_kernel(
         offsets = keep.tile([P, S // 16], U16, name="offsets")
         table = sb("table", [P, T], U32)
         table_planes = placed("table_planes", [P, T], U8, 0)
-        wg_raw = sb("wg_raw", [P, 2 * H], U8)
+        wg_raw = placed("wg_raw", [P, 2 * H], U8, 20480)
         wg_planes_raw = sb("wg_planes_raw", [P, H], U8)
-        wo_planes_raw = sb("wo_planes_raw", [P, N], U8)
-        wv_raw = [sb("wv_raw%d" % a, [P, PACK, GROUP], F32) for a in range(2)]
-        wo_raw = sb("wo_raw", [P, 2, N], U32)
-        bg_sb = sb("bg_sb", [P, 2, 8], F32)
-        erev_sb = sb("erev_sb", [P, 2, 8], F32)
-        bo_sb = sb("bo_sb", [P, 2, 8], F32)
+        wv_raw = [sb("wv_raw0", [P, PACK, GROUP], F32)]
 
         nc.vector.memset(wg_planes_raw[:].bitcast(I32), 0)
         nc.vector.memset(table_planes[:].bitcast(I32), 0)
-        nc.vector.memset(wo_planes_raw[:].bitcast(I32), 0)
 
         v_rows = sb("v_rows", [P, S], U8)
         v_plane = sb("v_plane", [P, S], U8)
@@ -110,13 +104,11 @@ def tile_list_synaptic_channel_currents_kernel(
         deal_wg(0)
         nc.vector.tensor_copy(v_rows[:], table_planes[:].indirect(offsets[:]))
         for q in range(QUADRANTS):
-            nc.sync.dma_start(v_plane[32 * q : 32 * q + 4, :].bitcast(I32), v_rows[32 * q : 32 * (q + 1) : 8, :].bitcast(I32))
+            nc.scalar.dma_start(v_plane[32 * q : 32 * q + 4, :].bitcast(I32), v_rows[32 * q : 32 * (q + 1) : 8, :].bitcast(I32))
+        bg_sb = placed("bg_sb", [P, 2, 8], F32, 2048)
+        erev_sb = placed("erev_sb", [P, 2, 8], F32, 2048 + 64)
         nc.sync.dma_start(bg_sb[:, :, 0:PACK], dealt(bg))
         nc.sync.dma_start(erev_sb[:, :, 0:PACK], dealt(erev))
-        load_wv(1)
-        nc.sync.dma_start(wo_raw[:].bitcast(I32), wo8_words.rearrange("a p c i -> p a (c i)").bitcast(I32))
-        load_packed_planes(wo_planes_raw, wo8_scales)
-        nc.sync.dma_start(bo_sb[:, :, 0:PACK], dealt(bo))
 
         wg.append(placed("wg1", [P, 2 * GROUP], U8, 0))
         wg_planes = placed("wg_planes", [P, H], U8, 2 * GROUP)
@@ -318,6 +310,15 @@ def tile_list_synaptic_channel_currents_kernel(
 
         deal_planes(wg_planes, wg_planes_raw)
         deal_wg(1)
+        wo_raw = placed("wo_raw", [P, 2, N], U32, 20480 - 8192 + 64)
+        bo_sb = placed("bo_sb", [P, 2, 8], F32, 20480 + 64)
+        wo_planes_raw = placed("wo_planes_raw", [P, N], U8, 20480 + 128)
+        wv_raw.append(placed("wv_raw1", [P, PACK, GROUP], F32, 20480 + 2048 - 64))
+        load_wv(1)
+        nc.vector.memset(wo_planes_raw[:].bitcast(I32), 0)
+        nc.sync.dma_start(wo_raw[:].bitcast(I32), wo8_words.rearrange("a p c i -> p a (c i)").bitcast(I32))
+        load_packed_planes(wo_planes_raw, wo8_scales)
+        nc.sync.dma_start(bo_sb[:, :, 0:PACK], dealt(bo))
         look_up_words(0)
         weave_wv(0)
         quantize_wv(0, 2)

@@ -25,12 +25,15 @@ QUADRANTS = 4
 
 CHUNKS = ((0,256),(256,256),(512,256),(768,256))
 G_CHUNKS = ((0,256),(256,256),(512,512))
-WV_VECTOR_SHARE = (80, 64)
+WV_VECTOR_SHARE = (128, 48)
+PLAIN = False
+MIX0 = 1
+G21LATE = 2
 G_BANKS = (0, 1, 2,)
 D_BANKS = (3, 4, 5,)
 Y_BANKS = (6, 7,)
-H_VECTOR_SHARE = (192, 192, 192, 192,)
-Y_VECTOR_SHARE = (160, 160, 160, 160,)
+H_VECTOR_SHARE = (160, 160, 160, 192)
+Y_VECTOR_SHARE = (160, 160, 160, 160)
 
 
 def tile_list_synaptic_channel_currents_kernel(
@@ -48,12 +51,11 @@ def tile_list_synaptic_channel_currents_kernel(
         def placed(name, shape, dtype, offset):
             return head.tile(shape, dtype, name=name, align_bytes=64, offset=offset)
 
-        taken = {"g": 0, "d": 0, "y": 0}
+        taken = []
 
-        def bank(role, banks):
-            index = banks[taken[role] % len(banks)]
-            taken[role] = taken[role] + 1
-            return psum.tile([P, BANK], F32, name=role + "_acc", tag="bank%d" % index)
+        def bank(role, banks=None):
+            taken.append(role)
+            return psum.tile([P, BANK], F32, name=role + "_acc", tag="bank%d" % (len(taken) % 8))
 
         offsets = keep.tile([P, S // 16], U16, name="offsets")
         table = sb("table", [P, T], U32)
@@ -107,12 +109,14 @@ def tile_list_synaptic_channel_currents_kernel(
             nc.scalar.dma_start(v_plane[32 * q : 32 * q + 4, :].bitcast(I32), v_rows[32 * q : 32 * (q + 1) : 8, :].bitcast(I32))
         bg_sb = placed("bg_sb", [P, 2, 8], F32, 2048)
         erev_sb = placed("erev_sb", [P, 2, 8], F32, 2048 + 64)
-        nc.sync.dma_start(bg_sb[:, :, 0:PACK], dealt(bg))
+        bg_raw = placed("bg_raw", [P, 2, 8], F32, 2048 + 128)
+        nc.scalar.dma_start(bg_raw[:, :, 0:PACK], dealt(bg))
+        nc.scalar.activation(bg_sb[:, :, 0:PACK], bg_raw[:, :, 0:PACK], ACT.Copy)
         nc.sync.dma_start(erev_sb[:, :, 0:PACK], dealt(erev))
 
         wg.append(placed("wg1", [P, 2 * GROUP], U8, 0))
         wg_planes = placed("wg_planes", [P, H], U8, 2 * GROUP)
-        wo = [sb("wo%d" % b, [P, 2, GROUP], U32) for b in range(2)]
+        wo = {}
         wo_planes = sb("wo_planes", [P, N], U8)
         wv_codes = [sb("wv_codes%d" % a, [P, GROUP], U32) for a in range(2)]
         wv_planes = [sb("wv_planes%d" % a, [P, GROUP], U8) for a in range(2)]
@@ -129,7 +133,7 @@ def tile_list_synaptic_channel_currents_kernel(
         y = {u: sb("y%d%d" % u, [P, PACK, width[u]], F32) for u in units}
         y_woven = {}
         y_codes = [sb("y_codes%d" % c, [P, 2, CHUNKS[c][1]], U32) for c in range(len(CHUNKS))]
-        wv_woven = [sb("wv_woven0", [P, PACK, P, PACK], BF16)]
+        wv_woven = {}
 
         def deal_planes(dst, src):
             nc.vector.tensor_copy(
@@ -137,7 +141,8 @@ def tile_list_synaptic_channel_currents_kernel(
                 src[:].rearrange("p (a k i t) -> p a k t i", a=2, t=PACK, i=16),
             )
 
-        def deal_wo(b):
+        def deal_wo(b, slot=None):
+            wo[b] = sb("wo%d" % b, [P, 2, GROUP], U32, tag=slot)
             nc.vector.tensor_copy(
                 wo[b][:].bitcast(I32).rearrange("p a (t k i) -> p a k t i", t=PACK, i=4),
                 wo_raw[:, :, GROUP * b : GROUP * (b + 1)].bitcast(I32).rearrange("p a (k i t) -> p a k t i", t=PACK, i=4),
@@ -146,22 +151,22 @@ def tile_list_synaptic_channel_currents_kernel(
         def list_of(c):
             return offsets[:, c * LOOKUP // 16 : (c + 1) * LOOKUP // 16]
 
-        def weave_wv(a):
-            split = WV_VECTOR_SHARE[a]
-            dst = wv_woven[a][:].rearrange("p t m j -> p m t j")
-            src = wv_raw[a][:].rearrange("p j (m t) -> p m t j", t=PACK)
-            nc.vector.tensor_scalar(dst[:, :split], src[:, :split], -1.0, None, ALU.mult)
-            nc.scalar.activation(dst[:, split:], src[:, split:], ACT.Copy, scale=-1.0)
+        def weave_wv(a, half, on_vector, slot=None):
+            wv_woven[a, half] = sb("wv_woven%d%d" % (a, half), [P, 2, P, PACK], BF16, tag=slot)
+            dst = wv_woven[a, half][:].rearrange("p t m j -> p m j t")
+            src = wv_raw[a][:].rearrange("p j (m t) -> p m j t", t=PACK)[:, :, :, 2 * half : 2 * half + 2]
+            if on_vector:
+                nc.vector.tensor_scalar(dst, src, -1.0, None, ALU.mult)
+            else:
+                nc.scalar.activation(dst, src, ACT.Copy, scale=-1.0)
 
-        def quantize_wv(a, calls=1):
-            slices = PACK // calls
-            for first in range(0, PACK, slices):
-                cols = slice(P * first, P * (first + slices))
-                nc.vector.quantize_mx(
-                    out=wv_codes[a][:, cols].bitcast(FP8X4),
-                    scales=wv_planes[a][:, cols],
-                    in_=wv_woven[a][:, first : first + slices].rearrange("p t m j -> p (t m j)"),
-                )
+        def quantize_wv(a, half):
+            cols = slice(2 * P * half, 2 * P * (half + 1))
+            nc.vector.quantize_mx(
+                out=wv_codes[a][:, cols].bitcast(FP8X4),
+                scales=wv_planes[a][:, cols],
+                in_=wv_woven[a, half][:].rearrange("p t m j -> p (t m j)"),
+            )
 
         def weave(woven, rows, share):
             for engine, first, last in (("vector", 0, share), ("scalar", share, woven.shape[1])):
@@ -279,7 +284,7 @@ def tile_list_synaptic_channel_currents_kernel(
 
         def mix_last(c, banks, on_vector, per_store=2):
             groups = [(b, ts) for b in range(2) for ts in bank_groups(CHUNKS[c][1])]
-            accs = [bank("y", banks) for group in groups]
+            accs = [bank("y") for group in groups]
             for acc, (b, ts) in zip(accs, groups):
                 for t in ts:
                     mix_pass(acc, c, b, ts, t, 0, t == ts[0], False)
@@ -320,26 +325,42 @@ def tile_list_synaptic_channel_currents_kernel(
         load_packed_planes(wo_planes_raw, wo8_scales)
         nc.sync.dma_start(bo_sb[:, :, 0:PACK], dealt(bo))
         look_up_words(0)
-        weave_wv(0)
-        quantize_wv(0, 2)
         look_up_words(1)
+        weave_wv(0, 0, True)
+        weave_wv(0, 1, True)
+        quantize_wv(0, 0)
+        quantize_wv(0, 1)
 
         conductances(0, 0)
-        conductances(0, 1)
         conductances(1, 0)
+        conductances(0, 1)
         currents(0, 0)
-        wv_woven.append(sb("wv_woven1", [P, PACK, P, PACK], BF16, tag="g00"))
-        weave_wv(1)
-        quantize_wv(1)
+        weave_wv(1, 1, False)
+        conductances(1, 1)
+        weave_wv(1, 0, True, "g00")
         weave_h(0, 0)
-        currents(1, 0)
-        currents(0, 1)
+        quantize_wv(1, 0)
+        quantize_wv(1, 1)
+        if not PLAIN:
+            currents(1, 0)
+        conductances(2, 0)
         quantize_h(0, 0)
-        weave_h(0, 1)
-        quantize_h(0, 1)
-        deal_wo(0)
+        deal_wo(0, "g00")
+        currents(0, 1)
         deal_planes(wo_planes, wo_planes_raw)
+        weave_h(0, 1)
+        if not G21LATE:
+            conductances(2, 1)
+        quantize_h(0, 1)
+        if MIX0:
+            mix(0, 0)
         deal_wo(1)
+        if G21LATE == 2:
+            conductances(2, 1)
+        if MIX0 > 1:
+            mix(0, 1)
+        if G21LATE == 3:
+            conductances(2, 1)
         last = len(CHUNKS) - 1
 
         def finish(c):
@@ -354,20 +375,18 @@ def tile_list_synaptic_channel_currents_kernel(
 
         for c in range(1, last + 1):
             banks = Y_BANKS if c == 1 else G_BANKS[:2] + Y_BANKS
-            if c > 1:
+            if c > 1 or PLAIN:
                 currents(c, 0)
             weave_h(c, 0)
-            if c == 1:
-                conductances(1, 1)
             currents(c, 1)
             quantize_h(c, 0)
             weave_h(c, 1)
             quantize_h(c, 1)
-            mix(c - 1, 0, 2, banks)
-            if c == 1:
-                conductances(2, 0)
-            mix(c - 1, 1, 2, banks)
-            if c == 1:
+            if c > 1 or not MIX0:
+                mix(c - 1, 0, 2, banks)
+            if c > 1 or MIX0 < 2:
+                mix(c - 1, 1, 2, banks)
+            if c == 1 and G21LATE == 1:
                 conductances(2, 1)
             if c == last:
                 mix_last(c, D_BANKS + G_BANKS[2:], (1,), 2)

@@ -324,6 +324,17 @@ def tile_list_synaptic_channel_currents_kernel(
         nc.sync.dma_start(wo_raw[:].bitcast(I32), wo8_words.rearrange("a p c i -> p a (c i)").bitcast(I32))
         load_packed_planes(wo_planes_raw, wo8_scales)
         nc.sync.dma_start(bo_sb[:, :, 0:PACK], dealt(bo))
+        warm = psum.tile([P, BANK], F32, name="warm", tag="bank7")
+        for repeat in range(4):
+            nc.tensor.matmul_mx(
+                out=warm[:],
+                lhsT=wg[0][:, : 2 * P].bitcast(FP4X4),
+                lhsT_scale=wg_planes[:, :P],
+                rhs=table[:, :BANK].bitcast(FP8X4),
+                rhs_scale=wg_planes[:, :BANK],
+                start=True,
+                stop=True,
+            )
         look_up_words(0)
         look_up_words(1)
         weave_wv(0, 0, True)

@@ -172,8 +172,8 @@ def tile_list_synaptic_channel_currents_kernel(
             for engine, first, last in (("vector", 0, share), ("scalar", share, woven.shape[1])):
                 if first == last:
                     continue
-                dst = woven[:, first:last, :].rearrange("p (c i) t -> p c t i", i=4)
-                src = rows[:, :, first:last].rearrange("p t (c i) -> p c t i", i=4)
+                dst = woven[:, first:last, :].rearrange("p (c i) t -> p c t i", i=8)
+                src = rows[:, :, first:last].rearrange("p t (c i) -> p c t i", i=8)
                 if engine == "vector":
                     nc.vector.tensor_copy(dst, src)
                 else:

@@ -26,6 +26,9 @@ QUADRANTS = 4
 CHUNKS = ((0,256),(256,256),(512,256),(768,256))
 G_CHUNKS = ((0,256),(256,256),(512,512))
 WV_VECTOR_SHARE = (128, 48)
+BLOCK = 32
+G_BLOCKS = 4
+G_UNITS = ((1, 0), (2, 0), (3, 0))
 PLAIN = False
 MIX0 = 1
 G21LATE = 2
@@ -126,8 +129,18 @@ def tile_list_synaptic_channel_currents_kernel(
         units = [(c, a) for c in range(len(CHUNKS)) for a in range(2)]
         width = {u: CHUNKS[u[0]][1] for u in units}
         g = {}
-        h_rows = {u: sb("h_rows%d%d" % u, [P, PACK, width[u]], BF16) for u in units}
-        h_woven = {u: sb("h_woven%d%d" % u, [P, width[u], PACK], BF16) for u in units}
+        blocks = 256 // BLOCK
+        ahead = (blocks - G_BLOCKS) * BLOCK * PACK
+        h_rows = {}
+        h_woven = {}
+        for u in units:
+            if u in G_UNITS:
+                both = sb("h_both%d%d" % u, [P, ahead + 256 * PACK], BF16)
+                h_woven[u] = both[:, : 256 * PACK].rearrange("p (j t) -> p j t", t=PACK)
+                h_rows[u] = both[:, ahead:].rearrange("p (k t i) -> p t k i", t=PACK, i=BLOCK)
+            else:
+                h_rows[u] = sb("h_rows%d%d" % u, [P, PACK, width[u]], BF16)[:]
+                h_woven[u] = sb("h_woven%d%d" % u, [P, width[u], PACK], BF16)[:]
         h_codes = {u: sb("h_codes%d%d" % u, [P, width[u]], U32) for u in units}
         h_planes = {u: sb("h_planes%d%d" % u, [P, width[u]], U8) for u in units}
         y = {u: sb("y%d%d" % u, [P, PACK, width[u]], F32) for u in units}
@@ -234,18 +247,34 @@ def tile_list_synaptic_channel_currents_kernel(
                         stop=True,
                     )
                 for t in ts:
-                    nc.vector.scalar_tensor_tensor(
-                        h_rows[c, a][:, t, :], part(acc, w, ts, t), erev_sb[:, a, t : t + 1], gates[:, t, :], ALU.add, ALU.mult
-                    )
+                    sums, gate = part(acc, w, ts, t), gates[:, t, :]
+                    if (c, a) in G_UNITS:
+                        sums, gate = [x.rearrange("p (k i) -> p k i", i=BLOCK) for x in (sums, gate)]
+                    nc.vector.scalar_tensor_tensor(h_rows[c, a][:, t], sums, erev_sb[:, a, t : t + 1], gate, ALU.add, ALU.mult)
 
         def weave_h(c, a):
-            weave(h_woven[c, a], h_rows[c, a], H_VECTOR_SHARE[c])
+            if (c, a) not in G_UNITS:
+                weave(h_woven[c, a], h_rows[c, a], H_VECTOR_SHARE[c])
+                return
+            mine = blocks - G_BLOCKS
+            nc.vector.tensor_copy(
+                h_woven[c, a][:, : mine * BLOCK, :].rearrange("p (k c i) t -> p c k t i", k=mine, i=8),
+                h_rows[c, a][:, :, :mine, :].rearrange("p t k (c i) -> p c k t i", i=8),
+            )
+            nc.gpsimd.tensor_scalar(
+                h_woven[c, a][:, mine * BLOCK :, :].rearrange("p (k i) t -> p k i t", i=BLOCK),
+                h_rows[c, a][:, :, mine:, :].rearrange("p t k i -> p k i t"),
+                1.0,
+                0.0,
+                ALU.mult,
+                ALU.add,
+            )
 
         def quantize_h(c, a):
             nc.vector.quantize_mx(
                 out=h_codes[c, a][:].bitcast(FP8X4),
                 scales=h_planes[c, a][:],
-                in_=h_woven[c, a][:].rearrange("p j t -> p (j t)"),
+                in_=h_woven[c, a].rearrange("p j t -> p (j t)"),
             )
 
         def columns(c):

@@ -212,6 +212,7 @@ def tile_list_synaptic_channel_currents_kernel(
             w = G_CHUNKS[c][1]
             g[c, a] = sb("g%d%d" % (c, a), [P, PACK, w], F32)
             codes, planes = looked_up(G_CHUNKS[c])
+            filled = []
             for ts in bank_groups(w):
                 acc = bank("g", G_BANKS)
                 for t in ts:
@@ -225,8 +226,12 @@ def tile_list_synaptic_channel_currents_kernel(
                         start=True,
                         stop=True,
                     )
-                for t in ts:
-                    nc.scalar.activation(g[c, a][:, t, :], part(acc, w, ts, t), ACT.Relu, bias=bg_sb[:, a, t : t + 1])
+                filled.append((acc, ts))
+                if len(filled) == 2:
+                    for acc, ts in filled if c + a == 0 else reversed(filled):
+                        for t in ts:
+                            nc.scalar.activation(g[c, a][:, t, :], part(acc, w, ts, t), ACT.Relu, bias=bg_sb[:, a, t : t + 1])
+                    filled = []
 
         def currents(c, a):
             w = CHUNKS[c][1]
@@ -234,6 +239,7 @@ def tile_list_synaptic_channel_currents_kernel(
             offset = CHUNKS[c][0] - G_CHUNKS[held][0]
             gates = g[held, a][:, :, offset : offset + w]
             codes, planes = looked_up(CHUNKS[c])
+            filled = []
             for ts in bank_groups(w):
                 acc = bank("d", D_BANKS)
                 for t in ts:
@@ -246,6 +252,8 @@ def tile_list_synaptic_channel_currents_kernel(
                         start=True,
                         stop=True,
                     )
+                filled.append((acc, ts))
+            for acc, ts in filled if c == 0 else reversed(filled):
                 for t in ts:
                     sums, gate = part(acc, w, ts, t), gates[:, t, :]
                     if (c, a) in G_UNITS:

@@ -58,7 +58,10 @@ def tile_list_synaptic_channel_currents_kernel(
 
         def bank(role, banks=None):
             taken.append(role)
-            return psum.tile([P, BANK], F32, name=role + "_acc", tag="bank%d" % (len(taken) % 8))
+            turn = len(taken)
+            if 7 <= turn <= 10:
+                turn = turn + 2 if turn <= 8 else turn - 2
+            return psum.tile([P, BANK], F32, name=role + "_acc", tag="bank%d" % (turn % 8))
 
         offsets = keep.tile([P, S // 16], U16, name="offsets")
         table = sb("table", [P, T], U32)
@@ -208,7 +211,7 @@ def tile_list_synaptic_channel_currents_kernel(
         def part(acc, w, ts, t):
             return acc[:, w * (t - ts[0]) : w * (t - ts[0] + 1)]
 
-        def conductances(c, a):
+        def conductances(c, a, between=None):
             w = G_CHUNKS[c][1]
             g[c, a] = sb("g%d%d" % (c, a), [P, PACK, w], F32)
             codes, planes = looked_up(G_CHUNKS[c])
@@ -228,6 +231,8 @@ def tile_list_synaptic_channel_currents_kernel(
                     )
                 filled.append((acc, ts))
                 if len(filled) == 2:
+                    if between is not None:
+                        between()
                     for acc, ts in filled if c + a == 0 else reversed(filled):
                         for t in ts:
                             nc.scalar.activation(g[c, a][:, t, :], part(acc, w, ts, t), ACT.Relu, bias=bg_sb[:, a, t : t + 1])
@@ -382,9 +387,12 @@ def tile_list_synaptic_channel_currents_kernel(
         conductances(0, 0)
         conductances(1, 0)
         conductances(0, 1)
-        currents(0, 0)
-        weave_wv(1, 1, False)
-        conductances(1, 1)
+
+        def first_currents():
+            currents(0, 0)
+            weave_wv(1, 1, False)
+
+        conductances(1, 1, first_currents)
         weave_wv(1, 0, True, "g00")
         weave_h(0, 0)
         quantize_wv(1, 0)

@@ -77,6 +77,12 @@ def tile_list_synaptic_channel_currents_kernel(
         v_plane = sb("v_plane", [P, S], U8)
         nc.vector.memset(v_plane[:].bitcast(I32), 0)
 
+        ones = sb("ones", [P, BANK * PACK], BF16)
+        warm_codes = sb("warm_codes", [P, BANK], U32)
+        warm_plane = sb("warm_plane", [P, BANK], U8)
+        nc.vector.memset(ones[:].bitcast(I32), 0x3F803F80)
+        nc.vector.quantize_mx(out=warm_codes[:].bitcast(FP8X4), scales=warm_plane[:], in_=ones[:])
+
         def dealt(vec):
             return vec.rearrange("(a p t) -> p a t", p=P, t=PACK)
 
@@ -370,10 +376,10 @@ def tile_list_synaptic_channel_currents_kernel(
         for repeat in range(4):
             nc.tensor.matmul_mx(
                 out=warm[:],
-                lhsT=wg[0][:, : 2 * P].bitcast(FP4X4),
-                lhsT_scale=wg_planes[:, :P],
-                rhs=table[:, :BANK].bitcast(FP8X4),
-                rhs_scale=wg_planes[:, :BANK],
+                lhsT=wg[1][:, : 2 * P].bitcast(FP4X4),
+                lhsT_scale=wg_planes[:, GROUP : GROUP + P],
+                rhs=warm_codes[:].bitcast(FP8X4),
+                rhs_scale=warm_plane[:],
                 start=True,
                 stop=True,
             )

@@ -22,21 +22,10 @@ GROUP = P * PACK
 BANK = 512
 LOOKUP = 512
 QUADRANTS = 4
-
-CHUNKS = ((0,256),(256,256),(512,256),(768,256))
-G_CHUNKS = ((0,256),(256,256),(512,512))
-WV_VECTOR_SHARE = (128, 48)
-BLOCK = 32
-G_BLOCKS = 4
-G_UNITS = ((1, 0), (2, 0), (3, 0))
-PLAIN = False
-MIX0 = 1
-G21LATE = 2
-G_BANKS = (0, 1, 2,)
-D_BANKS = (3, 4, 5,)
-Y_BANKS = (6, 7,)
-H_VECTOR_SHARE = (160, 160, 160, 192)
-Y_VECTOR_SHARE = (160, 160, 160, 160)
+CHUNK = 256
+CHUNKS = S // CHUNK
+LINE = 64
+YENG = (("scalar", "scalar", "scalar", "scalar"), ("vector", "vector", "vector", "vector"), ("vector", "vector", "vector", "vector"), ("vector", "scalar", "vector", "scalar"))
 
 
 def tile_list_synaptic_channel_currents_kernel(
@@ -54,48 +43,58 @@ def tile_list_synaptic_channel_currents_kernel(
         def placed(name, shape, dtype, offset):
             return head.tile(shape, dtype, name=name, align_bytes=64, offset=offset)
 
-        taken = []
-
-        def bank(role, banks=None):
-            taken.append(role)
-            turn = len(taken)
-            if 7 <= turn <= 10:
-                turn = turn + 2 if turn <= 8 else turn - 2
-            return psum.tile([P, BANK], F32, name=role + "_acc", tag="bank%d" % (turn % 8))
-
-        offsets = keep.tile([P, S // 16], U16, name="offsets")
-        table = sb("table", [P, T], U32)
-        table_planes = placed("table_planes", [P, T], U8, 0)
-        wg_raw = placed("wg_raw", [P, 2 * H], U8, 20480)
-        wg_planes_raw = sb("wg_planes_raw", [P, H], U8)
-        wv_raw = [sb("wv_raw0", [P, PACK, GROUP], F32)]
-
-        nc.vector.memset(wg_planes_raw[:].bitcast(I32), 0)
-        nc.vector.memset(table_planes[:].bitcast(I32), 0)
-
-        v_rows = sb("v_rows", [P, S], U8)
-        v_plane = sb("v_plane", [P, S], U8)
-        nc.vector.memset(v_plane[:].bitcast(I32), 0)
-
-        ones = sb("ones", [P, BANK * PACK], BF16)
-        warm_codes = sb("warm_codes", [P, BANK], U32)
-        warm_plane = sb("warm_plane", [P, BANK], U8)
-        nc.vector.memset(ones[:].bitcast(I32), 0x3F803F80)
-        nc.vector.quantize_mx(out=warm_codes[:].bitcast(FP8X4), scales=warm_plane[:], in_=ones[:])
+        def bank(pairs, index):
+            return psum.tile([P, BANK], F32, name="acc", tag="%s%d" % (pairs[index // 2], index % 2))
 
         def dealt(vec):
             return vec.rearrange("(a p t) -> p a t", p=P, t=PACK)
 
-        def load_plane(planes, scales):
-            rows = scales[0].rearrange("(q r) c -> r q c", r=4)
-            for r in range(4):
-                nc.sync.dma_start(planes[r:P:32, :].bitcast(I32), rows[r].bitcast(I32))
+        offsets = keep.tile([P, S // 16], U16, name="offsets")
+        table = sb("table", [P, T], U32)
+        rows_at = 8192
+        table_rows = placed("table_rows", [P, T], U8, rows_at)
+        wg_at = 32768
+        wg_raw = placed("wg_raw", [P, 2 * H], U8, wg_at)
+        wg_plane_raw = sb("wg_plane_raw", [P, H], U8)
+        v_rows = sb("v_rows", [P, S], U8)
+        v_plane = sb("v_plane", [P, S], U8)
 
-        def load_packed_planes(planes, scales):
-            for q in range(QUADRANTS):
-                nc.sync.dma_start(
-                    planes[32 * q : 32 * q + 8, :].bitcast(I32), scales[:, 4 * q : 4 * q + 4, :].bitcast(I32)
-                )
+        nc.vector.memset(wg_plane_raw[:].bitcast(I32), 0)
+        nc.vector.memset(table_rows[:].bitcast(I32), 0)
+        nc.vector.memset(v_plane[:].bitcast(I32), 0)
+
+        nc.sync.dma_start(wg_raw[:].bitcast(I32), wg4_words[0].bitcast(I32))
+        nc.sync.dma_start(offsets[:], offs)
+        wg_rows = wg4_scales[0].rearrange("(q r) c -> r q c", r=4)
+        for r in range(4):
+            nc.sync.dma_start(wg_plane_raw[r:P:32, :].bitcast(I32), wg_rows[r].bitcast(I32))
+        nc.sync.dma_start(table_rows[0:P:8, :].bitcast(I32), tab_scales[0].bitcast(I32))
+        nc.sync.dma_start(table[:].bitcast(I32), tab_words[0].rearrange("p t i -> p (t i)").bitcast(I32))
+
+        wv_first = [sb("wv_first0", [P, PACK, GROUP // 2], F32)]
+
+        def load_wv(tile, first):
+            rows = wv[:, first : first + tile.shape[2]].rearrange("(p j) c -> p j c", j=PACK)
+            nc.sync.dma_start(tile[:], rows)
+
+        load_wv(wv_first[0], 0)
+        nc.vector.tensor_copy(v_rows[:], table_rows[:].indirect(offsets[:]))
+        for q in range(QUADRANTS):
+            nc.sync.dma_start(v_plane[32 * q : 32 * q + 4, :].bitcast(I32), v_rows[32 * q : 32 * (q + 1) : 8, :].bitcast(I32))
+
+        wv_first.append(placed("wv_first1", [P, PACK, GROUP // 2], F32, rows_at + LINE - 4096))
+        wv_second = placed("wv_second", [P, PACK, GROUP], F32, rows_at + T - LINE)
+        wg = [placed("wg%d" % a, [P, 2 * GROUP], U8, rows_at + LINE + 2 * GROUP * a) for a in range(2)]
+        wg_plane = placed("wg_plane", [P, H], U8, rows_at + LINE + 4 * GROUP)
+        bg_raw = placed("bg_raw", [P, 2, 8], F32, rows_at + LINE + 6 * GROUP)
+        bg_sb = sb("bg_sb", [P, 2, 8], F32)
+        erev_sb = placed("erev_sb", [P, 2, 8], F32, rows_at + 3 * LINE + 6 * GROUP)
+
+        nc.sync.dma_start(bg_raw[:, :, 0:PACK], dealt(bg))
+        load_wv(wv_first[1], GROUP // 2)
+        nc.sync.dma_start(erev_sb[:, :, 0:PACK], dealt(erev))
+        load_wv(wv_second, GROUP)
+        nc.scalar.activation(bg_sb[:, :, 0:PACK], bg_raw[:, :, 0:PACK], ACT.Copy)
 
         def deal_wg(a):
             cols = slice(2 * GROUP * a, 2 * GROUP * (a + 1))
@@ -104,80 +103,69 @@ def tile_list_synaptic_channel_currents_kernel(
                 wg_raw[:, cols].bitcast(U16).rearrange("p (k i t) -> p k t i", t=PACK, i=8),
             )
 
-        def load_wv(a):
-            rows = wv[:, GROUP * a : GROUP * (a + 1)].rearrange("(p j) c -> p j c", j=PACK)
-            nc.sync.dma_start(wv_raw[a][:], rows)
-
-        nc.sync.dma_start(wg_raw[:].bitcast(I32), wg4_words[0].bitcast(I32))
-        nc.sync.dma_start(offsets[:], offs)
-        load_plane(wg_planes_raw, wg4_scales)
-        nc.sync.dma_start(table_planes[0:P:8, :].bitcast(I32), tab_scales[0].bitcast(I32))
-        nc.sync.dma_start(table[:].bitcast(I32), tab_words[0].rearrange("p t i -> p (t i)").bitcast(I32))
-        load_wv(0)
-        wg = [sb("wg0", [P, 2 * GROUP], U8)]
-        deal_wg(0)
-        nc.vector.tensor_copy(v_rows[:], table_planes[:].indirect(offsets[:]))
-        for q in range(QUADRANTS):
-            nc.scalar.dma_start(v_plane[32 * q : 32 * q + 4, :].bitcast(I32), v_rows[32 * q : 32 * (q + 1) : 8, :].bitcast(I32))
-        bg_sb = placed("bg_sb", [P, 2, 8], F32, 2048)
-        erev_sb = placed("erev_sb", [P, 2, 8], F32, 2048 + 64)
-        bg_raw = placed("bg_raw", [P, 2, 8], F32, 2048 + 128)
-        nc.scalar.dma_start(bg_raw[:, :, 0:PACK], dealt(bg))
-        nc.scalar.activation(bg_sb[:, :, 0:PACK], bg_raw[:, :, 0:PACK], ACT.Copy)
-        nc.sync.dma_start(erev_sb[:, :, 0:PACK], dealt(erev))
-
-        wg.append(placed("wg1", [P, 2 * GROUP], U8, 0))
-        wg_planes = placed("wg_planes", [P, H], U8, 2 * GROUP)
-        wo = {}
-        wo_planes = sb("wo_planes", [P, N], U8)
-        wv_codes = [sb("wv_codes%d" % a, [P, GROUP], U32) for a in range(2)]
-        wv_planes = [sb("wv_planes%d" % a, [P, GROUP], U8) for a in range(2)]
-        v_codes = []
-        v_planes = [v_plane[:, LOOKUP * half : LOOKUP * (half + 1)] for half in range(2)]
-        y_planes = sb("y_planes", [P, 2, S], U8)
-        units = [(c, a) for c in range(len(CHUNKS)) for a in range(2)]
-        width = {u: CHUNKS[u[0]][1] for u in units}
-        g = {}
-        blocks = 256 // BLOCK
-        ahead = (blocks - G_BLOCKS) * BLOCK * PACK
-        h_rows = {}
-        h_woven = {}
-        for u in units:
-            if u in G_UNITS:
-                both = sb("h_both%d%d" % u, [P, ahead + 256 * PACK], BF16)
-                h_woven[u] = both[:, : 256 * PACK].rearrange("p (j t) -> p j t", t=PACK)
-                h_rows[u] = both[:, ahead:].rearrange("p (k t i) -> p t k i", t=PACK, i=BLOCK)
-            else:
-                h_rows[u] = sb("h_rows%d%d" % u, [P, PACK, width[u]], BF16)[:]
-                h_woven[u] = sb("h_woven%d%d" % u, [P, width[u], PACK], BF16)[:]
-        h_codes = {u: sb("h_codes%d%d" % u, [P, width[u]], U32) for u in units}
-        h_planes = {u: sb("h_planes%d%d" % u, [P, width[u]], U8) for u in units}
-        y = {u: sb("y%d%d" % u, [P, PACK, width[u]], F32) for u in units}
-        y_woven = {}
-        y_codes = [sb("y_codes%d" % c, [P, 2, CHUNKS[c][1]], U32) for c in range(len(CHUNKS))]
-        wv_woven = {}
-
-        def deal_planes(dst, src):
+        def deal_plane(dst, src):
             nc.vector.tensor_copy(
                 dst[:].rearrange("p (a t k i) -> p a k t i", a=2, t=PACK, i=16),
                 src[:].rearrange("p (a k i t) -> p a k t i", a=2, t=PACK, i=16),
             )
 
-        def deal_wo(b, slot=None):
-            wo[b] = sb("wo%d" % b, [P, 2, GROUP], U32, tag=slot)
-            nc.vector.tensor_copy(
-                wo[b][:].bitcast(I32).rearrange("p a (t k i) -> p a k t i", t=PACK, i=4),
-                wo_raw[:, :, GROUP * b : GROUP * (b + 1)].bitcast(I32).rearrange("p a (k i t) -> p a k t i", t=PACK, i=4),
+        deal_wg(0)
+        deal_plane(wg_plane, wg_plane_raw)
+        deal_wg(1)
+
+        wo_raw = placed("wo_raw", [P, 2, N], U32, wg_at + LINE - 8192)
+        bo_sb = placed("bo_sb", [P, 2, 8], F32, wg_at + LINE)
+        wo_plane_raw = placed("wo_plane_raw", [P, N], U8, wg_at + 2 * LINE)
+        nc.vector.memset(wo_plane_raw[:].bitcast(I32), 0)
+        nc.sync.dma_start(wo_raw[:].bitcast(I32), wo8_words.rearrange("a p c i -> p a (c i)").bitcast(I32))
+        for q in range(QUADRANTS):
+            nc.sync.dma_start(
+                wo_plane_raw[32 * q : 32 * q + 8, :].bitcast(I32), wo8_scales[:, 4 * q : 4 * q + 4, :].bitcast(I32)
+            )
+        nc.sync.dma_start(bo_sb[:, :, 0:PACK], dealt(bo))
+
+        units = [(c, a) for c in range(CHUNKS) for a in range(2)]
+        wo = [sb("wo%d" % b, [P, 2, GROUP], U32) for b in range(2)]
+        wo_plane = sb("wo_plane", [P, N], U8)
+        wv_woven = [sb("wv_woven%d" % a, [P, PACK, P, PACK], BF16) for a in range(2)]
+        wv_codes = [sb("wv_codes%d" % a, [P, GROUP], U32) for a in range(2)]
+        wv_planes = [sb("wv_planes%d" % a, [P, GROUP], U8) for a in range(2)]
+        v_codes = [sb("v_codes%d" % half, [P, LOOKUP], U32) for half in range(2)]
+        g = {}
+        h_rows = {u: sb("h_rows%d%d" % u, [P, PACK, CHUNK], BF16) for u in units}
+        h_woven = {u: sb("h_woven%d%d" % u, [P, CHUNK, PACK], BF16) for u in units}
+        h_codes = {u: sb("h_codes%d%d" % u, [P, CHUNK], U32) for u in units}
+        h_planes = {u: sb("h_planes%d%d" % u, [P, CHUNK], U8) for u in units}
+        y = {u: sb("y%d%d" % u, [P, PACK, CHUNK], F32) for u in units}
+        y_woven = {u: sb("y_woven%d%d" % u, [P, CHUNK, PACK], BF16) for u in units}
+        y_codes = [sb("y_codes%d" % c, [P, 2, CHUNK], U32) for c in range(CHUNKS)]
+        y_planes = sb("y_planes", [P, 2, S], U8)
+
+        def move(engine, dst, src):
+            if engine == "vector":
+                nc.vector.tensor_copy(dst, src)
+            else:
+                nc.scalar.copy(dst, src)
+
+        def look_up_words(half):
+            entries = offsets[:, half * LOOKUP // 16 : (half + 1) * LOOKUP // 16]
+            nc.vector.tensor_copy(v_codes[half][:], table[:].indirect(entries))
+
+        def deal_wo(b, engine):
+            move(
+                engine,
+                wo[b][:].rearrange("p a (t k i) -> p a k t i", t=PACK, i=4),
+                wo_raw[:, :, GROUP * b : GROUP * (b + 1)].rearrange("p a (k i t) -> p a k t i", t=PACK, i=4),
             )
 
-        def list_of(c):
-            return offsets[:, c * LOOKUP // 16 : (c + 1) * LOOKUP // 16]
-
-        def weave_wv(a, half, on_vector, slot=None):
-            wv_woven[a, half] = sb("wv_woven%d%d" % (a, half), [P, 2, P, PACK], BF16, tag=slot)
-            dst = wv_woven[a, half][:].rearrange("p t m j -> p m j t")
-            src = wv_raw[a][:].rearrange("p j (m t) -> p m j t", t=PACK)[:, :, :, 2 * half : 2 * half + 2]
-            if on_vector:
+        def weave_wv(a, half, engine):
+            if a == 0:
+                dst = wv_woven[0][:, :, P // 2 * half : P // 2 * (half + 1), :].rearrange("p t m j -> p m j t")
+                src = wv_first[half][:].rearrange("p j (m t) -> p m j t", t=PACK)
+            else:
+                dst = wv_woven[1][:, 2 * half : 2 * half + 2].rearrange("p t m j -> p m j t")
+                src = wv_second[:].rearrange("p j (m t) -> p m j t", t=PACK)[:, :, :, 2 * half : 2 * half + 2]
+            if engine == "vector":
                 nc.vector.tensor_scalar(dst, src, -1.0, None, ALU.mult)
             else:
                 nc.scalar.activation(dst, src, ACT.Copy, scale=-1.0)
@@ -187,163 +175,119 @@ def tile_list_synaptic_channel_currents_kernel(
             nc.vector.quantize_mx(
                 out=wv_codes[a][:, cols].bitcast(FP8X4),
                 scales=wv_planes[a][:, cols],
-                in_=wv_woven[a, half][:].rearrange("p t m j -> p (t m j)"),
+                in_=wv_woven[a][:, 2 * half : 2 * half + 2].rearrange("p t m j -> p (t m j)"),
             )
 
-        def weave(woven, rows, share):
-            for engine, first, last in (("vector", 0, share), ("scalar", share, woven.shape[1])):
-                if first == last:
-                    continue
-                dst = woven[:, first:last, :].rearrange("p (c i) t -> p c t i", i=8)
-                src = rows[:, :, first:last].rearrange("p t (c i) -> p c t i", i=8)
-                if engine == "vector":
-                    nc.vector.tensor_copy(dst, src)
-                else:
-                    nc.scalar.copy(dst, src)
+        def weave(woven, rows, engine, first=0, last=CHUNK):
+            dst = woven[:, first:last, :].rearrange("p (c i) t -> p c t i", i=8)
+            src = rows[:, :, first:last].rearrange("p t (c i) -> p c t i", i=8)
+            move(engine, dst, src)
 
-        def looked_up(chunk):
-            half, first = divmod(chunk[0], LOOKUP)
-            cols = slice(first, first + chunk[1])
-            return v_codes[half][:, cols].bitcast(FP8X4), v_planes[half][:, cols]
+        def looked_up(first, width):
+            half, start = divmod(first, LOOKUP)
+            return v_codes[half][:, start : start + width].bitcast(FP8X4), v_plane[:, first : first + width]
 
-        def look_up_words(half, slot=None):
-            v_codes.append(sb("v_codes%d" % half, [P, LOOKUP], U32, tag=slot))
-            nc.vector.tensor_copy(v_codes[half][:], table[:].indirect(list_of(half)))
-
-        def bank_groups(w):
-            side = min(BANK // w, PACK)
-            return [range(t, t + side) for t in range(0, PACK, side)]
-
-        def part(acc, w, ts, t):
-            return acc[:, w * (t - ts[0]) : w * (t - ts[0] + 1)]
-
-        def conductances(c, a, between=None):
-            w = G_CHUNKS[c][1]
-            g[c, a] = sb("g%d%d" % (c, a), [P, PACK, w], F32)
-            codes, planes = looked_up(G_CHUNKS[c])
-            filled = []
-            for ts in bank_groups(w):
-                acc = bank("g", G_BANKS)
-                for t in ts:
+        def conductances(c, a, pairs):
+            chunks = len(pairs)
+            width = chunks * CHUNK
+            tile = sb("g%d%d" % (c, a), [P, PACK, width], F32)
+            for i in range(chunks):
+                g[c + i, a] = tile[:, :, CHUNK * i : CHUNK * (i + 1)]
+            codes, plane = looked_up(CHUNK * c, width)
+            side = BANK // width
+            for first in range(0, PACK, side):
+                acc = bank(pairs, first // side)
+                for t in range(first, first + side):
                     col = GROUP * a + P * t
                     nc.tensor.matmul_mx(
-                        out=part(acc, w, ts, t),
+                        out=acc[:, width * (t - first) : width * (t - first + 1)],
                         lhsT=wg[a][:, 2 * P * t : 2 * P * (t + 1)].bitcast(FP4X4),
-                        lhsT_scale=wg_planes[:, col : col + P],
+                        lhsT_scale=wg_plane[:, col : col + P],
                         rhs=codes,
-                        rhs_scale=planes,
+                        rhs_scale=plane,
                         start=True,
                         stop=True,
                     )
-                filled.append((acc, ts))
-                if len(filled) == 2:
-                    if between is not None:
-                        between()
-                    for acc, ts in filled if c + a == 0 else reversed(filled):
-                        for t in ts:
-                            nc.scalar.activation(g[c, a][:, t, :], part(acc, w, ts, t), ACT.Relu, bias=bg_sb[:, a, t : t + 1])
-                    filled = []
+                for t in range(first, first + side):
+                    sums = acc[:, width * (t - first) : width * (t - first + 1)]
+                    nc.scalar.activation(tile[:, t, :], sums, ACT.Relu, bias=bg_sb[:, a, t : t + 1])
 
-        def currents(c, a):
-            w = CHUNKS[c][1]
-            held = max(i for i, chunk in enumerate(G_CHUNKS) if chunk[0] <= CHUNKS[c][0])
-            offset = CHUNKS[c][0] - G_CHUNKS[held][0]
-            gates = g[held, a][:, :, offset : offset + w]
-            codes, planes = looked_up(CHUNKS[c])
-            filled = []
-            for ts in bank_groups(w):
-                acc = bank("d", D_BANKS)
-                for t in ts:
+        def currents(c, a, pair):
+            codes, plane = looked_up(CHUNK * c, CHUNK)
+            for first in range(0, PACK, 2):
+                acc = bank(pair, first // 2)
+                for t in range(first, first + 2):
                     nc.tensor.matmul_mx(
-                        out=part(acc, w, ts, t),
+                        out=acc[:, CHUNK * (t - first) : CHUNK * (t - first + 1)],
                         lhsT=wv_codes[a][:, P * t : P * (t + 1)].bitcast(FP8X4),
                         lhsT_scale=wv_planes[a][:, P * t : P * (t + 1)],
                         rhs=codes,
-                        rhs_scale=planes,
+                        rhs_scale=plane,
                         start=True,
                         stop=True,
                     )
-                filled.append((acc, ts))
-            for acc, ts in filled if c == 0 else reversed(filled):
-                for t in ts:
-                    sums, gate = part(acc, w, ts, t), gates[:, t, :]
-                    if (c, a) in G_UNITS:
-                        sums, gate = [x.rearrange("p (k i) -> p k i", i=BLOCK) for x in (sums, gate)]
-                    nc.vector.scalar_tensor_tensor(h_rows[c, a][:, t], sums, erev_sb[:, a, t : t + 1], gate, ALU.add, ALU.mult)
+                for t in range(first, first + 2):
+                    sums = acc[:, CHUNK * (t - first) : CHUNK * (t - first + 1)]
+                    nc.vector.scalar_tensor_tensor(
+                        h_rows[c, a][:, t, :], sums, erev_sb[:, a, t : t + 1], g[c, a][:, t, :], ALU.add, ALU.mult
+                    )
 
-        def weave_h(c, a):
-            if (c, a) not in G_UNITS:
-                weave(h_woven[c, a], h_rows[c, a], H_VECTOR_SHARE[c])
-                return
-            mine = blocks - G_BLOCKS
-            nc.vector.tensor_copy(
-                h_woven[c, a][:, : mine * BLOCK, :].rearrange("p (k c i) t -> p c k t i", k=mine, i=8),
-                h_rows[c, a][:, :, :mine, :].rearrange("p t k (c i) -> p c k t i", i=8),
-            )
-            nc.gpsimd.tensor_scalar(
-                h_woven[c, a][:, mine * BLOCK :, :].rearrange("p (k i) t -> p k i t", i=BLOCK),
-                h_rows[c, a][:, :, mine:, :].rearrange("p t k i -> p k i t"),
-                1.0,
-                0.0,
-                ALU.mult,
-                ALU.add,
-            )
+        def weave_h(c, a, engine, first=0, last=CHUNK):
+            weave(h_woven[c, a], h_rows[c, a], engine, first, last)
 
         def quantize_h(c, a):
             nc.vector.quantize_mx(
                 out=h_codes[c, a][:].bitcast(FP8X4),
                 scales=h_planes[c, a][:],
-                in_=h_woven[c, a].rearrange("p j t -> p (j t)"),
+                in_=h_woven[c, a][:].rearrange("p j t -> p (j t)"),
             )
 
         def columns(c):
-            return slice(CHUNKS[c][0], CHUNKS[c][0] + CHUNKS[c][1])
+            return slice(CHUNK * c, CHUNK * (c + 1))
 
-        def mix_pass(acc, c, b, ts, t, a, start, stop):
+        def mix_pass(acc, c, b, first, t, a, start, stop):
             col = GROUP * b + P * t
             nc.tensor.matmul_mx(
-                out=part(acc, CHUNKS[c][1], ts, t),
+                out=acc[:, CHUNK * (t - first) : CHUNK * (t - first + 1)],
                 lhsT=wo[b][:, a, P * t : P * (t + 1)].bitcast(FP8X4),
-                lhsT_scale=wo_planes[4 * a :, col : col + P],
+                lhsT_scale=wo_plane[4 * a :, col : col + P],
                 rhs=h_codes[c, a][:].bitcast(FP8X4),
                 rhs_scale=h_planes[c, a][:],
                 start=start,
                 stop=stop,
             )
 
-        def add_bias(acc, c, b, ts, on_vector, per_store):
+        def add_bias(acc, c, b, first, reader):
             rows = out_0[GROUP * b : GROUP * (b + 1), columns(c)].rearrange("(p t) j -> p t j", t=PACK)
-            for t in ts:
-                sums = part(acc, CHUNKS[c][1], ts, t)
-                if on_vector:
+            for t in range(first, first + 2):
+                sums = acc[:, CHUNK * (t - first) : CHUNK * (t - first + 1)]
+                if reader == "vector":
                     nc.vector.tensor_scalar(y[c, b][:, t, :], sums, bo_sb[:, b, t : t + 1], None, ALU.add)
                 else:
                     nc.scalar.activation(y[c, b][:, t, :], sums, ACT.Identity, bias=bo_sb[:, b, t : t + 1])
-                if (t + 1) % per_store == 0:
-                    nc.sync.dma_start(rows[:, t + 1 - per_store : t + 1, :], y[c, b][:, t + 1 - per_store : t + 1, :])
+            nc.sync.dma_start(rows[:, first : first + 2, :], y[c, b][:, first : first + 2, :])
 
-        def mix(c, b, per_store=2, banks=Y_BANKS):
-            for ts in bank_groups(CHUNKS[c][1]):
-                acc = bank("y", banks)
-                for t in ts:
+        def mix(c, b, pair):
+            for first in range(0, PACK, 2):
+                acc = bank(pair, first // 2)
+                for t in range(first, first + 2):
                     for a in range(2):
-                        mix_pass(acc, c, b, ts, t, a, a == 0, a == 1)
-                add_bias(acc, c, b, ts, False, per_store)
+                        mix_pass(acc, c, b, first, t, 1 - a, a == 0, a == 1)
+                add_bias(acc, c, b, first, "scalar")
 
-        def mix_last(c, banks, on_vector, per_store=2):
-            groups = [(b, ts) for b in range(2) for ts in bank_groups(CHUNKS[c][1])]
-            accs = [bank("y") for group in groups]
-            for acc, (b, ts) in zip(accs, groups):
-                for t in ts:
-                    mix_pass(acc, c, b, ts, t, 0, t == ts[0], False)
-            for index, (b, ts) in enumerate(groups):
-                for t in ts:
-                    mix_pass(accs[index], c, b, ts, t, 1, False, t == ts[-1])
-                add_bias(accs[index], c, b, ts, index in on_vector, per_store)
+        def mix_last(c, pairs, readers):
+            groups = [(b, first) for b in range(2) for first in range(0, PACK, 2)]
+            accs = [bank(pairs, index) for index in range(len(groups))]
+            for acc, (b, first) in zip(accs, groups):
+                for t in range(first, first + 2):
+                    mix_pass(acc, c, b, first, t, 0, t == first, False)
+            for acc, (b, first), reader in zip(accs, groups, readers):
+                for t in range(first, first + 2):
+                    mix_pass(acc, c, b, first, t, 1, False, t == first + 1)
+                add_bias(acc, c, b, first, reader)
 
-        def weave_y(c, b, slot=None):
-            y_woven[c, b] = sb("y_woven%d%d" % (c, b), [P, CHUNKS[c][1], PACK], BF16, tag=slot)
-            weave(y_woven[c, b], y[c, b], Y_VECTOR_SHARE[c])
+        def weave_y(c, b, engine, first=0, last=CHUNK):
+            weave(y_woven[c, b], y[c, b], engine, first, last)
 
         def quantize_y(c, b):
             nc.vector.quantize_mx(
@@ -356,104 +300,72 @@ def tile_list_synaptic_channel_currents_kernel(
             words = out_1.rearrange("b p m t -> p b (m t)").bitcast(I32)[:, first:last, columns(c)]
             nc.sync.dma_start(words, y_codes[c][:, first:last, :].bitcast(I32))
 
-        def store_y_planes(first, last, queues):
-            rows = out_2[:, :, first:last].rearrange("b (q r) m -> r q b m", r=4)
+        def store_y_planes(queues):
+            rows = out_2.rearrange("b (q r) m -> r q b m", r=4)
             for r in range(4):
-                queues[r % len(queues)].dma_start(rows[r].bitcast(I32), y_planes[r:P:32, :, first:last].bitcast(I32))
+                queues[r % len(queues)].dma_start(rows[r].bitcast(I32), y_planes[r:P:32, :, :].bitcast(I32))
 
-        deal_planes(wg_planes, wg_planes_raw)
-        deal_wg(1)
-        wo_raw = placed("wo_raw", [P, 2, N], U32, 20480 - 8192 + 64)
-        bo_sb = placed("bo_sb", [P, 2, 8], F32, 20480 + 64)
-        wo_planes_raw = placed("wo_planes_raw", [P, N], U8, 20480 + 128)
-        wv_raw.append(placed("wv_raw1", [P, PACK, GROUP], F32, 20480 + 2048 - 64))
-        load_wv(1)
-        nc.vector.memset(wo_planes_raw[:].bitcast(I32), 0)
-        nc.sync.dma_start(wo_raw[:].bitcast(I32), wo8_words.rearrange("a p c i -> p a (c i)").bitcast(I32))
-        load_packed_planes(wo_planes_raw, wo8_scales)
-        nc.sync.dma_start(bo_sb[:, :, 0:PACK], dealt(bo))
-        warm = psum.tile([P, BANK], F32, name="warm", tag="bank7")
-        for repeat in range(4):
-            nc.tensor.matmul_mx(
-                out=warm[:],
-                lhsT=wg[1][:, : 2 * P].bitcast(FP4X4),
-                lhsT_scale=wg_planes[:, GROUP : GROUP + P],
-                rhs=warm_codes[:].bitcast(FP8X4),
-                rhs_scale=warm_plane[:],
-                start=True,
-                stop=True,
-            )
         look_up_words(0)
         look_up_words(1)
-        weave_wv(0, 0, True)
-        weave_wv(0, 1, True)
+        conductances(0, 0, "A")
+        conductances(1, 0, "B")
+        conductances(0, 1, "C")
+        weave_wv(0, 0, "vector")
+        weave_wv(0, 1, "vector")
         quantize_wv(0, 0)
         quantize_wv(0, 1)
-
-        conductances(0, 0)
-        conductances(1, 0)
-        conductances(0, 1)
-
-        def first_currents():
-            currents(0, 0)
-            weave_wv(1, 1, False)
-
-        conductances(1, 1, first_currents)
-        weave_wv(1, 0, True, "g00")
-        weave_h(0, 0)
+        currents(0, 0, "D")
+        weave_wv(1, 1, "scalar")
+        weave_wv(1, 0, "vector")
+        conductances(1, 1, "A")
+        currents(1, 0, "B")
         quantize_wv(1, 0)
         quantize_wv(1, 1)
-        if not PLAIN:
-            currents(1, 0)
-        conductances(2, 0)
+        weave_h(0, 0, "vector")
+        currents(0, 1, "C")
+        deal_wo(0, "scalar")
+        conductances(2, 0, "DA")
+        deal_plane(wo_plane, wo_plane_raw)
+        weave_h(0, 1, "vector")
         quantize_h(0, 0)
-        deal_wo(0, "g00")
-        currents(0, 1)
-        deal_planes(wo_planes, wo_planes_raw)
-        weave_h(0, 1)
-        if not G21LATE:
-            conductances(2, 1)
         quantize_h(0, 1)
-        if MIX0:
-            mix(0, 0)
-        deal_wo(1)
-        if G21LATE == 2:
-            conductances(2, 1)
-        if MIX0 > 1:
-            mix(0, 1)
-        if G21LATE == 3:
-            conductances(2, 1)
-        last = len(CHUNKS) - 1
-
-        def finish(c):
+        deal_wo(1, "scalar")
+        weave_h(1, 0, "vector")
+        currents(1, 1, "B")
+        conductances(2, 1, "C")
+        mix(0, 0, "D")
+        quantize_h(1, 0)
+        weave_h(1, 1, "vector")
+        quantize_h(1, 1)
+        currents(2, 0, "B")
+        mix(0, 1, "A")
+        weave_h(2, 0, "vector")
+        currents(2, 1, "C")
+        conductances(3, 1, "D")
+        mix(1, 0, "A")
+        quantize_h(2, 0)
+        weave_h(2, 1, "vector")
+        quantize_h(2, 1)
+        currents(3, 0, "B")
+        mix(1, 1, "D")
+        weave_h(3, 0, "vector")
+        currents(3, 1, "C")
+        mix(2, 0, "A")
+        quantize_h(3, 0)
+        weave_h(3, 1, "vector")
+        quantize_h(3, 1)
+        mix(2, 1, "D")
+        mix_last(3, "BC", ("scalar", "vector", "scalar", "scalar"))
+        last = CHUNKS - 1
+        half = CHUNK // 2
+        for c in range(CHUNKS):
             for b in range(2):
-                weave_y(c, b)
+                for first in range(0, CHUNK, half):
+                    weave_y(c, b, YENG[c][2 * b + first // half], first, first + half)
             for b in range(2):
                 quantize_y(c, b)
                 if c == last:
                     store_y_codes(c, b, b + 1)
             if c < last:
                 store_y_codes(c, 0, 2)
-
-        for c in range(1, last + 1):
-            banks = Y_BANKS if c == 1 else G_BANKS[:2] + Y_BANKS
-            if c > 1 or PLAIN:
-                currents(c, 0)
-            weave_h(c, 0)
-            currents(c, 1)
-            quantize_h(c, 0)
-            weave_h(c, 1)
-            quantize_h(c, 1)
-            if c > 1 or not MIX0:
-                mix(c - 1, 0, 2, banks)
-            if c > 1 or MIX0 < 2:
-                mix(c - 1, 1, 2, banks)
-            if c == 1 and G21LATE == 1:
-                conductances(2, 1)
-            if c == last:
-                mix_last(c, D_BANKS + G_BANKS[2:], (1,), 2)
-            if c >= 3:
-                finish(c - 3)
-        for c in range(last + 1 - 3, last + 1):
-            finish(c)
-        store_y_planes(0, S, (nc.scalar, nc.sync))
+        store_y_planes((nc.scalar, nc.sync))

@@ -25,7 +25,7 @@ QUADRANTS = 4
 CHUNK = 256
 CHUNKS = S // CHUNK
 LINE = 64
-YENG = (("scalar", "scalar", "scalar", "scalar"), ("vector", "vector", "vector", "vector"), ("vector", "vector", "vector", "vector"), ("vector", "scalar", "vector", "scalar"))
+YENG = (("scalar", "scalar", "scalar", "vector"), ("vector", "vector", "vector", "vector"), ("vector", "vector", "scalar", "scalar"), ("scalar", "scalar", "scalar", "vector"))
 
 
 def tile_list_synaptic_channel_currents_kernel(
@@ -62,6 +62,12 @@ def tile_list_synaptic_channel_currents_kernel(
         nc.vector.memset(wg_plane_raw[:].bitcast(I32), 0)
         nc.vector.memset(table_rows[:].bitcast(I32), 0)
         nc.vector.memset(v_plane[:].bitcast(I32), 0)
+
+        ones = sb("ones", [P, BANK * PACK], BF16)
+        warm_codes = sb("warm_codes", [P, BANK], U32)
+        warm_plane = sb("warm_plane", [P, BANK], U8)
+        nc.vector.memset(ones[:].bitcast(I32), 0x3F803F80)
+        nc.vector.quantize_mx(out=warm_codes[:].bitcast(FP8X4), scales=warm_plane[:], in_=ones[:])
 
         nc.sync.dma_start(wg_raw[:].bitcast(I32), wg4_words[0].bitcast(I32))
         nc.sync.dma_start(offsets[:], offs)
@@ -112,6 +118,17 @@ def tile_list_synaptic_channel_currents_kernel(
         deal_wg(0)
         deal_plane(wg_plane, wg_plane_raw)
         deal_wg(1)
+        warm = bank("D", 1)
+        for repeat in range(4):
+            nc.tensor.matmul_mx(
+                out=warm[:],
+                lhsT=wg[0][:, : 2 * P].bitcast(FP4X4),
+                lhsT_scale=wg_plane[:, :P],
+                rhs=warm_codes[:].bitcast(FP8X4),
+                rhs_scale=warm_plane[:],
+                start=True,
+                stop=True,
+            )
 
         wo_raw = placed("wo_raw", [P, 2, N], U32, wg_at + LINE - 8192)
         bo_sb = placed("bo_sb", [P, 2, 8], F32, wg_at + LINE)
@@ -127,13 +144,13 @@ def tile_list_synaptic_channel_currents_kernel(
         units = [(c, a) for c in range(CHUNKS) for a in range(2)]
         wo = [sb("wo%d" % b, [P, 2, GROUP], U32) for b in range(2)]
         wo_plane = sb("wo_plane", [P, N], U8)
-        wv_woven = [sb("wv_woven%d" % a, [P, PACK, P, PACK], BF16) for a in range(2)]
+        wv_woven = [sb("wv_woven%d" % a, [P, PACK, P, PACK], BF16, "woven%d" % (a - 2)) for a in range(2)]
         wv_codes = [sb("wv_codes%d" % a, [P, GROUP], U32) for a in range(2)]
         wv_planes = [sb("wv_planes%d" % a, [P, GROUP], U8) for a in range(2)]
         v_codes = [sb("v_codes%d" % half, [P, LOOKUP], U32) for half in range(2)]
         g = {}
         h_rows = {u: sb("h_rows%d%d" % u, [P, PACK, CHUNK], BF16) for u in units}
-        h_woven = {u: sb("h_woven%d%d" % u, [P, CHUNK, PACK], BF16) for u in units}
+        h_woven = {}
         h_codes = {u: sb("h_codes%d%d" % u, [P, CHUNK], U32) for u in units}
         h_planes = {u: sb("h_planes%d%d" % u, [P, CHUNK], U8) for u in units}
         y = {u: sb("y%d%d" % u, [P, PACK, CHUNK], F32) for u in units}
@@ -232,8 +249,13 @@ def tile_list_synaptic_channel_currents_kernel(
                         h_rows[c, a][:, t, :], sums, erev_sb[:, a, t : t + 1], g[c, a][:, t, :], ALU.add, ALU.mult
                     )
 
-        def weave_h(c, a, engine, first=0, last=CHUNK):
-            weave(h_woven[c, a], h_rows[c, a], engine, first, last)
+        def weave_h(c, a):
+            h_woven[c, a] = sb("h_woven%d%d" % (c, a), [P, CHUNK, PACK], BF16, "woven%d" % (c + a - 1))
+            if a == 0:
+                rows = h_rows[c, a][:].rearrange("p t j -> p j t")
+                nc.gpsimd.tensor_scalar(h_woven[c, a][:], rows, 1.0, 0.0, ALU.mult, ALU.add)
+            else:
+                weave(h_woven[c, a], h_rows[c, a], "vector")
 
         def quantize_h(c, a):
             nc.vector.quantize_mx(
@@ -267,13 +289,13 @@ def tile_list_synaptic_channel_currents_kernel(
                     nc.scalar.activation(y[c, b][:, t, :], sums, ACT.Identity, bias=bo_sb[:, b, t : t + 1])
             nc.sync.dma_start(rows[:, first : first + 2, :], y[c, b][:, first : first + 2, :])
 
-        def mix(c, b, pair):
+        def mix(c, b, pair, reader="scalar"):
             for first in range(0, PACK, 2):
                 acc = bank(pair, first // 2)
                 for t in range(first, first + 2):
                     for a in range(2):
                         mix_pass(acc, c, b, first, t, 1 - a, a == 0, a == 1)
-                add_bias(acc, c, b, first, "scalar")
+                add_bias(acc, c, b, first, reader)
 
         def mix_last(c, pairs, readers):
             groups = [(b, first) for b in range(2) for first in range(0, PACK, 2)]
@@ -318,44 +340,44 @@ def tile_list_synaptic_channel_currents_kernel(
         weave_wv(1, 1, "scalar")
         weave_wv(1, 0, "vector")
         conductances(1, 1, "A")
-        currents(1, 0, "B")
         quantize_wv(1, 0)
         quantize_wv(1, 1)
-        weave_h(0, 0, "vector")
+        weave_h(0, 0)
+        currents(1, 0, "B")
         currents(0, 1, "C")
         deal_wo(0, "scalar")
         conductances(2, 0, "DA")
         deal_plane(wo_plane, wo_plane_raw)
-        weave_h(0, 1, "vector")
+        weave_h(0, 1)
         quantize_h(0, 0)
         quantize_h(0, 1)
-        deal_wo(1, "scalar")
-        weave_h(1, 0, "vector")
+        weave_h(1, 0)
         currents(1, 1, "B")
-        conductances(2, 1, "C")
+        currents(2, 0, "C")
+        deal_wo(1, "scalar")
         mix(0, 0, "D")
+        conductances(2, 1, "A")
+        weave_h(1, 1)
         quantize_h(1, 0)
-        weave_h(1, 1, "vector")
         quantize_h(1, 1)
-        currents(2, 0, "B")
-        mix(0, 1, "A")
-        weave_h(2, 0, "vector")
+        weave_h(2, 0)
+        mix(0, 1, "B")
         currents(2, 1, "C")
-        conductances(3, 1, "D")
-        mix(1, 0, "A")
+        currents(3, 0, "D")
+        conductances(3, 1, "A")
+        mix(1, 0, "C")
+        weave_h(2, 1)
         quantize_h(2, 0)
-        weave_h(2, 1, "vector")
         quantize_h(2, 1)
-        currents(3, 0, "B")
-        mix(1, 1, "D")
-        weave_h(3, 0, "vector")
-        currents(3, 1, "C")
+        weave_h(3, 0)
+        currents(3, 1, "D")
+        mix(1, 1, "B", "vector")
         mix(2, 0, "A")
         quantize_h(3, 0)
-        weave_h(3, 1, "vector")
+        weave_h(3, 1)
         quantize_h(3, 1)
-        mix(2, 1, "D")
-        mix_last(3, "BC", ("scalar", "vector", "scalar", "scalar"))
+        mix(2, 1, "C")
+        mix_last(3, "DA", ("scalar", "vector", "scalar", "scalar"))
         last = CHUNKS - 1
         half = CHUNK // 2
         for c in range(CHUNKS):

@@ -25,7 +25,7 @@ QUADRANTS = 4
 CHUNK = 256
 CHUNKS = S // CHUNK
 LINE = 64
-YENG = (("scalar", "scalar", "scalar", "vector"), ("vector", "vector", "vector", "vector"), ("vector", "vector", "scalar", "scalar"), ("scalar", "scalar", "scalar", "vector"))
+Y_VECTOR_SHARE = ((256,256), (256,256), (256,256), (0,0))
 
 
 def tile_list_synaptic_channel_currents_kernel(
@@ -144,7 +144,8 @@ def tile_list_synaptic_channel_currents_kernel(
         units = [(c, a) for c in range(CHUNKS) for a in range(2)]
         wo = [sb("wo%d" % b, [P, 2, GROUP], U32) for b in range(2)]
         wo_plane = sb("wo_plane", [P, N], U8)
-        wv_woven = [sb("wv_woven%d" % a, [P, PACK, P, PACK], BF16, "woven%d" % (a - 2)) for a in range(2)]
+        wv_woven = [sb("wv_woven0", [P, PACK, P, PACK], BF16)]
+        wv_pairs = [sb("wv_pair%d" % half, [P, 2, P, PACK], BF16, "first_group" if half == 1 else None) for half in range(2)]
         wv_codes = [sb("wv_codes%d" % a, [P, GROUP], U32) for a in range(2)]
         wv_planes = [sb("wv_planes%d" % a, [P, GROUP], U8) for a in range(2)]
         v_codes = [sb("v_codes%d" % half, [P, LOOKUP], U32) for half in range(2)]
@@ -175,13 +176,10 @@ def tile_list_synaptic_channel_currents_kernel(
                 wo_raw[:, :, GROUP * b : GROUP * (b + 1)].rearrange("p a (k i t) -> p a k t i", t=PACK, i=4),
             )
 
-        def weave_wv(a, half, engine):
-            if a == 0:
-                dst = wv_woven[0][:, :, P // 2 * half : P // 2 * (half + 1), :].rearrange("p t m j -> p m j t")
-                src = wv_first[half][:].rearrange("p j (m t) -> p m j t", t=PACK)
-            else:
-                dst = wv_woven[1][:, 2 * half : 2 * half + 2].rearrange("p t m j -> p m j t")
-                src = wv_second[:].rearrange("p j (m t) -> p m j t", t=PACK)[:, :, :, 2 * half : 2 * half + 2]
+        def weave_wv(a, raw, first, slices, engine):
+            src = raw[:].rearrange("p j (m t) -> p m j t", t=PACK)[:, :, :, slices]
+            woven = wv_woven[0][:, slices] if a == 0 else wv_pairs[slices.start // 2][:]
+            dst = woven[:, :, first : first + src.shape[1], :].rearrange("p t m j -> p m j t")
             if engine == "vector":
                 nc.vector.tensor_scalar(dst, src, -1.0, None, ALU.mult)
             else:
@@ -189,10 +187,11 @@ def tile_list_synaptic_channel_currents_kernel(
 
         def quantize_wv(a, half):
             cols = slice(2 * P * half, 2 * P * (half + 1))
+            woven = wv_woven[0][:, 2 * half : 2 * half + 2] if a == 0 else wv_pairs[half][:]
             nc.vector.quantize_mx(
                 out=wv_codes[a][:, cols].bitcast(FP8X4),
                 scales=wv_planes[a][:, cols],
-                in_=wv_woven[a][:, 2 * half : 2 * half + 2].rearrange("p t m j -> p (t m j)"),
+                in_=woven.rearrange("p t m j -> p (t m j)"),
             )
 
         def weave(woven, rows, engine, first=0, last=CHUNK):
@@ -249,13 +248,14 @@ def tile_list_synaptic_channel_currents_kernel(
                         h_rows[c, a][:, t, :], sums, erev_sb[:, a, t : t + 1], g[c, a][:, t, :], ALU.add, ALU.mult
                     )
 
-        def weave_h(c, a):
-            h_woven[c, a] = sb("h_woven%d%d" % (c, a), [P, CHUNK, PACK], BF16, "woven%d" % (c + a - 1))
-            if a == 0:
-                rows = h_rows[c, a][:].rearrange("p t j -> p j t")
-                nc.gpsimd.tensor_scalar(h_woven[c, a][:], rows, 1.0, 0.0, ALU.mult, ALU.add)
+        def weave_h(c, a, engine, first=0, last=CHUNK):
+            if (c, a) not in h_woven:
+                h_woven[c, a] = sb("h_woven%d%d" % (c, a), [P, CHUNK, PACK], BF16, "first_group" if a == 0 else None)
+            if engine == "gpsimd":
+                rows = h_rows[c, a][:, :, first:last].rearrange("p t j -> p j t")
+                nc.gpsimd.tensor_scalar(h_woven[c, a][:, first:last, :], rows, 1.0, 0.0, ALU.mult, ALU.add)
             else:
-                weave(h_woven[c, a], h_rows[c, a], "vector")
+                weave(h_woven[c, a], h_rows[c, a], engine, first, last)
 
         def quantize_h(c, a):
             nc.vector.quantize_mx(
@@ -289,24 +289,13 @@ def tile_list_synaptic_channel_currents_kernel(
                     nc.scalar.activation(y[c, b][:, t, :], sums, ACT.Identity, bias=bo_sb[:, b, t : t + 1])
             nc.sync.dma_start(rows[:, first : first + 2, :], y[c, b][:, first : first + 2, :])
 
-        def mix(c, b, pair, reader="scalar"):
+        def mix(c, b, pair, readers=("scalar", "scalar")):
             for first in range(0, PACK, 2):
                 acc = bank(pair, first // 2)
                 for t in range(first, first + 2):
                     for a in range(2):
                         mix_pass(acc, c, b, first, t, 1 - a, a == 0, a == 1)
-                add_bias(acc, c, b, first, reader)
-
-        def mix_last(c, pairs, readers):
-            groups = [(b, first) for b in range(2) for first in range(0, PACK, 2)]
-            accs = [bank(pairs, index) for index in range(len(groups))]
-            for acc, (b, first) in zip(accs, groups):
-                for t in range(first, first + 2):
-                    mix_pass(acc, c, b, first, t, 0, t == first, False)
-            for acc, (b, first), reader in zip(accs, groups, readers):
-                for t in range(first, first + 2):
-                    mix_pass(acc, c, b, first, t, 1, False, t == first + 1)
-                add_bias(acc, c, b, first, reader)
+                add_bias(acc, c, b, first, readers[first // 2])
 
         def weave_y(c, b, engine, first=0, last=CHUNK):
             weave(y_woven[c, b], y[c, b], engine, first, last)
@@ -329,61 +318,65 @@ def tile_list_synaptic_channel_currents_kernel(
 
         look_up_words(0)
         look_up_words(1)
-        conductances(0, 0, "A")
-        conductances(1, 0, "B")
-        conductances(0, 1, "C")
-        weave_wv(0, 0, "vector")
-        weave_wv(0, 1, "vector")
+        conductances(0, 0, "AB")
+        weave_wv(0, wv_first[0], 0, slice(0, 4), "vector")
+        weave_wv(0, wv_first[1], P // 2, slice(0, 4), "vector")
         quantize_wv(0, 0)
         quantize_wv(0, 1)
-        currents(0, 0, "D")
-        weave_wv(1, 1, "scalar")
-        weave_wv(1, 0, "vector")
-        conductances(1, 1, "A")
+        currents(0, 0, "A")
+        weave_wv(1, wv_second, 0, slice(2, 4), "scalar")
+        weave_wv(1, wv_second, 0, slice(0, 2), "vector")
+        conductances(0, 1, "CD")
         quantize_wv(1, 0)
         quantize_wv(1, 1)
-        weave_h(0, 0)
+        weave_h(0, 0, "gpsimd")
         currents(1, 0, "B")
         currents(0, 1, "C")
         deal_wo(0, "scalar")
-        conductances(2, 0, "DA")
+        conductances(2, 0, "AD")
         deal_plane(wo_plane, wo_plane_raw)
-        weave_h(0, 1)
+        weave_h(0, 1, "vector")
         quantize_h(0, 0)
         quantize_h(0, 1)
-        weave_h(1, 0)
+        weave_h(1, 0, "gpsimd")
         currents(1, 1, "B")
         currents(2, 0, "C")
         deal_wo(1, "scalar")
-        mix(0, 0, "D")
         conductances(2, 1, "A")
-        weave_h(1, 1)
+        mix(0, 0, "D")
+        weave_h(1, 1, "gpsimd", 0, 96)
+        weave_h(1, 1, "vector", 96, CHUNK)
         quantize_h(1, 0)
         quantize_h(1, 1)
-        weave_h(2, 0)
+        weave_h(2, 0, "gpsimd")
         mix(0, 1, "B")
         currents(2, 1, "C")
         currents(3, 0, "D")
         conductances(3, 1, "A")
         mix(1, 0, "C")
-        weave_h(2, 1)
+        weave_h(2, 1, "gpsimd", 0, 96)
+        weave_h(2, 1, "vector", 96, CHUNK)
         quantize_h(2, 0)
         quantize_h(2, 1)
-        weave_h(3, 0)
+        weave_h(3, 0, "gpsimd", 0, 128)
         currents(3, 1, "D")
-        mix(1, 1, "B", "vector")
+        weave_h(3, 0, "vector", 128, CHUNK)
+        mix(1, 1, "B")
         mix(2, 0, "A")
+        weave_h(3, 1, "vector")
         quantize_h(3, 0)
-        weave_h(3, 1)
         quantize_h(3, 1)
         mix(2, 1, "C")
-        mix_last(3, "DA", ("scalar", "vector", "scalar", "scalar"))
+        mix(3, 0, "D", ("scalar", "vector"))
+        mix(3, 1, "B")
         last = CHUNKS - 1
-        half = CHUNK // 2
         for c in range(CHUNKS):
             for b in range(2):
-                for first in range(0, CHUNK, half):
-                    weave_y(c, b, YENG[c][2 * b + first // half], first, first + half)
+                share = Y_VECTOR_SHARE[c][b]
+                if share > 0:
+                    weave_y(c, b, "vector", 0, share)
+                if share < CHUNK:
+                    weave_y(c, b, "scalar", share, CHUNK)
             for b in range(2):
                 quantize_y(c, b)
                 if c == last:

@@ -145,7 +145,7 @@ def tile_list_synaptic_channel_currents_kernel(
         wo = [sb("wo%d" % b, [P, 2, GROUP], U32) for b in range(2)]
         wo_plane = sb("wo_plane", [P, N], U8)
         wv_woven = [sb("wv_woven0", [P, PACK, P, PACK], BF16)]
-        wv_pairs = [sb("wv_pair%d" % half, [P, 2, P, PACK], BF16, "first_group" if half == 1 else None) for half in range(2)]
+        wv_pairs = [sb("wv_pair%d" % half, [P, 2, P, PACK], BF16, "woven0" if half == 1 else None) for half in range(2)]
         wv_codes = [sb("wv_codes%d" % a, [P, GROUP], U32) for a in range(2)]
         wv_planes = [sb("wv_planes%d" % a, [P, GROUP], U8) for a in range(2)]
         v_codes = [sb("v_codes%d" % half, [P, LOOKUP], U32) for half in range(2)]
@@ -250,7 +250,7 @@ def tile_list_synaptic_channel_currents_kernel(
 
         def weave_h(c, a, engine, first=0, last=CHUNK):
             if (c, a) not in h_woven:
-                h_woven[c, a] = sb("h_woven%d%d" % (c, a), [P, CHUNK, PACK], BF16, "first_group" if a == 0 else None)
+                h_woven[c, a] = sb("h_woven%d%d" % (c, a), [P, CHUNK, PACK], BF16, "woven%d" % (c + a))
             if engine == "gpsimd":
                 rows = h_rows[c, a][:, :, first:last].rearrange("p t j -> p j t")
                 nc.gpsimd.tensor_scalar(h_woven[c, a][:, first:last, :], rows, 1.0, 0.0, ALU.mult, ALU.add)
@@ -344,8 +344,7 @@ def tile_list_synaptic_channel_currents_kernel(
         deal_wo(1, "scalar")
         conductances(2, 1, "A")
         mix(0, 0, "D")
-        weave_h(1, 1, "gpsimd", 0, 96)
-        weave_h(1, 1, "vector", 96, CHUNK)
+        weave_h(1, 1, "vector")
         quantize_h(1, 0)
         quantize_h(1, 1)
         weave_h(2, 0, "gpsimd")
@@ -354,8 +353,7 @@ def tile_list_synaptic_channel_currents_kernel(
         currents(3, 0, "D")
         conductances(3, 1, "A")
         mix(1, 0, "C")
-        weave_h(2, 1, "gpsimd", 0, 96)
-        weave_h(2, 1, "vector", 96, CHUNK)
+        weave_h(2, 1, "vector")
         quantize_h(2, 0)
         quantize_h(2, 1)
         weave_h(3, 0, "gpsimd", 0, 128)

@@ -63,12 +63,6 @@ def tile_list_synaptic_channel_currents_kernel(
         nc.vector.memset(table_rows[:].bitcast(I32), 0)
         nc.vector.memset(v_plane[:].bitcast(I32), 0)
 
-        ones = sb("ones", [P, BANK * PACK], BF16)
-        warm_codes = sb("warm_codes", [P, BANK], U32)
-        warm_plane = sb("warm_plane", [P, BANK], U8)
-        nc.vector.memset(ones[:].bitcast(I32), 0x3F803F80)
-        nc.vector.quantize_mx(out=warm_codes[:].bitcast(FP8X4), scales=warm_plane[:], in_=ones[:])
-
         nc.sync.dma_start(wg_raw[:].bitcast(I32), wg4_words[0].bitcast(I32))
         nc.sync.dma_start(offsets[:], offs)
         wg_rows = wg4_scales[0].rearrange("(q r) c -> r q c", r=4)
@@ -118,17 +112,6 @@ def tile_list_synaptic_channel_currents_kernel(
         deal_wg(0)
         deal_plane(wg_plane, wg_plane_raw)
         deal_wg(1)
-        warm = bank("D", 1)
-        for repeat in range(4):
-            nc.tensor.matmul_mx(
-                out=warm[:],
-                lhsT=wg[0][:, : 2 * P].bitcast(FP4X4),
-                lhsT_scale=wg_plane[:, :P],
-                rhs=warm_codes[:].bitcast(FP8X4),
-                rhs_scale=warm_plane[:],
-                start=True,
-                stop=True,
-            )
 
         wo_raw = placed("wo_raw", [P, 2, N], U32, wg_at + LINE - 8192)
         bo_sb = placed("bo_sb", [P, 2, 8], F32, wg_at + LINE)

@@ -348,7 +348,7 @@ def tile_list_synaptic_channel_currents_kernel(
         quantize_h(3, 0)
         quantize_h(3, 1)
         mix(2, 1, "C")
-        mix(3, 0, "D", ("scalar", "vector"))
+        mix(3, 0, "D")
         mix(3, 1, "B")
         last = CHUNKS - 1
         for c in range(CHUNKS):

@@ -25,7 +25,8 @@ QUADRANTS = 4
 CHUNK = 256
 CHUNKS = S // CHUNK
 LINE = 64
-Y_VECTOR_SHARE = ((256,256), (256,256), (256,256), (0,0))
+Y_VECTOR_SHARE = ((256,256), (256,256), (256,256), (128,0))
+WV_AHEAD = 128
 
 
 def tile_list_synaptic_channel_currents_kernel(
@@ -71,7 +72,7 @@ def tile_list_synaptic_channel_currents_kernel(
         nc.sync.dma_start(table_rows[0:P:8, :].bitcast(I32), tab_scales[0].bitcast(I32))
         nc.sync.dma_start(table[:].bitcast(I32), tab_words[0].rearrange("p t i -> p (t i)").bitcast(I32))
 
-        wv_first = [sb("wv_first0", [P, PACK, GROUP // 2], F32)]
+        wv_first = [sb("wv_first0", [P, PACK, WV_AHEAD], F32)]
 
         def load_wv(tile, first):
             rows = wv[:, first : first + tile.shape[2]].rearrange("(p j) c -> p j c", j=PACK)
@@ -82,7 +83,7 @@ def tile_list_synaptic_channel_currents_kernel(
         for q in range(QUADRANTS):
             nc.sync.dma_start(v_plane[32 * q : 32 * q + 4, :].bitcast(I32), v_rows[32 * q : 32 * (q + 1) : 8, :].bitcast(I32))
 
-        wv_first.append(placed("wv_first1", [P, PACK, GROUP // 2], F32, rows_at + LINE - 4096))
+        wv_first.append(placed("wv_first1", [P, PACK, GROUP - WV_AHEAD], F32, rows_at + LINE - 16 * (GROUP - WV_AHEAD)))
         wv_second = placed("wv_second", [P, PACK, GROUP], F32, rows_at + T - LINE)
         wg = [placed("wg%d" % a, [P, 2 * GROUP], U8, rows_at + LINE + 2 * GROUP * a) for a in range(2)]
         wg_plane = placed("wg_plane", [P, H], U8, rows_at + LINE + 4 * GROUP)
@@ -91,7 +92,7 @@ def tile_list_synaptic_channel_currents_kernel(
         erev_sb = placed("erev_sb", [P, 2, 8], F32, rows_at + 3 * LINE + 6 * GROUP)
 
         nc.sync.dma_start(bg_raw[:, :, 0:PACK], dealt(bg))
-        load_wv(wv_first[1], GROUP // 2)
+        load_wv(wv_first[1], WV_AHEAD)
         nc.sync.dma_start(erev_sb[:, :, 0:PACK], dealt(erev))
         load_wv(wv_second, GROUP)
         nc.scalar.activation(bg_sb[:, :, 0:PACK], bg_raw[:, :, 0:PACK], ACT.Copy)
@@ -148,9 +149,10 @@ def tile_list_synaptic_channel_currents_kernel(
             else:
                 nc.scalar.copy(dst, src)
 
-        def look_up_words(half):
-            entries = offsets[:, half * LOOKUP // 16 : (half + 1) * LOOKUP // 16]
-            nc.vector.tensor_copy(v_codes[half][:], table[:].indirect(entries))
+        def look_up_words(first, count):
+            half, start = divmod(first, LOOKUP)
+            entries = offsets[:, first // 16 : (first + count) // 16]
+            nc.vector.tensor_copy(v_codes[half][:, start : start + count], table[:].indirect(entries))
 
         def deal_wo(b, engine):
             move(
@@ -299,34 +301,36 @@ def tile_list_synaptic_channel_currents_kernel(
             for r in range(4):
                 queues[r % len(queues)].dma_start(rows[r].bitcast(I32), y_planes[r:P:32, :, :].bitcast(I32))
 
-        look_up_words(0)
-        look_up_words(1)
-        conductances(0, 0, "AB")
+        look_up_words(0, CHUNK)
+        look_up_words(CHUNK, CHUNK)
+        look_up_words(LOOKUP, LOOKUP)
+        conductances(0, 0, "A")
+        conductances(1, 0, "B")
         weave_wv(0, wv_first[0], 0, slice(0, 4), "vector")
-        weave_wv(0, wv_first[1], P // 2, slice(0, 4), "vector")
+        weave_wv(0, wv_first[1], WV_AHEAD // PACK, slice(0, 4), "vector")
         quantize_wv(0, 0)
         quantize_wv(0, 1)
-        currents(0, 0, "A")
+        currents(0, 0, "D")
         weave_wv(1, wv_second, 0, slice(2, 4), "scalar")
         weave_wv(1, wv_second, 0, slice(0, 2), "vector")
-        conductances(0, 1, "CD")
+        conductances(0, 1, "CA")
         quantize_wv(1, 0)
         quantize_wv(1, 1)
         weave_h(0, 0, "gpsimd")
         currents(1, 0, "B")
         currents(0, 1, "C")
         deal_wo(0, "scalar")
-        conductances(2, 0, "AD")
+        conductances(2, 0, "DA")
         deal_plane(wo_plane, wo_plane_raw)
         weave_h(0, 1, "vector")
         quantize_h(0, 0)
         quantize_h(0, 1)
         weave_h(1, 0, "gpsimd")
         currents(1, 1, "B")
-        currents(2, 0, "C")
+        currents(2, 0, "A")
         deal_wo(1, "scalar")
-        conductances(2, 1, "A")
         mix(0, 0, "D")
+        conductances(2, 1, "C")
         weave_h(1, 1, "vector")
         quantize_h(1, 0)
         quantize_h(1, 1)

@@ -157,8 +157,8 @@ def tile_list_synaptic_channel_currents_kernel(
         def deal_wo(b, engine):
             move(
                 engine,
-                wo[b][:].rearrange("p a (t k i) -> p a k t i", t=PACK, i=4),
-                wo_raw[:, :, GROUP * b : GROUP * (b + 1)].rearrange("p a (k i t) -> p a k t i", t=PACK, i=4),
+                wo[b][:].rearrange("p a (t m) -> p a m t", t=PACK),
+                wo_raw[:, :, GROUP * b : GROUP * (b + 1)].rearrange("p a (m t) -> p a m t", t=PACK),
             )
 
         def weave_wv(a, raw, first, slices, engine):
@@ -179,9 +179,9 @@ def tile_list_synaptic_channel_currents_kernel(
                 in_=woven.rearrange("p t m j -> p (t m j)"),
             )
 
-        def weave(woven, rows, engine, first=0, last=CHUNK):
-            dst = woven[:, first:last, :].rearrange("p (c i) t -> p c t i", i=8)
-            src = rows[:, :, first:last].rearrange("p t (c i) -> p c t i", i=8)
+        def weave(woven, rows, engine, first, last, run):
+            dst = woven[:, first:last, :].rearrange("p (c i) t -> p c t i", i=run)
+            src = rows[:, :, first:last].rearrange("p t (c i) -> p c t i", i=run)
             move(engine, dst, src)
 
         def looked_up(first, width):
@@ -240,7 +240,7 @@ def tile_list_synaptic_channel_currents_kernel(
                 rows = h_rows[c, a][:, :, first:last].rearrange("p t j -> p j t")
                 nc.gpsimd.tensor_scalar(h_woven[c, a][:, first:last, :], rows, 1.0, 0.0, ALU.mult, ALU.add)
             else:
-                weave(h_woven[c, a], h_rows[c, a], engine, first, last)
+                weave(h_woven[c, a], h_rows[c, a], engine, first, last, 4)
 
         def quantize_h(c, a):
             nc.vector.quantize_mx(
@@ -283,7 +283,7 @@ def tile_list_synaptic_channel_currents_kernel(
                 add_bias(acc, c, b, first, readers[first // 2])
 
         def weave_y(c, b, engine, first=0, last=CHUNK):
-            weave(y_woven[c, b], y[c, b], engine, first, last)
+            weave(y_woven[c, b], y[c, b], engine, first, last, 2)
 
         def quantize_y(c, b):
             nc.vector.quantize_mx(

from contextlib import ExitStack

import concourse.mybir as mybir

K, H, N, T, S = 512, 1024, 1024, 4096, 1024
FLOPS = 2 * S * (2 * K * H + H * N)

F32 = mybir.dt.float32
BF16 = mybir.dt.bfloat16
I32 = mybir.dt.int32
U32 = mybir.dt.uint32
U16 = mybir.dt.uint16
U8 = mybir.dt.uint8
FP8X4 = mybir.dt.float8_e4m3fn_x4
FP4X4 = mybir.dt.float4_e2m1fn_x4
ALU = mybir.AluOpType
ACT = mybir.ActivationFunctionType

P = 128
PACK = 4
GROUP = P * PACK
BANK = 512
LOOKUP = 512
QUADRANTS = 4
CHUNK = 256
CHUNKS = S // CHUNK
LINE = 64
Y_VECTOR_SHARE = ((256,256), (256,256), (256,256), (128,0))
WV_AHEAD = 128


def tile_list_synaptic_channel_currents_kernel(
    tc, tab_words, tab_scales, offs, wg4_words, wg4_scales, bg, wv, erev, wo8_words, wo8_scales, bo, out_0, out_1, out_2
):
    nc = tc.nc
    with ExitStack() as ctx:
        keep = ctx.enter_context(tc.tile_pool(name="keep", bufs=1))
        head = ctx.enter_context(tc.tile_pool(name="head", bufs=1))
        psum = ctx.enter_context(tc.psum_pool(name="psum", bufs=1))

        def sb(name, shape, dtype, tag=None):
            return keep.tile(shape, dtype, name=name, tag=tag or name, align_bytes=64)

        def placed(name, shape, dtype, offset):
            return head.tile(shape, dtype, name=name, align_bytes=64, offset=offset)

        def bank(pairs, index):
            return psum.tile([P, BANK], F32, name="acc", tag="%s%d" % (pairs[index // 2], index % 2))

        def dealt(vec):
            return vec.rearrange("(a p t) -> p a t", p=P, t=PACK)

        offsets = keep.tile([P, S // 16], U16, name="offsets")
        table = sb("table", [P, T], U32)
        rows_at = 8192
        table_rows = placed("table_rows", [P, T], U8, rows_at)
        wg_at = 32768
        wg_raw = placed("wg_raw", [P, 2 * H], U8, wg_at)
        wg_plane_raw = sb("wg_plane_raw", [P, H], U8)
        v_rows = sb("v_rows", [P, S], U8)
        v_plane = sb("v_plane", [P, S], U8)

        nc.vector.memset(wg_plane_raw[:].bitcast(I32), 0)
        nc.vector.memset(table_rows[:].bitcast(I32), 0)
        nc.vector.memset(v_plane[:].bitcast(I32), 0)

        nc.sync.dma_start(wg_raw[:].bitcast(I32), wg4_words[0].bitcast(I32))
        nc.sync.dma_start(offsets[:], offs)
        wg_rows = wg4_scales[0].rearrange("(q r) c -> r q c", r=4)
        for r in range(4):
            nc.sync.dma_start(wg_plane_raw[r:P:32, :].bitcast(I32), wg_rows[r].bitcast(I32))
        nc.sync.dma_start(table_rows[0:P:8, :].bitcast(I32), tab_scales[0].bitcast(I32))
        nc.sync.dma_start(table[:].bitcast(I32), tab_words[0].rearrange("p t i -> p (t i)").bitcast(I32))

        wv_first = [sb("wv_first0", [P, PACK, WV_AHEAD], F32)]

        def load_wv(tile, first):
            rows = wv[:, first : first + tile.shape[2]].rearrange("(p j) c -> p j c", j=PACK)
            nc.sync.dma_start(tile[:], rows)

        load_wv(wv_first[0], 0)
        nc.vector.tensor_copy(v_rows[:], table_rows[:].indirect(offsets[:]))
        for q in range(QUADRANTS):
            nc.sync.dma_start(v_plane[32 * q : 32 * q + 4, :].bitcast(I32), v_rows[32 * q : 32 * (q + 1) : 8, :].bitcast(I32))

        wv_first.append(placed("wv_first1", [P, PACK, GROUP - WV_AHEAD], F32, rows_at + LINE - 16 * (GROUP - WV_AHEAD)))
        wv_second = placed("wv_second", [P, PACK, GROUP], F32, rows_at + T - LINE)
        wg = [placed("wg%d" % a, [P, 2 * GROUP], U8, rows_at + LINE + 2 * GROUP * a) for a in range(2)]
        wg_plane = placed("wg_plane", [P, H], U8, rows_at + LINE + 4 * GROUP)
        bg_raw = placed("bg_raw", [P, 2, 8], F32, rows_at + LINE + 6 * GROUP)
        bg_sb = sb("bg_sb", [P, 2, 8], F32)
        erev_sb = placed("erev_sb", [P, 2, 8], F32, rows_at + 3 * LINE + 6 * GROUP)

        nc.sync.dma_start(bg_raw[:, :, 0:PACK], dealt(bg))
        load_wv(wv_first[1], WV_AHEAD)
        nc.sync.dma_start(erev_sb[:, :, 0:PACK], dealt(erev))
        load_wv(wv_second, GROUP)
        nc.scalar.activation(bg_sb[:, :, 0:PACK], bg_raw[:, :, 0:PACK], ACT.Copy)

        def deal_wg(a):
            cols = slice(2 * GROUP * a, 2 * GROUP * (a + 1))
            nc.vector.tensor_copy(
                wg[a][:].bitcast(U16).rearrange("p (t k i) -> p k t i", t=PACK, i=8),
                wg_raw[:, cols].bitcast(U16).rearrange("p (k i t) -> p k t i", t=PACK, i=8),
            )

        def deal_plane(dst, src):
            nc.vector.tensor_copy(
                dst[:].rearrange("p (a t k i) -> p a k t i", a=2, t=PACK, i=16),
                src[:].rearrange("p (a k i t) -> p a k t i", a=2, t=PACK, i=16),
            )

        deal_wg(0)
        deal_plane(wg_plane, wg_plane_raw)
        deal_wg(1)

        wo_raw = placed("wo_raw", [P, 2, N], U32, wg_at + LINE - 8192)
        bo_sb = placed("bo_sb", [P, 2, 8], F32, wg_at + LINE)
        wo_plane_raw = placed("wo_plane_raw", [P, N], U8, wg_at + 2 * LINE)
        nc.vector.memset(wo_plane_raw[:].bitcast(I32), 0)
        nc.sync.dma_start(wo_raw[:].bitcast(I32), wo8_words.rearrange("a p c i -> p a (c i)").bitcast(I32))
        for q in range(QUADRANTS):
            nc.sync.dma_start(
                wo_plane_raw[32 * q : 32 * q + 8, :].bitcast(I32), wo8_scales[:, 4 * q : 4 * q + 4, :].bitcast(I32)
            )
        nc.sync.dma_start(bo_sb[:, :, 0:PACK], dealt(bo))

        units = [(c, a) for c in range(CHUNKS) for a in range(2)]
        wo = [sb("wo%d" % b, [P, 2, GROUP], U32) for b in range(2)]
        wo_plane = sb("wo_plane", [P, N], U8)
        wv_woven = [sb("wv_woven0", [P, PACK, P, PACK], BF16)]
        wv_pairs = [sb("wv_pair%d" % half, [P, 2, P, PACK], BF16, "woven0" if half == 1 else None) for half in range(2)]
        wv_codes = [sb("wv_codes%d" % a, [P, GROUP], U32) for a in range(2)]
        wv_planes = [sb("wv_planes%d" % a, [P, GROUP], U8) for a in range(2)]
        v_codes = [sb("v_codes%d" % half, [P, LOOKUP], U32) for half in range(2)]
        g = {}
        h_rows = {u: sb("h_rows%d%d" % u, [P, PACK, CHUNK], BF16) for u in units}
        h_woven = {}
        h_codes = {u: sb("h_codes%d%d" % u, [P, CHUNK], U32) for u in units}
        h_planes = {u: sb("h_planes%d%d" % u, [P, CHUNK], U8) for u in units}
        y = {u: sb("y%d%d" % u, [P, PACK, CHUNK], F32) for u in units}
        y_woven = {u: sb("y_woven%d%d" % u, [P, CHUNK, PACK], BF16) for u in units}
        y_codes = [sb("y_codes%d" % c, [P, 2, CHUNK], U32) for c in range(CHUNKS)]
        y_planes = sb("y_planes", [P, 2, S], U8)

        def move(engine, dst, src):
            if engine == "vector":
                nc.vector.tensor_copy(dst, src)
            else:
                nc.scalar.copy(dst, src)

        def look_up_words(first, count):
            half, start = divmod(first, LOOKUP)
            entries = offsets[:, first // 16 : (first + count) // 16]
            nc.vector.tensor_copy(v_codes[half][:, start : start + count], table[:].indirect(entries))

        def deal_wo(b, engine):
            move(
                engine,
                wo[b][:].rearrange("p a (t m) -> p a m t", t=PACK),
                wo_raw[:, :, GROUP * b : GROUP * (b + 1)].rearrange("p a (m t) -> p a m t", t=PACK),
            )

        def weave_wv(a, raw, first, slices, engine):
            src = raw[:].rearrange("p j (m t) -> p m j t", t=PACK)[:, :, :, slices]
            woven = wv_woven[0][:, slices] if a == 0 else wv_pairs[slices.start // 2][:]
            dst = woven[:, :, first : first + src.shape[1], :].rearrange("p t m j -> p m j t")
            if engine == "vector":
                nc.vector.tensor_scalar(dst, src, -1.0, None, ALU.mult)
            else:
                nc.scalar.activation(dst, src, ACT.Copy, scale=-1.0)

        def quantize_wv(a, half):
            cols = slice(2 * P * half, 2 * P * (half + 1))
            woven = wv_woven[0][:, 2 * half : 2 * half + 2] if a == 0 else wv_pairs[half][:]
            nc.vector.quantize_mx(
                out=wv_codes[a][:, cols].bitcast(FP8X4),
                scales=wv_planes[a][:, cols],
                in_=woven.rearrange("p t m j -> p (t m j)"),
            )

        def weave(woven, rows, engine, first, last, run):
            dst = woven[:, first:last, :].rearrange("p (c i) t -> p c t i", i=run)
            src = rows[:, :, first:last].rearrange("p t (c i) -> p c t i", i=run)
            move(engine, dst, src)

        def looked_up(first, width):
            half, start = divmod(first, LOOKUP)
            return v_codes[half][:, start : start + width].bitcast(FP8X4), v_plane[:, first : first + width]

        def conductances(c, a, pairs):
            chunks = len(pairs)
            width = chunks * CHUNK
            tile = sb("g%d%d" % (c, a), [P, PACK, width], F32)
            for i in range(chunks):
                g[c + i, a] = tile[:, :, CHUNK * i : CHUNK * (i + 1)]
            codes, plane = looked_up(CHUNK * c, width)
            side = BANK // width
            for first in range(0, PACK, side):
                acc = bank(pairs, first // side)
                for t in range(first, first + side):
                    col = GROUP * a + P * t
                    nc.tensor.matmul_mx(
                        out=acc[:, width * (t - first) : width * (t - first + 1)],
                        lhsT=wg[a][:, 2 * P * t : 2 * P * (t + 1)].bitcast(FP4X4),
                        lhsT_scale=wg_plane[:, col : col + P],
                        rhs=codes,
                        rhs_scale=plane,
                        start=True,
                        stop=True,
                    )
                for t in range(first, first + side):
                    sums = acc[:, width * (t - first) : width * (t - first + 1)]
                    nc.scalar.activation(tile[:, t, :], sums, ACT.Relu, bias=bg_sb[:, a, t : t + 1])

        def currents(c, a, pair):
            codes, plane = looked_up(CHUNK * c, CHUNK)
            for first in range(0, PACK, 2):
                acc = bank(pair, first // 2)
                for t in range(first, first + 2):
                    nc.tensor.matmul_mx(
                        out=acc[:, CHUNK * (t - first) : CHUNK * (t - first + 1)],
                        lhsT=wv_codes[a][:, P * t : P * (t + 1)].bitcast(FP8X4),
                        lhsT_scale=wv_planes[a][:, P * t : P * (t + 1)],
                        rhs=codes,
                        rhs_scale=plane,
                        start=True,
                        stop=True,
                    )
                for t in range(first, first + 2):
                    sums = acc[:, CHUNK * (t - first) : CHUNK * (t - first + 1)]
                    nc.vector.scalar_tensor_tensor(
                        h_rows[c, a][:, t, :], sums, erev_sb[:, a, t : t + 1], g[c, a][:, t, :], ALU.add, ALU.mult
                    )

        def weave_h(c, a, engine, first=0, last=CHUNK):
            if (c, a) not in h_woven:
                h_woven[c, a] = sb("h_woven%d%d" % (c, a), [P, CHUNK, PACK], BF16, "woven%d" % (c + a))
            if engine == "gpsimd":
                rows = h_rows[c, a][:, :, first:last].rearrange("p t j -> p j t")
                nc.gpsimd.tensor_scalar(h_woven[c, a][:, first:last, :], rows, 1.0, 0.0, ALU.mult, ALU.add)
            else:
                weave(h_woven[c, a], h_rows[c, a], engine, first, last, 4)

        def quantize_h(c, a):
            nc.vector.quantize_mx(
                out=h_codes[c, a][:].bitcast(FP8X4),
                scales=h_planes[c, a][:],
                in_=h_woven[c, a][:].rearrange("p j t -> p (j t)"),
            )

        def columns(c):
            return slice(CHUNK * c, CHUNK * (c + 1))

        def mix_pass(acc, c, b, first, t, a, start, stop):
            col = GROUP * b + P * t
            nc.tensor.matmul_mx(
                out=acc[:, CHUNK * (t - first) : CHUNK * (t - first + 1)],
                lhsT=wo[b][:, a, P * t : P * (t + 1)].bitcast(FP8X4),
                lhsT_scale=wo_plane[4 * a :, col : col + P],
                rhs=h_codes[c, a][:].bitcast(FP8X4),
                rhs_scale=h_planes[c, a][:],
                start=start,
                stop=stop,
            )

        def add_bias(acc, c, b, first, reader):
            rows = out_0[GROUP * b : GROUP * (b + 1), columns(c)].rearrange("(p t) j -> p t j", t=PACK)
            for t in range(first, first + 2):
                sums = acc[:, CHUNK * (t - first) : CHUNK * (t - first + 1)]
                if reader == "vector":
                    nc.vector.tensor_scalar(y[c, b][:, t, :], sums, bo_sb[:, b, t : t + 1], None, ALU.add)
                else:
                    nc.scalar.activation(y[c, b][:, t, :], sums, ACT.Identity, bias=bo_sb[:, b, t : t + 1])
            nc.sync.dma_start(rows[:, first : first + 2, :], y[c, b][:, first : first + 2, :])

        def mix(c, b, pair, readers=("scalar", "scalar")):
            for first in range(0, PACK, 2):
                acc = bank(pair, first // 2)
                for t in range(first, first + 2):
                    for a in range(2):
                        mix_pass(acc, c, b, first, t, 1 - a, a == 0, a == 1)
                add_bias(acc, c, b, first, readers[first // 2])

        def weave_y(c, b, engine, first=0, last=CHUNK):
            weave(y_woven[c, b], y[c, b], engine, first, last, 2)

        def quantize_y(c, b):
            nc.vector.quantize_mx(
                out=y_codes[c][:, b, :].bitcast(FP8X4),
                scales=y_planes[:, b, columns(c)],
                in_=y_woven[c, b][:].rearrange("p j t -> p (j t)"),
            )

        def store_y_codes(c, first, last):
            words = out_1.rearrange("b p m t -> p b (m t)").bitcast(I32)[:, first:last, columns(c)]
            nc.sync.dma_start(words, y_codes[c][:, first:last, :].bitcast(I32))

        def store_y_planes(queues):
            rows = out_2.rearrange("b (q r) m -> r q b m", r=4)
            for r in range(4):
                queues[r % len(queues)].dma_start(rows[r].bitcast(I32), y_planes[r:P:32, :, :].bitcast(I32))

        look_up_words(0, CHUNK)
        look_up_words(CHUNK, CHUNK)
        look_up_words(LOOKUP, LOOKUP)
        conductances(0, 0, "A")
        conductances(1, 0, "B")
        weave_wv(0, wv_first[0], 0, slice(0, 4), "vector")
        weave_wv(0, wv_first[1], WV_AHEAD // PACK, slice(0, 4), "vector")
        quantize_wv(0, 0)
        quantize_wv(0, 1)
        currents(0, 0, "D")
        weave_wv(1, wv_second, 0, slice(2, 4), "scalar")
        weave_wv(1, wv_second, 0, slice(0, 2), "vector")
        conductances(0, 1, "CA")
        quantize_wv(1, 0)
        quantize_wv(1, 1)
        weave_h(0, 0, "gpsimd")
        currents(1, 0, "B")
        currents(0, 1, "C")
        deal_wo(0, "scalar")
        conductances(2, 0, "DA")
        deal_plane(wo_plane, wo_plane_raw)
        weave_h(0, 1, "vector")
        quantize_h(0, 0)
        quantize_h(0, 1)
        weave_h(1, 0, "gpsimd")
        currents(1, 1, "B")
        currents(2, 0, "A")
        deal_wo(1, "scalar")
        mix(0, 0, "D")
        conductances(2, 1, "C")
        weave_h(1, 1, "vector")
        quantize_h(1, 0)
        quantize_h(1, 1)
        weave_h(2, 0, "gpsimd")
        mix(0, 1, "B")
        currents(2, 1, "C")
        currents(3, 0, "D")
        conductances(3, 1, "A")
        mix(1, 0, "C")
        weave_h(2, 1, "vector")
        quantize_h(2, 0)
        quantize_h(2, 1)
        weave_h(3, 0, "gpsimd", 0, 128)
        currents(3, 1, "D")
        weave_h(3, 0, "vector", 128, CHUNK)
        mix(1, 1, "B")
        mix(2, 0, "A")
        weave_h(3, 1, "vector")
        quantize_h(3, 0)
        quantize_h(3, 1)
        mix(2, 1, "C")
        mix(3, 0, "D")
        mix(3, 1, "B")
        last = CHUNKS - 1
        for c in range(CHUNKS):
            for b in range(2):
                share = Y_VECTOR_SHARE[c][b]
                if share > 0:
                    weave_y(c, b, "vector", 0, share)
                if share < CHUNK:
                    weave_y(c, b, "scalar", share, CHUNK)
            for b in range(2):
                quantize_y(c, b)
                if c == last:
                    store_y_codes(c, b, b + 1)
            if c < last:
                store_y_codes(c, 0, 2)
        store_y_planes((nc.scalar, nc.sync))
